import numpy as np
import ml_dtypes


def mxq(x, axis, fmt="e4m3"):
    dtype, down = {"e4m3": (ml_dtypes.float8_e4m3fn, 7), "e5m2": (ml_dtypes.float8_e5m2, 14)}[fmt]
    v = np.moveaxis(np.asarray(x, np.float32).astype(ml_dtypes.bfloat16).astype(np.float64), axis, -1)
    blocks = v.reshape(v.shape[:-1] + (-1, 32))
    amax = np.abs(blocks).max(-1, keepdims=True)
    byte = np.maximum(np.where(amax > 0, np.frexp(amax)[1] - 1 + 127, 0) - down, 1)
    scale = np.exp2(byte - 127.0)
    codes = (blocks / scale).astype(np.float32).astype(dtype).astype(np.float64)
    return np.moveaxis((codes * scale).reshape(v.shape), -1, axis)


WIDE = False


def mx_kscale(k):
    if not WIDE:
        return np.ones(k)
    levels = np.array([18, -18])
    if k % 512:
        return np.exp2(np.random.permutation(np.resize(levels, k // 32))).repeat(32)
    a = np.empty((k // 512, 16))
    for p in range(k // 512):
        a[p, :8] = np.random.permutation(np.resize(levels, 8))
        for g in range(8):
            far = levels[np.abs(levels - a[p, g]) >= 10]
            a[p, g + 8] = far[np.random.randint(len(far))]
    return np.exp2(a.ravel()).repeat(32)


def f64(x):
    return np.asarray(x).astype(np.float64)


def striped(idx):
    return np.tile(np.asarray(idx).reshape(-1, 16).T, (8, 1)).astype(np.uint16)


def unstriped(offs):
    return offs[:16].T.reshape(-1).astype(np.int64)


N, C, D, R = 512, 2048, 512, 1024


def eight(codes):
    return np.concatenate([codes[h].reshape(-1, 16).T for h in range(8)]).astype(np.uint16)


def uneight(offs):
    return np.stack([offs[16 * h:16 * h + 16].T.reshape(-1) for h in range(8)]).astype(np.int64)


def setup_inputs():
    n = np.random.standard_normal
    s = mx_kscale(D)[:, None]
    u = mx_kscale(N)
    grid = lambda x: np.round(x * 32) / 32
    return {
        "xT": (n((D, R)) * (1.0 / np.sqrt(D)) * s).astype(np.float32),
        "cb": (grid(n((D, C))) / s).astype(np.float32),
        "norm": np.tile(np.random.randint(32, 129, N) / 64.0 / u, (128, 1)).astype(np.float32),
        "ts": np.tile(np.random.uniform(0.5, 1.5, N) * u, (128, 1)).astype(np.float32),
        "y": (2 * np.random.randint(0, 2, (R, N)) - 1).astype(np.float32),
        "wt": (np.random.uniform(0.5, 1.5, (R, 1)) * 1.0 / np.sqrt(N)).astype(np.float32),
        "offs": eight(np.random.randint(0, C, (8, N))),
    }


def reference(xT, cb, norm, ts, y, wt, offs):
    code = uneight(offs)
    k = np.concatenate([f64(cb)[64 * h:64 * h + 64][:, code[h]] for h in range(8)]) * f64(norm)[:1]
    a = f64(ts)[:1] * (mxq(f64(xT), 0, "e4m3").T @ mxq(k, 0, "e4m3"))
    g = -f64(wt) * f64(y) * np.maximum(1.0 - f64(y) * a, 0.0)
    h = f64(ts)[:1] * g
    return mxq(h, 1, "e5m2") @ mxq(k, 1, "e4m3").T

@@ -1,0 +1,151 @@
+from contextlib import ExitStack
+
+import concourse.mybir as mybir
+from concourse.masks import make_identity
+
+N, C, D, R = 512, 2048, 512, 1024
+FLOPS = 2 * 2 * R * N * D
+
+F32 = mybir.dt.float32
+BF16 = mybir.dt.bfloat16
+U32 = mybir.dt.uint32
+U16 = mybir.dt.uint16
+U8 = mybir.dt.uint8
+E4 = mybir.dt.float8_e4m3fn_x4
+E5 = mybir.dt.float8_e5m2_x4
+MULT = mybir.AluOpType.mult
+ACT = mybir.ActivationFunctionType
+
+P = 128
+PACK = 4
+BLOCKS = R // P
+X_CHUNK = 256
+HALF = N // 2
+
+
+def tile_attend_gpq_sqh_x_kernel(tc, xT, cb, norm, ts, y, wt, offs, out):
+    nc = tc.nc
+    with ExitStack() as ctx:
+        keep = ctx.enter_context(tc.tile_pool(name="keep", bufs=1))
+        work = ctx.enter_context(tc.tile_pool(name="work", bufs=3))
+        ps_s = ctx.enter_context(tc.psum_pool(name="ps_s", bufs=2))
+        ps_o = ctx.enter_context(tc.psum_pool(name="ps_o", bufs=2))
+        ps_h = ctx.enter_context(tc.psum_pool(name="ps_h", bufs=2))
+        ps_k = ctx.enter_context(tc.psum_pool(name="ps_k", bufs=2))
+
+        offsets = keep.tile([P, N // 16], U16, name="offsets")
+        nc.sync.dma_start(offsets[:], offs)
+
+        cb_planes = cb.rearrange("(p t) c -> t p c", t=PACK)
+        books = []
+        for t in range(PACK):
+            book = keep.tile([P, C], F32, name=f"book{t}")
+            nc.sync.dma_start(book[:], cb_planes[t])
+            books.append(book)
+            if t == 0:
+                rows = keep.tile([P, P], F32, name="rows")
+                nc.vector.memset(rows[:], 0.0)
+                nc.sync.dma_start(rows[0:4, :], norm[0:1, :].rearrange("o (c q) -> (o c) q", q=P))
+                nc.sync.dma_start(rows[4:8, :], ts[0:1, :].rearrange("o (c q) -> (o c) q", q=P))
+                nc.sync.dma_start(rows[8:16, :], wt.rearrange("(b q) o -> b (q o)", q=P))
+
+        x_rows = xT.rearrange("(p t) r -> p t r", t=PACK)
+        x_raw, y_raw = [], []
+        for c in range(R // X_CHUNK):
+            xc = keep.tile([P, PACK, X_CHUNK], F32, name=f"x{c}")
+            nc.sync.dma_start(xc[:], x_rows[:, :, c * X_CHUNK : (c + 1) * X_CHUNK])
+            x_raw.append(xc)
+            yc = keep.tile([P, 2, N], F32, name=f"y{c}")
+            nc.sync.dma_start(yc[:], y[c * X_CHUNK : (c + 1) * X_CHUNK, :].rearrange("(b p) n -> p b n", p=P))
+            y_raw.append(yc)
+
+        ident = keep.tile([P, P], F32, name="ident")
+        make_identity(nc, ident[:])
+        cols_ps = ps_k.tile([P, N], F32, name="kbank")
+        nc.tensor.transpose(cols_ps[:, 0:P], rows[:], ident[:])
+        cols = keep.tile([P, 16], F32, name="cols")
+        nc.scalar.copy(cols[:], cols_ps[:, 0:16])
+
+        norm_b = keep.tile([P, N], F32, name="norm_b")
+        spread = ps_k.tile([P, N], F32, name="kbank")
+        for c in range(4):
+            nc.tensor.transpose(spread[:, c * P : (c + 1) * P], cols[:, c : c + 1].to_broadcast([P, P]), ident[:])
+        nc.scalar.copy(norm_b[:], spread[:])
+        neg_ts = keep.tile([P, N], F32, name="neg_ts")
+        spread = ps_k.tile([P, N], F32, name="kbank")
+        for c in range(4):
+            nc.tensor.transpose(spread[:, c * P : (c + 1) * P], cols[:, 4 + c : 5 + c].to_broadcast([P, P]), ident[:])
+        nc.scalar.activation(neg_ts[:], spread[:], ACT.Copy, scale=-1.0)
+
+        k_f32 = keep.tile([P, PACK, N], F32, name="k_f32")
+        k_bf = keep.tile([P, N, PACK], BF16, name="k_bf", align_bytes=64)
+        kt_bf = keep.tile([P, D, PACK], BF16, name="kt_bf", align_bytes=64)
+        k_codes = keep.tile([P, N], U32, name="k_codes", align_bytes=64)
+        k_scales = keep.tile([P, N], U8, name="k_scales", align_bytes=64)
+        kt_codes = keep.tile([P, D], U32, name="kt_codes", align_bytes=64)
+        kt_scales = keep.tile([P, D], U8, name="kt_scales", align_bytes=64)
+
+        def interleave(copy, dst, src):
+            copy(dst.rearrange("p (c i) t -> p c t i", i=4), src.rearrange("p t (c i) -> p c t i", i=4))
+
+        def turn_plane(t):
+            bank = ps_k.tile([P, PACK, P], F32, name="kbank")
+            for j in range(PACK):
+                nc.tensor.transpose(bank[:, j, :], k_f32[:, t, j::PACK], ident[:])
+            nc.scalar.copy(kt_bf[:, t * P : (t + 1) * P, :], bank[:].rearrange("p j q -> p q j"))
+
+        for t in range(PACK):
+            for half in range(2):
+                cs = slice(half * HALF, (half + 1) * HALF)
+                listed = books[t][:].indirect(offsets[:, half * HALF // 16 : (half + 1) * HALF // 16])
+                nc.vector.tensor_tensor(k_f32[:, t, cs], listed, norm_b[:, cs], MULT)
+            if t < PACK - 1:
+                turn_plane(t)
+        interleave(nc.scalar.copy, k_bf[:, 0:HALF, :], k_f32[:, :, 0:HALF])
+        interleave(nc.vector.tensor_copy, k_bf[:, HALF:N, :], k_f32[:, :, HALF:N])
+        nc.vector.quantize_mx(k_codes[:].bitcast(E4), k_scales[:], k_bf[:].rearrange("p n t -> p (n t)"))
+
+        x_codes = keep.tile([P, R], U32, name="x_codes", align_bytes=64)
+        x_scales = keep.tile([P, R], U8, name="x_scales", align_bytes=64)
+
+        for b in range(BLOCKS):
+            rs = slice(b * P, (b + 1) * P)
+            if b % 2 == 0:
+                c = b // 2
+                xs = slice(c * X_CHUNK, (c + 1) * X_CHUNK)
+                x_bf = work.tile([P, X_CHUNK, PACK], BF16, name="x_bf", align_bytes=64)
+                interleave(nc.scalar.copy, x_bf[:], x_raw[c][:])
+                nc.vector.quantize_mx(x_codes[:, xs].bitcast(E4), x_scales[:, xs], x_bf[:].rearrange("p r t -> p (r t)"))
+                neg_yt2 = work.tile([P, 2, N], F32, name="neg_yt")
+                nc.vector.tensor_tensor(neg_yt2[:], y_raw[c][:], neg_ts[:].unsqueeze(1).to_broadcast([P, 2, N]), MULT)
+            neg_yt = neg_yt2[:, b % 2, :]
+
+            s = ps_s.tile([P, N], F32, name="s")
+            nc.tensor.matmul_mx(s[:], lhsT=x_codes[:, rs].bitcast(E4), lhsT_scale=x_scales[:, rs],
+                                rhs=k_codes[:].bitcast(E4), rhs_scale=k_scales[:], start=True, stop=True)
+            if b == 0:
+                turn_plane(PACK - 1)
+                nc.vector.quantize_mx(kt_codes[:].bitcast(E4), kt_scales[:], kt_bf[:].rearrange("p d j -> p (d j)"))
+            neg_ya = work.tile([P, N], F32, name="neg_ya")
+            nc.vector.tensor_tensor(neg_ya[:], s[:], neg_yt, MULT)
+            margin = work.tile([P, N], F32, name="margin")
+            nc.scalar.activation(margin[:], neg_ya[:], ACT.Relu, bias=1.0, scale=1.0)
+            h = work.tile([P, N], BF16, name="h")
+            nc.vector.scalar_tensor_tensor(h[:], margin[:], cols[:, 8 + b : 9 + b], neg_yt, MULT, MULT)
+
+            h_words = h[:].bitcast(F32)
+            turned = ps_h.tile([P, 2, P], F32, name="turned")
+            for u in range(2):
+                nc.tensor.transpose(turned[:, u, :], h_words[:, u::2], ident[:])
+            ht_bf = work.tile([P, P * PACK], BF16, name="ht_bf", align_bytes=64)
+            nc.scalar.copy(ht_bf[:].bitcast(F32).rearrange("p (r u) -> p r u", u=2), turned[:].rearrange("p u r -> p r u"))
+            h_codes = work.tile([P, P], U32, name="h_codes", align_bytes=64)
+            h_scales = work.tile([P, P], U8, name="h_scales", align_bytes=64)
+            nc.vector.quantize_mx(h_codes[:].bitcast(E5), h_scales[:], ht_bf[:])
+
+            o = ps_o.tile([P, D], F32, name="o")
+            nc.tensor.matmul_mx(o[:], lhsT=h_codes[:].bitcast(E5), lhsT_scale=h_scales[:],
+                                rhs=kt_codes[:].bitcast(E4), rhs_scale=kt_scales[:], start=True, stop=True)
+            res = work.tile([P, P, PACK], F32, name="res")
+            nc.scalar.copy(res[:], o[:].rearrange("p (t q) -> p q t", t=PACK))
+            nc.sync.dma_start(out[rs, :], res[:].rearrange("p q t -> p (q t)"))

@@ -13,11 +13,13 @@ U16 = mybir.dt.uint16
 U8 = mybir.dt.uint8
 E4 = mybir.dt.float8_e4m3fn_x4
 E5 = mybir.dt.float8_e5m2_x4
-MULT = mybir.AluOpType.mult
+ALU = mybir.AluOpType
+MULT = ALU.mult
 ACT = mybir.ActivationFunctionType
 
 P = 128
 PACK = 4
+RUN = 8
 BLOCKS = R // P
 X_CHUNK = 256
 HALF = N // 2
@@ -27,55 +29,74 @@ def tile_attend_gpq_sqh_x_kernel(tc, xT, cb, norm, ts, y, wt, offs, out):
     nc = tc.nc
     with ExitStack() as ctx:
         keep = ctx.enter_context(tc.tile_pool(name="keep", bufs=1))
-        work = ctx.enter_context(tc.tile_pool(name="work", bufs=3))
-        ps_s = ctx.enter_context(tc.psum_pool(name="ps_s", bufs=2))
-        ps_o = ctx.enter_context(tc.psum_pool(name="ps_o", bufs=2))
-        ps_h = ctx.enter_context(tc.psum_pool(name="ps_h", bufs=2))
-        ps_k = ctx.enter_context(tc.psum_pool(name="ps_k", bufs=2))
+        work = ctx.enter_context(tc.tile_pool(name="work", bufs=8))
+        ps_o = ctx.enter_context(tc.psum_pool(name="ps_o", bufs=8))
 
         offsets = keep.tile([P, N // 16], U16, name="offsets")
         nc.sync.dma_start(offsets[:], offs)
+        norm_c = keep.tile([P, PACK], F32, name="norm_c")
+        nc.sync.dma_start(norm_c[:], norm[0:1, :].rearrange("o (p j) -> (o p) j", j=PACK))
+        ts_c = keep.tile([P, PACK], F32, name="ts_c")
+        nc.sync.dma_start(ts_c[:], ts[0:1, :].rearrange("o (p j) -> (o p) j", j=PACK))
 
         cb_planes = cb.rearrange("(p t) c -> t p c", t=PACK)
-        books = []
-        for t in range(PACK):
+        x_rows = xT.rearrange("(p t) r -> p t r", t=PACK)
+        books, x_raw, y_raw = [], [], []
+
+        def load_book(t):
             book = keep.tile([P, C], F32, name=f"book{t}")
             nc.sync.dma_start(book[:], cb_planes[t])
             books.append(book)
-            if t == 0:
-                rows = keep.tile([P, P], F32, name="rows")
-                nc.vector.memset(rows[:], 0.0)
-                nc.sync.dma_start(rows[0:4, :], norm[0:1, :].rearrange("o (c q) -> (o c) q", q=P))
-                nc.sync.dma_start(rows[4:8, :], ts[0:1, :].rearrange("o (c q) -> (o c) q", q=P))
-                nc.sync.dma_start(rows[8:16, :], wt.rearrange("(b q) o -> b (q o)", q=P))
 
-        x_rows = xT.rearrange("(p t) r -> p t r", t=PACK)
-        x_raw, y_raw = [], []
-        for c in range(R // X_CHUNK):
+        def load_x(c):
             xc = keep.tile([P, PACK, X_CHUNK], F32, name=f"x{c}")
             nc.sync.dma_start(xc[:], x_rows[:, :, c * X_CHUNK : (c + 1) * X_CHUNK])
             x_raw.append(xc)
+
+        def load_y(c):
             yc = keep.tile([P, 2, N], F32, name=f"y{c}")
             nc.sync.dma_start(yc[:], y[c * X_CHUNK : (c + 1) * X_CHUNK, :].rearrange("(b p) n -> p b n", p=P))
             y_raw.append(yc)
 
+        load_book(0)
+        rows = keep.tile([P, P], F32, name="rows")
+        nc.vector.memset(rows[:], 0.0)
+        nc.sync.dma_start(rows[0:4, :].rearrange("j (q i) -> j q i", i=RUN),
+                          ts[0:1, :].rearrange("o (q j i) -> (o j) q i", j=PACK, i=RUN))
+        nc.sync.dma_start(rows[8:16, :], wt.rearrange("(b q) o -> b (q o)", q=P))
+        load_book(1)
+        load_book(2)
+        load_book(3)
+        load_x(0)
+        load_y(0)
+        load_x(1)
+        load_y(1)
+        load_x(2)
+        load_y(2)
+        load_x(3)
+        load_y(3)
+
         ident = keep.tile([P, P], F32, name="ident")
         make_identity(nc, ident[:])
-        cols_ps = ps_k.tile([P, N], F32, name="kbank")
-        nc.tensor.transpose(cols_ps[:, 0:P], rows[:], ident[:])
-        cols = keep.tile([P, 16], F32, name="cols")
-        nc.scalar.copy(cols[:], cols_ps[:, 0:16])
 
+        sign = keep.tile([P, PACK], F32, name="sign")
+        nc.vector.tensor_scalar(sign[:], ts_c[:], 0.0, 2.0, ALU.is_ge, MULT)
+        signed = keep.tile([P, PACK], F32, name="signed")
+        nc.vector.scalar_tensor_tensor(signed[:], sign[:], -1.0, norm_c[:], ALU.add, MULT)
         norm_b = keep.tile([P, N], F32, name="norm_b")
-        spread = ps_k.tile([P, N], F32, name="kbank")
-        for c in range(4):
-            nc.tensor.transpose(spread[:, c * P : (c + 1) * P], cols[:, c : c + 1].to_broadcast([P, P]), ident[:])
-        nc.scalar.copy(norm_b[:], spread[:])
-        neg_ts = keep.tile([P, N], F32, name="neg_ts")
-        spread = ps_k.tile([P, N], F32, name="kbank")
-        for c in range(4):
-            nc.tensor.transpose(spread[:, c * P : (c + 1) * P], cols[:, 4 + c : 5 + c].to_broadcast([P, P]), ident[:])
-        nc.scalar.activation(neg_ts[:], spread[:], ACT.Copy, scale=-1.0)
+        spread = ps_o.tile([P, PACK, P], F32, name="o")
+        for j in range(PACK):
+            nc.tensor.transpose(spread[:, j, :], signed[:, j : j + 1].to_broadcast([P, P]), ident[:])
+        nc.scalar.copy(norm_b[:].rearrange("p (m j) -> p m j", j=PACK), spread[:].rearrange("p j m -> p m j"))
+
+        cols_ps = ps_o.tile([P, P], F32, name="o")
+        nc.tensor.transpose(cols_ps[:], rows[:], ident[:])
+        abs_ts = keep.tile([P, PACK], F32, name="abs_ts")
+        nc.scalar.activation(abs_ts[:], cols_ps[:, 0:4], ACT.Abs)
+        neg_wt = keep.tile([P, BLOCKS], F32, name="neg_wt")
+        nc.scalar.activation(neg_wt[:], cols_ps[:, 8:16], ACT.Copy, scale=-1.0)
+        neg_ts2 = keep.tile([P, PACK], F32, name="neg_ts2")
+        nc.vector.scalar_tensor_tensor(neg_ts2[:], abs_ts[:], -1.0, abs_ts[:], MULT, MULT)
 
         k_f32 = keep.tile([P, PACK, N], F32, name="k_f32")
         k_bf = keep.tile([P, N, PACK], BF16, name="k_bf", align_bytes=64)
@@ -89,17 +110,21 @@ def tile_attend_gpq_sqh_x_kernel(tc, xT, cb, norm, ts, y, wt, offs, out):
             copy(dst.rearrange("p (c i) t -> p c t i", i=4), src.rearrange("p t (c i) -> p c t i", i=4))
 
         def turn_plane(t):
-            bank = ps_k.tile([P, PACK, P], F32, name="kbank")
+            k_runs = work.tile([P, PACK, P], F32, name="k_runs")
+            nc.scalar.copy(k_runs[:].rearrange("p j (q i) -> p j q i", i=RUN), k_f32[:, t, :].rearrange("p (q j i) -> p j q i", j=PACK, i=RUN))
+            bank = ps_o.tile([P, PACK, P], F32, name="o")
             for j in range(PACK):
-                nc.tensor.transpose(bank[:, j, :], k_f32[:, t, j::PACK], ident[:])
-            nc.scalar.copy(kt_bf[:, t * P : (t + 1) * P, :], bank[:].rearrange("p j q -> p q j"))
+                nc.tensor.transpose(bank[:, j, :], k_runs[:, j, :], ident[:])
+            ds = slice(t * P, (t + 1) * P)
+            nc.scalar.copy(kt_bf[:, ds, :], bank[:].rearrange("p j q -> p q j"))
+            nc.vector.quantize_mx(kt_codes[:, ds].bitcast(E4), kt_scales[:, ds], kt_bf[:, ds, :].rearrange("p d j -> p (d j)"))
 
         for t in range(PACK):
             for half in range(2):
                 cs = slice(half * HALF, (half + 1) * HALF)
                 listed = books[t][:].indirect(offsets[:, half * HALF // 16 : (half + 1) * HALF // 16])
                 nc.vector.tensor_tensor(k_f32[:, t, cs], listed, norm_b[:, cs], MULT)
-            if t < PACK - 1:
+            if t < PACK - 2:
                 turn_plane(t)
         interleave(nc.scalar.copy, k_bf[:, 0:HALF, :], k_f32[:, :, 0:HALF])
         interleave(nc.vector.tensor_copy, k_bf[:, HALF:N, :], k_f32[:, :, HALF:N])
@@ -108,44 +133,108 @@ def tile_attend_gpq_sqh_x_kernel(tc, xT, cb, norm, ts, y, wt, offs, out):
         x_codes = keep.tile([P, R], U32, name="x_codes", align_bytes=64)
         x_scales = keep.tile([P, R], U8, name="x_scales", align_bytes=64)
 
-        for b in range(BLOCKS):
-            rs = slice(b * P, (b + 1) * P)
-            if b % 2 == 0:
-                c = b // 2
-                xs = slice(c * X_CHUNK, (c + 1) * X_CHUNK)
-                x_bf = work.tile([P, X_CHUNK, PACK], BF16, name="x_bf", align_bytes=64)
-                interleave(nc.scalar.copy, x_bf[:], x_raw[c][:])
-                nc.vector.quantize_mx(x_codes[:, xs].bitcast(E4), x_scales[:, xs], x_bf[:].rearrange("p r t -> p (r t)"))
-                neg_yt2 = work.tile([P, 2, N], F32, name="neg_yt")
-                nc.vector.tensor_tensor(neg_yt2[:], y_raw[c][:], neg_ts[:].unsqueeze(1).to_broadcast([P, 2, N]), MULT)
-            neg_yt = neg_yt2[:, b % 2, :]
+        st = {}
 
-            s = ps_s.tile([P, N], F32, name="s")
+        def prep_x(r0, width):
+            xs = slice(r0, r0 + width)
+            c0 = r0 % X_CHUNK
+            x_bf = work.tile([P, width, PACK], BF16, name="x_bf", align_bytes=64)
+            interleave(nc.scalar.copy, x_bf[:], x_raw[r0 // X_CHUNK][:, :, c0 : c0 + width])
+            nc.vector.quantize_mx(x_codes[:, xs].bitcast(E4), x_scales[:, xs], x_bf[:].rearrange("p r t -> p (r t)"))
+
+        def y_runs(b):
+            return y_raw[b // 2][:, b % 2, :].rearrange("p (q j i) -> p j q i", j=PACK, i=RUN)
+
+        def scores(b):
+            rs = slice(b * P, (b + 1) * P)
+            s = ps_o.tile([P, N], F32, name="o")
             nc.tensor.matmul_mx(s[:], lhsT=x_codes[:, rs].bitcast(E4), lhsT_scale=x_scales[:, rs],
                                 rhs=k_codes[:].bitcast(E4), rhs_scale=k_scales[:], start=True, stop=True)
-            if b == 0:
-                turn_plane(PACK - 1)
-                nc.vector.quantize_mx(kt_codes[:].bitcast(E4), kt_scales[:], kt_bf[:].rearrange("p d j -> p (d j)"))
-            neg_ya = work.tile([P, N], F32, name="neg_ya")
-            nc.vector.tensor_tensor(neg_ya[:], s[:], neg_yt, MULT)
-            margin = work.tile([P, N], F32, name="margin")
-            nc.scalar.activation(margin[:], neg_ya[:], ACT.Relu, bias=1.0, scale=1.0)
-            h = work.tile([P, N], BF16, name="h")
-            nc.vector.scalar_tensor_tensor(h[:], margin[:], cols[:, 8 + b : 9 + b], neg_yt, MULT, MULT)
+            ys = work.tile([P, PACK, P], F32, name="ys")
+            nc.vector.tensor_tensor(ys[:].rearrange("p j (q i) -> p j q i", i=RUN),
+                                    s[:].rearrange("p (q j i) -> p j q i", j=PACK, i=RUN), y_runs(b), MULT)
+            st["ys", b] = ys
 
-            h_words = h[:].bitcast(F32)
-            turned = ps_h.tile([P, 2, P], F32, name="turned")
-            for u in range(2):
-                nc.tensor.transpose(turned[:, u, :], h_words[:, u::2], ident[:])
-            ht_bf = work.tile([P, P * PACK], BF16, name="ht_bf", align_bytes=64)
-            nc.scalar.copy(ht_bf[:].bitcast(F32).rearrange("p (r u) -> p r u", u=2), turned[:].rearrange("p u r -> p r u"))
+        def weigh(b):
+            yw = work.tile([P, PACK, P], F32, name="yw")
+            nc.vector.tensor_scalar(yw[:].rearrange("p j (q i) -> p j q i", i=RUN), y_runs(b), neg_wt[:, b : b + 1], None, MULT)
+            st["yw", b] = yw
+
+        def margins(b):
+            ys_t = ps_o.tile([P, PACK, P], F32, name="o")
+            for j in range(PACK):
+                nc.tensor.transpose(ys_t[:, j, :], st["ys", b][:, j, :], ident[:])
+            yw_t = ps_o.tile([P, PACK, P], F32, name="o")
+            for j in range(PACK):
+                nc.tensor.transpose(yw_t[:, j, :], st["yw", b][:, j, :], ident[:])
+            margin = work.tile([P, PACK, P], F32, name="margin")
+            for j in range(PACK):
+                nc.scalar.activation(margin[:, j, :], ys_t[:, j, :], ACT.Relu, bias=abs_ts[:, j : j + 1], scale=neg_ts2[:, j : j + 1])
+            st["m", b] = (margin, yw_t)
+
+        def grads(b):
+            margin, yw_t = st["m", b]
+            ht_bf = work.tile([P, P, PACK], BF16, name="ht_bf", align_bytes=64)
+            nc.vector.tensor_tensor(ht_bf[:].rearrange("p (c i) j -> p c j i", i=4),
+                                    yw_t[:].rearrange("p j (c i) -> p c j i", i=4),
+                                    margin[:].rearrange("p j (c i) -> p c j i", i=4), MULT)
+            st["h", b] = ht_bf
+
+        def finish(b):
             h_codes = work.tile([P, P], U32, name="h_codes", align_bytes=64)
             h_scales = work.tile([P, P], U8, name="h_scales", align_bytes=64)
-            nc.vector.quantize_mx(h_codes[:].bitcast(E5), h_scales[:], ht_bf[:])
-
+            nc.vector.quantize_mx(h_codes[:].bitcast(E5), h_scales[:], st["h", b][:].rearrange("p r j -> p (r j)"))
             o = ps_o.tile([P, D], F32, name="o")
             nc.tensor.matmul_mx(o[:], lhsT=h_codes[:].bitcast(E5), lhsT_scale=h_scales[:],
                                 rhs=kt_codes[:].bitcast(E4), rhs_scale=kt_scales[:], start=True, stop=True)
             res = work.tile([P, P, PACK], F32, name="res")
             nc.scalar.copy(res[:], o[:].rearrange("p (t q) -> p q t", t=PACK))
-            nc.sync.dma_start(out[rs, :], res[:].rearrange("p q t -> p (q t)"))
+            nc.sync.dma_start(out[b * P : (b + 1) * P, :], res[:].rearrange("p q t -> p (q t)"))
+
+        prep_x(0, P)
+        prep_x(P, P)
+        prep_x(2 * P, X_CHUNK)
+        scores(0)
+        weigh(0)
+        turn_plane(2)
+        turn_plane(3)
+        scores(1)
+        weigh(1)
+        margins(0)
+        prep_x(4 * P, X_CHUNK)
+        scores(2)
+        weigh(2)
+        margins(1)
+        grads(0)
+        scores(3)
+        weigh(3)
+        margins(2)
+        grads(1)
+        finish(0)
+        prep_x(6 * P, X_CHUNK)
+        scores(4)
+        weigh(4)
+        margins(3)
+        grads(2)
+        finish(1)
+        scores(5)
+        weigh(5)
+        margins(4)
+        grads(3)
+        finish(2)
+        scores(6)
+        weigh(6)
+        margins(5)
+        grads(4)
+        finish(3)
+        scores(7)
+        weigh(7)
+        margins(6)
+        grads(5)
+        finish(4)
+        margins(7)
+        grads(6)
+        finish(5)
+        grads(7)
+        finish(6)
+        finish(7)

@@ -23,17 +23,26 @@ RUN = 8
 BLOCKS = R // P
 X_CHUNK = 256
 HALF = N // 2
+SPLIT = 256
 
 
 def tile_attend_gpq_sqh_x_kernel(tc, xT, cb, norm, ts, y, wt, offs, out):
     nc = tc.nc
     with ExitStack() as ctx:
         keep = ctx.enter_context(tc.tile_pool(name="keep", bufs=1))
-        work = ctx.enter_context(tc.tile_pool(name="work", bufs=8))
-        ps_o = ctx.enter_context(tc.psum_pool(name="ps_o", bufs=8))
+        by_vector = ctx.enter_context(tc.tile_pool(name="by_vector", bufs=32))
+        by_scalar = ctx.enter_context(tc.tile_pool(name="by_scalar", bufs=20))
+        by_gpsimd = ctx.enter_context(tc.tile_pool(name="by_gpsimd", bufs=8))
+        small = ctx.enter_context(tc.tile_pool(name="small", bufs=8))
+        banks = ctx.enter_context(tc.psum_pool(name="banks", bufs=8))
 
-        offsets = keep.tile([P, N // 16], U16, name="offsets")
-        nc.sync.dma_start(offsets[:], offs)
+        def ring(engine, shape, dtype):
+            pool = {"V": by_vector, "S": by_scalar, "G": by_gpsimd}[engine]
+            return pool.tile(shape, dtype, name="ring", align_bytes=64)
+
+        def bank(shape):
+            return banks.tile(shape, F32, name="bank")
+
         norm_c = keep.tile([P, PACK], F32, name="norm_c")
         nc.sync.dma_start(norm_c[:], norm[0:1, :].rearrange("o (p j) -> (o p) j", j=PACK))
         ts_c = keep.tile([P, PACK], F32, name="ts_c")
@@ -59,6 +68,8 @@ def tile_attend_gpq_sqh_x_kernel(tc, xT, cb, norm, ts, y, wt, offs, out):
             y_raw.append(yc)
 
         load_book(0)
+        offsets = keep.tile([P, N // 16], U16, name="offsets")
+        nc.sync.dma_start(offsets[:], offs)
         rows = keep.tile([P, P], F32, name="rows")
         nc.vector.memset(rows[:], 0.0)
         nc.sync.dma_start(rows[0:4, :].rearrange("j (q i) -> j q i", i=RUN),
@@ -84,157 +95,153 @@ def tile_attend_gpq_sqh_x_kernel(tc, xT, cb, norm, ts, y, wt, offs, out):
         signed = keep.tile([P, PACK], F32, name="signed")
         nc.vector.scalar_tensor_tensor(signed[:], sign[:], -1.0, norm_c[:], ALU.add, MULT)
         norm_b = keep.tile([P, N], F32, name="norm_b")
-        spread = ps_o.tile([P, PACK, P], F32, name="o")
+        spread = bank([P, PACK, P])
         for j in range(PACK):
             nc.tensor.transpose(spread[:, j, :], signed[:, j : j + 1].to_broadcast([P, P]), ident[:])
         nc.scalar.copy(norm_b[:].rearrange("p (m j) -> p m j", j=PACK), spread[:].rearrange("p j m -> p m j"))
 
-        cols_ps = ps_o.tile([P, P], F32, name="o")
+        cols_ps = bank([P, P])
         nc.tensor.transpose(cols_ps[:], rows[:], ident[:])
         abs_ts = keep.tile([P, PACK], F32, name="abs_ts")
         nc.scalar.activation(abs_ts[:], cols_ps[:, 0:4], ACT.Abs)
         neg_wt = keep.tile([P, BLOCKS], F32, name="neg_wt")
         nc.scalar.activation(neg_wt[:], cols_ps[:, 8:16], ACT.Copy, scale=-1.0)
-        neg_ts2 = keep.tile([P, PACK], F32, name="neg_ts2")
-        nc.vector.scalar_tensor_tensor(neg_ts2[:], abs_ts[:], -1.0, abs_ts[:], MULT, MULT)
 
+        neg_ts2 = keep.tile([P, PACK], F32, name="neg_ts2")
         k_f32 = keep.tile([P, PACK, N], F32, name="k_f32")
         k_bf = keep.tile([P, N, PACK], BF16, name="k_bf", align_bytes=64)
-        kt_bf = keep.tile([P, D, PACK], BF16, name="kt_bf", align_bytes=64)
-        k_codes = keep.tile([P, N], U32, name="k_codes", align_bytes=64)
         k_scales = keep.tile([P, N], U8, name="k_scales", align_bytes=64)
         kt_codes = keep.tile([P, D], U32, name="kt_codes", align_bytes=64)
         kt_scales = keep.tile([P, D], U8, name="kt_scales", align_bytes=64)
-
-        def interleave(copy, dst, src):
-            copy(dst.rearrange("p (c i) t -> p c t i", i=4), src.rearrange("p t (c i) -> p c t i", i=4))
-
-        def turn_plane(t):
-            k_runs = work.tile([P, PACK, P], F32, name="k_runs")
-            nc.scalar.copy(k_runs[:].rearrange("p j (q i) -> p j q i", i=RUN), k_f32[:, t, :].rearrange("p (q j i) -> p j q i", j=PACK, i=RUN))
-            bank = ps_o.tile([P, PACK, P], F32, name="o")
-            for j in range(PACK):
-                nc.tensor.transpose(bank[:, j, :], k_runs[:, j, :], ident[:])
-            ds = slice(t * P, (t + 1) * P)
-            nc.scalar.copy(kt_bf[:, ds, :], bank[:].rearrange("p j q -> p q j"))
-            nc.vector.quantize_mx(kt_codes[:, ds].bitcast(E4), kt_scales[:, ds], kt_bf[:, ds, :].rearrange("p d j -> p (d j)"))
-
-        for t in range(PACK):
-            for half in range(2):
-                cs = slice(half * HALF, (half + 1) * HALF)
-                listed = books[t][:].indirect(offsets[:, half * HALF // 16 : (half + 1) * HALF // 16])
-                nc.vector.tensor_tensor(k_f32[:, t, cs], listed, norm_b[:, cs], MULT)
-            if t < PACK - 2:
-                turn_plane(t)
-        interleave(nc.scalar.copy, k_bf[:, 0:HALF, :], k_f32[:, :, 0:HALF])
-        interleave(nc.vector.tensor_copy, k_bf[:, HALF:N, :], k_f32[:, :, HALF:N])
-        nc.vector.quantize_mx(k_codes[:].bitcast(E4), k_scales[:], k_bf[:].rearrange("p n t -> p (n t)"))
-
-        x_codes = keep.tile([P, R], U32, name="x_codes", align_bytes=64)
-        x_scales = keep.tile([P, R], U8, name="x_scales", align_bytes=64)
-
+        k_codes = keep.tile([P, N], U32, name="k_codes", align_bytes=64)
         st = {}
+        ENG = {("kruns", 0): "V", ("kruns", 1): "V", ("kruns", 2): "V"}
 
-        def prep_x(r0, width):
-            xs = slice(r0, r0 + width)
-            c0 = r0 % X_CHUNK
-            x_bf = work.tile([P, width, PACK], BF16, name="x_bf", align_bytes=64)
-            interleave(nc.scalar.copy, x_bf[:], x_raw[r0 // X_CHUNK][:, :, c0 : c0 + width])
-            nc.vector.quantize_mx(x_codes[:, xs].bitcast(E4), x_scales[:, xs], x_bf[:].rearrange("p r t -> p (r t)"))
+        def engine_of(stage, b, default):
+            return ENG.get((stage, b), ENG.get(stage, default))
 
-        def y_runs(b):
-            return y_raw[b // 2][:, b % 2, :].rearrange("p (q j i) -> p j q i", j=PACK, i=RUN)
+        def copy(e, dst, src):
+            if e == "S":
+                nc.scalar.copy(dst, src)
+            elif e == "V":
+                nc.vector.tensor_copy(dst, src)
+            else:
+                nc.gpsimd.tensor_scalar(dst, src, 1.0, 0.0, MULT, ALU.add)
 
-        def scores(b):
-            rs = slice(b * P, (b + 1) * P)
-            s = ps_o.tile([P, N], F32, name="o")
-            nc.tensor.matmul_mx(s[:], lhsT=x_codes[:, rs].bitcast(E4), lhsT_scale=x_scales[:, rs],
+        def interleave(e, dst, src):
+            copy(e, dst.rearrange("p (c i) t -> p c t i", i=4), src.rearrange("p t (c i) -> p c t i", i=4))
+
+        def in_runs(ap):
+            return ap.rearrange("p (q j i) -> p j q i", j=PACK, i=RUN)
+
+        def gather(t):
+            for lo, hi in ((0, SPLIT), (SPLIT, N)):
+                listed = books[t][:].indirect(offsets[:, lo // 16 : hi // 16])
+                nc.vector.tensor_tensor(k_f32[:, t, lo:hi], listed, norm_b[:, lo:hi], MULT)
+
+            if t == 0:
+                nc.vector.scalar_tensor_tensor(neg_ts2[:], abs_ts[:], -1.0, abs_ts[:], MULT, MULT)
+
+        def kruns(t):
+            e = engine_of("kruns", t, "S")
+            st["kruns", t] = ring(e, [P, PACK, P], F32)
+            copy(e, st["kruns", t][:].rearrange("p j (q i) -> p j q i", i=RUN), in_runs(k_f32[:, t, :]))
+
+        def kturn(t):
+            st["kturn", t] = bank([P, PACK, P])
+            for j in range(PACK):
+                nc.tensor.transpose(st["kturn", t][:, j, :], st["kruns", t][:, j, :], ident[:])
+
+        def ktcopy(t):
+            e = engine_of("ktcopy", t, "S")
+            st["kt", t] = ring(e, [P, P, PACK], BF16)
+            copy(e, st["kt", t][:], st["kturn", t][:].rearrange("p j q -> p q j"))
+
+        def ktq(t):
+            ds = slice(t * P, (t + 1) * P)
+            nc.vector.quantize_mx(kt_codes[:, ds].bitcast(E4), kt_scales[:, ds], st["kt", t][:].rearrange("p d j -> p (d j)"))
+
+        def kil(half):
+            cs = (slice(0, SPLIT), slice(SPLIT, N))[half]
+            interleave(engine_of("kil", half, "SV"[half]), k_bf[:, cs, :], k_f32[:, :, cs])
+
+        def kq(z):
+            nc.vector.quantize_mx(k_codes[:].bitcast(E4), k_scales[:], k_bf[:].rearrange("p n t -> p (n t)"))
+
+        def xil(b):
+            e = engine_of("xil", b, "S")
+            c0 = b * P % X_CHUNK
+            st["xil", b] = ring(e, [P, P, PACK], BF16)
+            interleave(e, st["xil", b][:], x_raw[b // 2][:, :, c0 : c0 + P])
+
+        def xq(b):
+            st["xc", b] = ring("V", [P, P], U32)
+            st["xs", b] = small.tile([P, P], U8, name="x_scales", align_bytes=64)
+            nc.vector.quantize_mx(st["xc", b][:].bitcast(E4), st["xs", b][:], st["xil", b][:].rearrange("p r t -> p (r t)"))
+
+        def mm1(b):
+            st["s", b] = bank([P, N])
+            nc.tensor.matmul_mx(st["s", b][:], lhsT=st["xc", b][:].bitcast(E4), lhsT_scale=st["xs", b][:],
                                 rhs=k_codes[:].bitcast(E4), rhs_scale=k_scales[:], start=True, stop=True)
-            ys = work.tile([P, PACK, P], F32, name="ys")
-            nc.vector.tensor_tensor(ys[:].rearrange("p j (q i) -> p j q i", i=RUN),
-                                    s[:].rearrange("p (q j i) -> p j q i", j=PACK, i=RUN), y_runs(b), MULT)
-            st["ys", b] = ys
 
-        def weigh(b):
-            yw = work.tile([P, PACK, P], F32, name="yw")
-            nc.vector.tensor_scalar(yw[:].rearrange("p j (q i) -> p j q i", i=RUN), y_runs(b), neg_wt[:, b : b + 1], None, MULT)
-            st["yw", b] = yw
+        def ys(b):
+            st["ys", b] = ring("V", [P, PACK, P], F32)
+            nc.vector.tensor_tensor(st["ys", b][:].rearrange("p j (q i) -> p j q i", i=RUN),
+                                    in_runs(st["s", b][:]), in_runs(y_raw[b // 2][:, b % 2, :]), MULT)
 
-        def margins(b):
-            ys_t = ps_o.tile([P, PACK, P], F32, name="o")
+        def yw(b):
+            e = engine_of("yw", b, "V")
+            st["yw", b] = ring(e, [P, PACK, P], F32)
+            dst, src = st["yw", b][:].rearrange("p j (q i) -> p j q i", i=RUN), in_runs(y_raw[b // 2][:, b % 2, :])
+            if e == "V":
+                nc.vector.tensor_scalar(dst, src, neg_wt[:, b : b + 1], None, MULT)
+            elif e == "S":
+                nc.scalar.activation(dst, src, ACT.Copy, scale=neg_wt[:, b : b + 1])
+            else:
+                nc.gpsimd.tensor_scalar(dst, src, neg_wt[:, b : b + 1], 0.0, MULT, ALU.add)
+
+        def tys(b):
+            st["tys", b] = bank([P, PACK, P])
             for j in range(PACK):
-                nc.tensor.transpose(ys_t[:, j, :], st["ys", b][:, j, :], ident[:])
-            yw_t = ps_o.tile([P, PACK, P], F32, name="o")
-            for j in range(PACK):
-                nc.tensor.transpose(yw_t[:, j, :], st["yw", b][:, j, :], ident[:])
-            margin = work.tile([P, PACK, P], F32, name="margin")
-            for j in range(PACK):
-                nc.scalar.activation(margin[:, j, :], ys_t[:, j, :], ACT.Relu, bias=abs_ts[:, j : j + 1], scale=neg_ts2[:, j : j + 1])
-            st["m", b] = (margin, yw_t)
+                nc.tensor.transpose(st["tys", b][:, j, :], st["ys", b][:, j, :], ident[:])
 
-        def grads(b):
-            margin, yw_t = st["m", b]
-            ht_bf = work.tile([P, P, PACK], BF16, name="ht_bf", align_bytes=64)
-            nc.vector.tensor_tensor(ht_bf[:].rearrange("p (c i) j -> p c j i", i=4),
-                                    yw_t[:].rearrange("p j (c i) -> p c j i", i=4),
-                                    margin[:].rearrange("p j (c i) -> p c j i", i=4), MULT)
-            st["h", b] = ht_bf
+        def tyw(b):
+            st["tyw", b] = bank([P, PACK, P])
+            for j in range(PACK):
+                nc.tensor.transpose(st["tyw", b][:, j, :], st["yw", b][:, j, :], ident[:])
 
-        def finish(b):
-            h_codes = work.tile([P, P], U32, name="h_codes", align_bytes=64)
-            h_scales = work.tile([P, P], U8, name="h_scales", align_bytes=64)
-            nc.vector.quantize_mx(h_codes[:].bitcast(E5), h_scales[:], st["h", b][:].rearrange("p r j -> p (r j)"))
-            o = ps_o.tile([P, D], F32, name="o")
-            nc.tensor.matmul_mx(o[:], lhsT=h_codes[:].bitcast(E5), lhsT_scale=h_scales[:],
+        def margin(b):
+            st["m", b] = ring("S", [P, PACK, P], F32)
+            for j in range(PACK):
+                nc.scalar.activation(st["m", b][:, j, :], st["tys", b][:, j, :], ACT.Relu,
+                                     bias=abs_ts[:, j : j + 1], scale=neg_ts2[:, j : j + 1])
+
+        def ht(b):
+            st["h", b] = ring("V", [P, P, PACK], BF16)
+            nc.vector.tensor_tensor(st["h", b][:].rearrange("p (c i) j -> p c j i", i=4),
+                                    st["tyw", b][:].rearrange("p j (c i) -> p c j i", i=4),
+                                    st["m", b][:].rearrange("p j (c i) -> p c j i", i=4), MULT)
+
+        def hq(b):
+            st["hc", b] = ring("V", [P, P], U32)
+            st["hs", b] = small.tile([P, P], U8, name="h_scales", align_bytes=64)
+            nc.vector.quantize_mx(st["hc", b][:].bitcast(E5), st["hs", b][:], st["h", b][:].rearrange("p r j -> p (r j)"))
+
+        def mm2(b):
+            st["o", b] = bank([P, D])
+            nc.tensor.matmul_mx(st["o", b][:], lhsT=st["hc", b][:].bitcast(E5), lhsT_scale=st["hs", b][:],
                                 rhs=kt_codes[:].bitcast(E4), rhs_scale=kt_scales[:], start=True, stop=True)
-            res = work.tile([P, P, PACK], F32, name="res")
-            nc.scalar.copy(res[:], o[:].rearrange("p (t q) -> p q t", t=PACK))
-            nc.sync.dma_start(out[b * P : (b + 1) * P, :], res[:].rearrange("p q t -> p (q t)"))
 
-        prep_x(0, P)
-        prep_x(P, P)
-        prep_x(2 * P, X_CHUNK)
-        scores(0)
-        weigh(0)
-        turn_plane(2)
-        turn_plane(3)
-        scores(1)
-        weigh(1)
-        margins(0)
-        prep_x(4 * P, X_CHUNK)
-        scores(2)
-        weigh(2)
-        margins(1)
-        grads(0)
-        scores(3)
-        weigh(3)
-        margins(2)
-        grads(1)
-        finish(0)
-        prep_x(6 * P, X_CHUNK)
-        scores(4)
-        weigh(4)
-        margins(3)
-        grads(2)
-        finish(1)
-        scores(5)
-        weigh(5)
-        margins(4)
-        grads(3)
-        finish(2)
-        scores(6)
-        weigh(6)
-        margins(5)
-        grads(4)
-        finish(3)
-        scores(7)
-        weigh(7)
-        margins(6)
-        grads(5)
-        finish(4)
-        margins(7)
-        grads(6)
-        finish(5)
-        grads(7)
-        finish(6)
-        finish(7)
+        def res(b):
+            e = engine_of("res", b, "S")
+            result = ring(e, [P, P, PACK], F32)
+            parts = 2 if b == BLOCKS - 1 else 1
+            w = P // parts
+            for a in range(parts):
+                qs = slice(a * w, (a + 1) * w)
+                copy(e, result[:, qs, :], st["o", b][:].rearrange("p (t q) -> p q t", t=PACK)[:, qs, :])
+                nc.sync.dma_start(out[b * P : (b + 1) * P, a * w * PACK : (a + 1) * w * PACK], result[:, qs, :].rearrange("p q t -> p (q t)"))
+
+        ORDER = [(gather, 0), (kruns, 0), (kturn, 0), (ktcopy, 0), (gather, 1), (kruns, 1), (kturn, 1), (ktcopy, 1), (gather, 2), (ktq, 0), (kruns, 2), (kturn, 2), (ktcopy, 2), (ktq, 1), (gather, 3), (kil, 0), (kil, 1), (ktq, 2), (kq, 0), (xil, 0), (xq, 0), (xil, 1), (yw, 0), (xq, 1), (mm1, 0), (kruns, 3), (xil, 2), (yw, 1), (ys, 0), (xq, 2), (mm1, 1), (xil, 3), (yw, 2), (ys, 1), (kturn, 3), (ktcopy, 3), (tys, 0), (xq, 3), (mm1, 2), (xil, 4), (yw, 3), (margin, 0), (tyw, 0), (ys, 2), (tys, 1), (xq, 4), (mm1, 3), (xil, 5), (ktq, 3), (yw, 4), (ht, 0), (margin, 1), (tyw, 1), (ys, 3), (tys, 2), (xq, 5), (mm1, 4), (hq, 0), (xil, 6), (yw, 5), (ht, 1), (margin, 2), (tyw, 2), (ys, 4), (tys, 3), (xq, 6), (mm2, 0), (mm1, 5), (hq, 1), (xil, 7), (yw, 6), (ht, 2), (margin, 3), (tyw, 3), (res, 0), (ys, 5), (tys, 4), (xq, 7), (mm2, 1), (mm1, 6), (hq, 2), (yw, 7), (ht, 3), (margin, 4), (tyw, 4), (res, 1), (ys, 6), (tys, 5), (mm2, 2), (mm1, 7), (hq, 3), (ht, 4), (margin, 5), (tyw, 5), (res, 2), (ys, 7), (tys, 6), (mm2, 3), (hq, 4), (ht, 5), (margin, 6), (tyw, 6), (res, 3), (tys, 7), (mm2, 4), (hq, 5), (ht, 6), (margin, 7), (tyw, 7), (res, 4), (mm2, 5), (hq, 6), (ht, 7), (res, 5), (mm2, 6), (hq, 7), (res, 6), (mm2, 7), (res, 7)]
+        for stage, b in ORDER:
+            stage(b)

@@ -11,237 +11,294 @@ BF16 = mybir.dt.bfloat16
 U32 = mybir.dt.uint32
 U16 = mybir.dt.uint16
 U8 = mybir.dt.uint8
-E4 = mybir.dt.float8_e4m3fn_x4
-E5 = mybir.dt.float8_e5m2_x4
+E4M3 = mybir.dt.float8_e4m3fn_x4
+E5M2 = mybir.dt.float8_e5m2_x4
 ALU = mybir.AluOpType
-MULT = ALU.mult
 ACT = mybir.ActivationFunctionType
 
 P = 128
 PACK = 4
 RUN = 8
+LIST = 16
 BLOCKS = R // P
-X_CHUNK = 256
-HALF = N // 2
-SPLIT = 256
+CHUNK = 2 * P
+HALVES = (slice(0, N // 2), slice(N // 2, N))
+LAST_PLANE = PACK - 1
+VECTOR_RING = 32
+SCALAR_RING = 20
+PSUM_BANKS = 8
 
 
 def tile_attend_gpq_sqh_x_kernel(tc, xT, cb, norm, ts, y, wt, offs, out):
     nc = tc.nc
     with ExitStack() as ctx:
         keep = ctx.enter_context(tc.tile_pool(name="keep", bufs=1))
-        by_vector = ctx.enter_context(tc.tile_pool(name="by_vector", bufs=32))
-        by_scalar = ctx.enter_context(tc.tile_pool(name="by_scalar", bufs=20))
-        by_gpsimd = ctx.enter_context(tc.tile_pool(name="by_gpsimd", bufs=8))
-        small = ctx.enter_context(tc.tile_pool(name="small", bufs=8))
-        banks = ctx.enter_context(tc.psum_pool(name="banks", bufs=8))
+        by_vector = ctx.enter_context(tc.tile_pool(name="by_vector", bufs=VECTOR_RING))
+        by_scalar = ctx.enter_context(tc.tile_pool(name="by_scalar", bufs=SCALAR_RING))
+        scales = ctx.enter_context(tc.tile_pool(name="scales", bufs=BLOCKS))
+        banks = ctx.enter_context(tc.psum_pool(name="banks", bufs=PSUM_BANKS))
 
-        def ring(engine, shape, dtype):
-            pool = {"V": by_vector, "S": by_scalar, "G": by_gpsimd}[engine]
-            return pool.tile(shape, dtype, name="ring", align_bytes=64)
+        def vector_tile(shape, dtype):
+            return by_vector.tile(shape, dtype, name="ring", align_bytes=64)
+
+        def scalar_tile(shape, dtype):
+            return by_scalar.tile(shape, dtype, name="ring", align_bytes=64)
 
         def bank(shape):
             return banks.tile(shape, F32, name="bank")
 
-        norm_c = keep.tile([P, PACK], F32, name="norm_c")
-        nc.sync.dma_start(norm_c[:], norm[0:1, :].rearrange("o (p j) -> (o p) j", j=PACK))
-        ts_c = keep.tile([P, PACK], F32, name="ts_c")
-        nc.sync.dma_start(ts_c[:], ts[0:1, :].rearrange("o (p j) -> (o p) j", j=PACK))
+        norm_cols = keep.tile([P, PACK], F32, name="norm_cols")
+        nc.sync.dma_start(norm_cols[:], norm[0:1, :].rearrange("o (p e) -> (o p) e", e=PACK))
+        ts_cols = keep.tile([P, PACK], F32, name="ts_cols")
+        nc.sync.dma_start(ts_cols[:], ts[0:1, :].rearrange("o (p e) -> (o p) e", e=PACK))
 
         cb_planes = cb.rearrange("(p t) c -> t p c", t=PACK)
-        x_rows = xT.rearrange("(p t) r -> p t r", t=PACK)
-        books, x_raw, y_raw = [], [], []
-
-        def load_book(t):
-            book = keep.tile([P, C], F32, name=f"book{t}")
-            nc.sync.dma_start(book[:], cb_planes[t])
-            books.append(book)
-
-        def load_x(c):
-            xc = keep.tile([P, PACK, X_CHUNK], F32, name=f"x{c}")
-            nc.sync.dma_start(xc[:], x_rows[:, :, c * X_CHUNK : (c + 1) * X_CHUNK])
-            x_raw.append(xc)
-
-        def load_y(c):
-            yc = keep.tile([P, 2, N], F32, name=f"y{c}")
-            nc.sync.dma_start(yc[:], y[c * X_CHUNK : (c + 1) * X_CHUNK, :].rearrange("(b p) n -> p b n", p=P))
-            y_raw.append(yc)
-
-        load_book(0)
-        offsets = keep.tile([P, N // 16], U16, name="offsets")
+        books = [keep.tile([P, C], F32, name=f"book{t}") for t in range(PACK)]
+        nc.sync.dma_start(books[0][:], cb_planes[0])
+        offsets = keep.tile([P, N // LIST], U16, name="offsets")
         nc.sync.dma_start(offsets[:], offs)
-        rows = keep.tile([P, P], F32, name="rows")
-        nc.vector.memset(rows[:], 0.0)
-        nc.sync.dma_start(rows[0:4, :].rearrange("j (q i) -> j q i", i=RUN),
-                          ts[0:1, :].rearrange("o (q j i) -> (o j) q i", j=PACK, i=RUN))
-        nc.sync.dma_start(rows[8:16, :], wt.rearrange("(b q) o -> b (q o)", q=P))
-        load_book(1)
-        load_book(2)
-        load_book(3)
-        load_x(0)
-        load_y(0)
-        load_x(1)
-        load_y(1)
-        load_x(2)
-        load_y(2)
-        load_x(3)
-        load_y(3)
+        wt_rows = keep.tile([P, P], F32, name="wt_rows")
+        nc.vector.memset(wt_rows[:], 0.0)
+        nc.sync.dma_start(wt_rows[0:BLOCKS, :], wt.rearrange("(b q) o -> b (q o)", q=P))
+        for t in range(1, PACK):
+            nc.sync.dma_start(books[t][:], cb_planes[t])
+
+        x_planes = xT.rearrange("(p t) r -> p t r", t=PACK)
+        x_raw, y_raw = [], []
+        for c in range(R // CHUNK):
+            rows = slice(c * CHUNK, (c + 1) * CHUNK)
+            x_raw.append(keep.tile([P, PACK, CHUNK], F32, name=f"x{c}"))
+            nc.sync.dma_start(x_raw[c][:], x_planes[:, :, rows])
+            y_raw.append(keep.tile([P, CHUNK // P, N], F32, name=f"y{c}"))
+            nc.sync.dma_start(y_raw[c][:], y[rows, :].rearrange("(b p) n -> p b n", p=P))
 
         ident = keep.tile([P, P], F32, name="ident")
         make_identity(nc, ident[:])
 
-        sign = keep.tile([P, PACK], F32, name="sign")
-        nc.vector.tensor_scalar(sign[:], ts_c[:], 0.0, 2.0, ALU.is_ge, MULT)
-        signed = keep.tile([P, PACK], F32, name="signed")
-        nc.vector.scalar_tensor_tensor(signed[:], sign[:], -1.0, norm_c[:], ALU.add, MULT)
-        norm_b = keep.tile([P, N], F32, name="norm_b")
-        spread = bank([P, PACK, P])
+        def spread(cols):
+            spread_bank = bank([P, PACK, P])
+            for e in range(PACK):
+                nc.tensor.transpose(spread_bank[:, e, :], cols[:, e : e + 1].to_broadcast([P, P]), ident[:])
+            return spread_bank
+
+        def turn(runs):
+            turned = bank([P, PACK, P])
+            for j in range(PACK):
+                nc.tensor.transpose(turned[:, j, :], runs[:, j, :], ident[:])
+            return turned
+
+        twice_step = keep.tile([P, PACK], F32, name="twice_step")
+        nc.vector.tensor_scalar(twice_step[:], ts_cols[:], 0.0, 2.0, ALU.is_ge, ALU.mult)
+        signed_cols = keep.tile([P, PACK], F32, name="signed_cols")
+        nc.vector.scalar_tensor_tensor(signed_cols[:], twice_step[:], -1.0, norm_cols[:], ALU.add, ALU.mult)
+        signed_norm = keep.tile([P, N], F32, name="signed_norm")
+        nc.scalar.copy(
+            signed_norm[:].rearrange("m (p e) -> m p e", e=PACK),
+            spread(signed_cols)[:].rearrange("m e p -> m p e"),
+        )
+
+        wt_bank = bank([P, P])
+        nc.tensor.transpose(wt_bank[:], wt_rows[:], ident[:])
+        ts_spread = spread(ts_cols)
+        ts_runs = keep.tile([P, PACK, P], F32, name="ts_runs")
         for j in range(PACK):
-            nc.tensor.transpose(spread[:, j, :], signed[:, j : j + 1].to_broadcast([P, P]), ident[:])
-        nc.scalar.copy(norm_b[:].rearrange("p (m j) -> p m j", j=PACK), spread[:].rearrange("p j m -> p m j"))
-
-        cols_ps = bank([P, P])
-        nc.tensor.transpose(cols_ps[:], rows[:], ident[:])
+            nc.scalar.activation(
+                ts_runs[:, j, :].rearrange("m (q g e) -> m q g e", g=2, e=PACK),
+                ts_spread[:].rearrange("m e (q j g) -> m j q g e", j=PACK, g=2)[:, j],
+                ACT.Abs,
+            )
         abs_ts = keep.tile([P, PACK], F32, name="abs_ts")
-        nc.scalar.activation(abs_ts[:], cols_ps[:, 0:4], ACT.Abs)
+        nc.scalar.copy(abs_ts[:], turn(ts_runs)[:, :, 0])
         neg_wt = keep.tile([P, BLOCKS], F32, name="neg_wt")
-        nc.scalar.activation(neg_wt[:], cols_ps[:, 8:16], ACT.Copy, scale=-1.0)
+        nc.scalar.activation(neg_wt[:], wt_bank[:, 0:BLOCKS], ACT.Copy, scale=-1.0)
+        neg_ts_squared = keep.tile([P, PACK], F32, name="neg_ts_squared")
 
-        neg_ts2 = keep.tile([P, PACK], F32, name="neg_ts2")
         k_f32 = keep.tile([P, PACK, N], F32, name="k_f32")
         k_bf = keep.tile([P, N, PACK], BF16, name="k_bf", align_bytes=64)
         k_scales = keep.tile([P, N], U8, name="k_scales", align_bytes=64)
         kt_codes = keep.tile([P, D], U32, name="kt_codes", align_bytes=64)
         kt_scales = keep.tile([P, D], U8, name="kt_scales", align_bytes=64)
         k_codes = keep.tile([P, N], U32, name="k_codes", align_bytes=64)
-        st = {}
-        ENG = {("kruns", 0): "V", ("kruns", 1): "V", ("kruns", 2): "V"}
+        made = {}
 
-        def engine_of(stage, b, default):
-            return ENG.get((stage, b), ENG.get(stage, default))
+        def interleave(copy, dst, src):
+            copy(dst.rearrange("p (c i) t -> p c t i", i=4), src.rearrange("p t (c i) -> p c t i", i=4))
 
-        def copy(e, dst, src):
-            if e == "S":
-                nc.scalar.copy(dst, src)
-            elif e == "V":
-                nc.vector.tensor_copy(dst, src)
-            else:
-                nc.gpsimd.tensor_scalar(dst, src, 1.0, 0.0, MULT, ALU.add)
+        def read_in_runs(by_column):
+            return by_column.rearrange("p (q j i) -> p j q i", j=PACK, i=RUN)
 
-        def interleave(e, dst, src):
-            copy(e, dst.rearrange("p (c i) t -> p c t i", i=4), src.rearrange("p t (c i) -> p c t i", i=4))
-
-        def in_runs(ap):
-            return ap.rearrange("p (q j i) -> p j q i", j=PACK, i=RUN)
+        def write_in_runs(runs):
+            return runs[:].rearrange("p j (q i) -> p j q i", i=RUN)
 
         def gather(t):
-            for lo, hi in ((0, SPLIT), (SPLIT, N)):
-                listed = books[t][:].indirect(offsets[:, lo // 16 : hi // 16])
-                nc.vector.tensor_tensor(k_f32[:, t, lo:hi], listed, norm_b[:, lo:hi], MULT)
+            for cols in HALVES:
+                listed = books[t][:].indirect(offsets[:, cols.start // LIST : cols.stop // LIST])
+                nc.vector.tensor_tensor(k_f32[:, t, cols], listed, signed_norm[:, cols], ALU.mult)
 
-            if t == 0:
-                nc.vector.scalar_tensor_tensor(neg_ts2[:], abs_ts[:], -1.0, abs_ts[:], MULT, MULT)
-
-        def kruns(t):
-            e = engine_of("kruns", t, "S")
-            st["kruns", t] = ring(e, [P, PACK, P], F32)
-            copy(e, st["kruns", t][:].rearrange("p j (q i) -> p j q i", i=RUN), in_runs(k_f32[:, t, :]))
-
-        def kturn(t):
-            st["kturn", t] = bank([P, PACK, P])
-            for j in range(PACK):
-                nc.tensor.transpose(st["kturn", t][:, j, :], st["kruns", t][:, j, :], ident[:])
-
-        def ktcopy(t):
-            e = engine_of("ktcopy", t, "S")
-            st["kt", t] = ring(e, [P, P, PACK], BF16)
-            copy(e, st["kt", t][:], st["kturn", t][:].rearrange("p j q -> p q j"))
-
-        def ktq(t):
-            ds = slice(t * P, (t + 1) * P)
-            nc.vector.quantize_mx(kt_codes[:, ds].bitcast(E4), kt_scales[:, ds], st["kt", t][:].rearrange("p d j -> p (d j)"))
-
-        def kil(half):
-            cs = (slice(0, SPLIT), slice(SPLIT, N))[half]
-            interleave(engine_of("kil", half, "SV"[half]), k_bf[:, cs, :], k_f32[:, :, cs])
-
-        def kq(z):
-            nc.vector.quantize_mx(k_codes[:].bitcast(E4), k_scales[:], k_bf[:].rearrange("p n t -> p (n t)"))
-
-        def xil(b):
-            e = engine_of("xil", b, "S")
-            c0 = b * P % X_CHUNK
-            st["xil", b] = ring(e, [P, P, PACK], BF16)
-            interleave(e, st["xil", b][:], x_raw[b // 2][:, :, c0 : c0 + P])
-
-        def xq(b):
-            st["xc", b] = ring("V", [P, P], U32)
-            st["xs", b] = small.tile([P, P], U8, name="x_scales", align_bytes=64)
-            nc.vector.quantize_mx(st["xc", b][:].bitcast(E4), st["xs", b][:], st["xil", b][:].rearrange("p r t -> p (r t)"))
-
-        def mm1(b):
-            st["s", b] = bank([P, N])
-            nc.tensor.matmul_mx(st["s", b][:], lhsT=st["xc", b][:].bitcast(E4), lhsT_scale=st["xs", b][:],
-                                rhs=k_codes[:].bitcast(E4), rhs_scale=k_scales[:], start=True, stop=True)
-
-        def ys(b):
-            st["ys", b] = ring("V", [P, PACK, P], F32)
-            nc.vector.tensor_tensor(st["ys", b][:].rearrange("p j (q i) -> p j q i", i=RUN),
-                                    in_runs(st["s", b][:]), in_runs(y_raw[b // 2][:, b % 2, :]), MULT)
-
-        def yw(b):
-            e = engine_of("yw", b, "V")
-            st["yw", b] = ring(e, [P, PACK, P], F32)
-            dst, src = st["yw", b][:].rearrange("p j (q i) -> p j q i", i=RUN), in_runs(y_raw[b // 2][:, b % 2, :])
-            if e == "V":
-                nc.vector.tensor_scalar(dst, src, neg_wt[:, b : b + 1], None, MULT)
-            elif e == "S":
-                nc.scalar.activation(dst, src, ACT.Copy, scale=neg_wt[:, b : b + 1])
+        def k_runs(t):
+            if t == LAST_PLANE:
+                made["k_runs", t] = scalar_tile([P, PACK, P], F32)
+                nc.scalar.copy(write_in_runs(made["k_runs", t]), read_in_runs(k_f32[:, t, :]))
             else:
-                nc.gpsimd.tensor_scalar(dst, src, neg_wt[:, b : b + 1], 0.0, MULT, ALU.add)
+                made["k_runs", t] = vector_tile([P, PACK, P], F32)
+                nc.vector.tensor_copy(write_in_runs(made["k_runs", t]), read_in_runs(k_f32[:, t, :]))
 
-        def tys(b):
-            st["tys", b] = bank([P, PACK, P])
-            for j in range(PACK):
-                nc.tensor.transpose(st["tys", b][:, j, :], st["ys", b][:, j, :], ident[:])
+        def k_turn(t):
+            made["k_turned", t] = turn(made["k_runs", t])
 
-        def tyw(b):
-            st["tyw", b] = bank([P, PACK, P])
-            for j in range(PACK):
-                nc.tensor.transpose(st["tyw", b][:, j, :], st["yw", b][:, j, :], ident[:])
+        def kt_round(t):
+            made["kt_bf", t] = scalar_tile([P, P, PACK], BF16)
+            nc.scalar.copy(made["kt_bf", t][:], made["k_turned", t][:].rearrange("p j w -> p w j"))
+
+        def kt_quantise(t):
+            cols = slice(t * P, (t + 1) * P)
+            nc.vector.quantize_mx(
+                kt_codes[:, cols].bitcast(E4M3), kt_scales[:, cols], made["kt_bf", t][:].rearrange("p w j -> p (w j)")
+            )
+
+        def k_quantise(cols):
+            nc.vector.quantize_mx(
+                k_codes[:, cols].bitcast(E4M3), k_scales[:, cols], k_bf[:, cols, :].rearrange("p n t -> p (n t)")
+            )
+
+        def y_block(b):
+            return y_raw[b * P // CHUNK][:, b % (CHUNK // P), :]
+
+        def x_round(b):
+            first = b * P % CHUNK
+            made["x_bf", b] = scalar_tile([P, P, PACK], BF16)
+            interleave(nc.scalar.copy, made["x_bf", b][:], x_raw[b * P // CHUNK][:, :, first : first + P])
+
+        def x_quantise(b):
+            made["x_codes", b] = vector_tile([P, P], U32)
+            made["x_scales", b] = scales.tile([P, P], U8, name="x_scales", align_bytes=64)
+            nc.vector.quantize_mx(
+                made["x_codes", b][:].bitcast(E4M3), made["x_scales", b][:], made["x_bf", b][:].rearrange("p r t -> p (r t)")
+            )
+
+        def scores(b):
+            made["s", b] = bank([P, N])
+            nc.tensor.matmul_mx(
+                made["s", b][:],
+                lhsT=made["x_codes", b][:].bitcast(E4M3),
+                lhsT_scale=made["x_scales", b][:],
+                rhs=k_codes[:].bitcast(E4M3),
+                rhs_scale=k_scales[:],
+                start=True,
+                stop=True,
+            )
+
+        def y_times_s(b):
+            made["ys", b] = vector_tile([P, PACK, P], F32)
+            nc.vector.tensor_tensor(
+                write_in_runs(made["ys", b]), read_in_runs(made["s", b][:]), read_in_runs(y_block(b)), ALU.mult
+            )
+
+        def y_times_wt(b):
+            made["yw", b] = vector_tile([P, PACK, P], F32)
+            nc.vector.tensor_scalar(
+                write_in_runs(made["yw", b]), read_in_runs(y_block(b)), neg_wt[:, b : b + 1], None, ALU.mult
+            )
+
+        def ys_turn(b):
+            made["ys_turned", b] = turn(made["ys", b])
+
+        def yw_turn(b):
+            made["yw_turned", b] = turn(made["yw", b])
 
         def margin(b):
-            st["m", b] = ring("S", [P, PACK, P], F32)
+            made["margin", b] = scalar_tile([P, PACK, P], F32)
             for j in range(PACK):
-                nc.scalar.activation(st["m", b][:, j, :], st["tys", b][:, j, :], ACT.Relu,
-                                     bias=abs_ts[:, j : j + 1], scale=neg_ts2[:, j : j + 1])
+                nc.scalar.activation(
+                    made["margin", b][:, j, :],
+                    made["ys_turned", b][:, j, :],
+                    ACT.Relu,
+                    bias=abs_ts[:, j : j + 1],
+                    scale=neg_ts_squared[:, j : j + 1],
+                )
 
-        def ht(b):
-            st["h", b] = ring("V", [P, P, PACK], BF16)
-            nc.vector.tensor_tensor(st["h", b][:].rearrange("p (c i) j -> p c j i", i=4),
-                                    st["tyw", b][:].rearrange("p j (c i) -> p c j i", i=4),
-                                    st["m", b][:].rearrange("p j (c i) -> p c j i", i=4), MULT)
+        def h_round(b):
+            made["h_bf", b] = vector_tile([P, P, PACK], BF16)
+            nc.vector.tensor_tensor(
+                made["h_bf", b][:].rearrange("p (c i) j -> p c j i", i=4),
+                made["yw_turned", b][:].rearrange("p j (c i) -> p c j i", i=4),
+                made["margin", b][:].rearrange("p j (c i) -> p c j i", i=4),
+                ALU.mult,
+            )
 
-        def hq(b):
-            st["hc", b] = ring("V", [P, P], U32)
-            st["hs", b] = small.tile([P, P], U8, name="h_scales", align_bytes=64)
-            nc.vector.quantize_mx(st["hc", b][:].bitcast(E5), st["hs", b][:], st["h", b][:].rearrange("p r j -> p (r j)"))
+        def h_quantise(b):
+            made["h_codes", b] = vector_tile([P, P], U32)
+            made["h_scales", b] = scales.tile([P, P], U8, name="h_scales", align_bytes=64)
+            nc.vector.quantize_mx(
+                made["h_codes", b][:].bitcast(E5M2), made["h_scales", b][:], made["h_bf", b][:].rearrange("p r j -> p (r j)")
+            )
 
-        def mm2(b):
-            st["o", b] = bank([P, D])
-            nc.tensor.matmul_mx(st["o", b][:], lhsT=st["hc", b][:].bitcast(E5), lhsT_scale=st["hs", b][:],
-                                rhs=kt_codes[:].bitcast(E4), rhs_scale=kt_scales[:], start=True, stop=True)
+        def gradient(b):
+            made["o", b] = bank([P, D])
+            nc.tensor.matmul_mx(
+                made["o", b][:],
+                lhsT=made["h_codes", b][:].bitcast(E5M2),
+                lhsT_scale=made["h_scales", b][:],
+                rhs=kt_codes[:].bitcast(E4M3),
+                rhs_scale=kt_scales[:],
+                start=True,
+                stop=True,
+            )
 
-        def res(b):
-            e = engine_of("res", b, "S")
-            result = ring(e, [P, P, PACK], F32)
+        def store(b):
+            result = scalar_tile([P, P, PACK], F32)
             parts = 2 if b == BLOCKS - 1 else 1
-            w = P // parts
-            for a in range(parts):
-                qs = slice(a * w, (a + 1) * w)
-                copy(e, result[:, qs, :], st["o", b][:].rearrange("p (t q) -> p q t", t=PACK)[:, qs, :])
-                nc.sync.dma_start(out[b * P : (b + 1) * P, a * w * PACK : (a + 1) * w * PACK], result[:, qs, :].rearrange("p q t -> p (q t)"))
+            width = P // parts
+            for part in range(parts):
+                piece = slice(part * width, (part + 1) * width)
+                nc.scalar.copy(result[:, piece, :], made["o", b][:].rearrange("r (t p) -> r p t", t=PACK)[:, piece, :])
+                nc.sync.dma_start(
+                    out[b * P : (b + 1) * P, piece.start * PACK : piece.stop * PACK],
+                    result[:, piece, :].rearrange("r p t -> r (p t)"),
+                )
 
-        ORDER = [(gather, 0), (kruns, 0), (kturn, 0), (ktcopy, 0), (gather, 1), (kruns, 1), (kturn, 1), (ktcopy, 1), (gather, 2), (ktq, 0), (kruns, 2), (kturn, 2), (ktcopy, 2), (ktq, 1), (gather, 3), (kil, 0), (kil, 1), (ktq, 2), (kq, 0), (xil, 0), (xq, 0), (xil, 1), (yw, 0), (xq, 1), (mm1, 0), (kruns, 3), (xil, 2), (yw, 1), (ys, 0), (xq, 2), (mm1, 1), (xil, 3), (yw, 2), (ys, 1), (kturn, 3), (ktcopy, 3), (tys, 0), (xq, 3), (mm1, 2), (xil, 4), (yw, 3), (margin, 0), (tyw, 0), (ys, 2), (tys, 1), (xq, 4), (mm1, 3), (xil, 5), (ktq, 3), (yw, 4), (ht, 0), (margin, 1), (tyw, 1), (ys, 3), (tys, 2), (xq, 5), (mm1, 4), (hq, 0), (xil, 6), (yw, 5), (ht, 1), (margin, 2), (tyw, 2), (ys, 4), (tys, 3), (xq, 6), (mm2, 0), (mm1, 5), (hq, 1), (xil, 7), (yw, 6), (ht, 2), (margin, 3), (tyw, 3), (res, 0), (ys, 5), (tys, 4), (xq, 7), (mm2, 1), (mm1, 6), (hq, 2), (yw, 7), (ht, 3), (margin, 4), (tyw, 4), (res, 1), (ys, 6), (tys, 5), (mm2, 2), (mm1, 7), (hq, 3), (ht, 4), (margin, 5), (tyw, 5), (res, 2), (ys, 7), (tys, 6), (mm2, 3), (hq, 4), (ht, 5), (margin, 6), (tyw, 6), (res, 3), (tys, 7), (mm2, 4), (hq, 5), (ht, 6), (margin, 7), (tyw, 7), (res, 4), (mm2, 5), (hq, 6), (ht, 7), (res, 5), (mm2, 6), (hq, 7), (res, 6), (mm2, 7), (res, 7)]
-        for stage, b in ORDER:
-            stage(b)
+        for t in range(LAST_PLANE):
+            gather(t)
+            if t == 1:
+                nc.vector.scalar_tensor_tensor(neg_ts_squared[:], abs_ts[:], -1.0, abs_ts[:], ALU.mult, ALU.mult)
+                interleave(nc.scalar.copy, k_bf[:, :, 0:2], k_f32[:, 0:2, :])
+                kt_quantise(0)
+            k_runs(t)
+            if t == 2:
+                kt_quantise(1)
+            k_turn(t)
+            kt_round(t)
+        gather(LAST_PLANE)
+        interleave(nc.scalar.copy, k_bf[:, HALVES[0], 2:4], k_f32[:, 2:4, HALVES[0]])
+        interleave(nc.vector.tensor_copy, k_bf[:, HALVES[1], 2:4], k_f32[:, 2:4, HALVES[1]])
+        kt_quantise(2)
+        k_quantise(HALVES[1])
+        k_quantise(HALVES[0])
+
+        pipeline = (
+            (margin, 2),
+            (y_times_s, 0),
+            (x_round, -2),
+            (kt_round, 1),
+            (store, 5),
+            (yw_turn, 2),
+            (ys_turn, 1),
+            (h_quantise, 3),
+            (h_round, 2),
+            (gradient, 4),
+            (scores, -1),
+            (kt_quantise, 2),
+            (x_quantise, -2),
+            (k_runs, -1),
+            (y_times_wt, -2),
+            (k_turn, 0),
+        )
+        plane_stages = (k_runs, k_turn, kt_round, kt_quantise)
+        lags = [lag for stage, lag in pipeline]
+        for step in range(min(lags), BLOCKS + max(lags)):
+            for stage, lag in pipeline:
+                if stage in plane_stages:
+                    if step == lag:
+                        stage(LAST_PLANE)
+                elif 0 <= step - lag < BLOCKS:
+                    stage(step - lag)

@@ -28,6 +28,17 @@ VECTOR_RING = 32
 SCALAR_RING = 20
 PSUM_BANKS = 8
 
+VECTOR_ORDER = (
+    "xq yw yw xq kq kq ys kq xq ys xq yw yw ys hr kq xq ys xq hq yw hr ys hr hq xq yw hq "
+    "xq ys hr yw ys ys hq hr hr hq yw hq hr hq hr hq"
+).split()
+SCALAR_ORDER = (
+    "xr xr kc xr xr m xr xr m m xr st xr m m st st m m m st st st st st"
+).split()
+TENSOR_ORDER = (
+    "S S tw ty S S tw ty tw ty S G S ty tw ty G S G S ty tw tw ty ty tw G G tw G G G"
+).split()
+
 
 def tile_attend_gpq_sqh_x_kernel(tc, xT, cb, norm, ts, y, wt, offs, out):
     nc = tc.nc
@@ -91,7 +102,7 @@ def tile_attend_gpq_sqh_x_kernel(tc, xT, cb, norm, ts, y, wt, offs, out):
         nc.vector.tensor_scalar(twice_step[:], ts_cols[:], 0.0, 2.0, ALU.is_ge, ALU.mult)
         signed_cols = keep.tile([P, PACK], F32, name="signed_cols")
         nc.vector.scalar_tensor_tensor(signed_cols[:], twice_step[:], -1.0, norm_cols[:], ALU.add, ALU.mult)
-        signed_norm = keep.tile([P, N], F32, name="signed_norm")
+        signed_norm = keep.tile([P, N], F32, name="signed_norm", tag="norm_then_codes", align_bytes=64)
         nc.scalar.copy(
             signed_norm[:].rearrange("m (p e) -> m p e", e=PACK),
             spread(signed_cols)[:].rearrange("m e p -> m p e"),
@@ -116,7 +127,7 @@ def tile_attend_gpq_sqh_x_kernel(tc, xT, cb, norm, ts, y, wt, offs, out):
         k_f32 = keep.tile([P, PACK, N], F32, name="k_f32")
         k_bf = keep.tile([P, N, PACK], BF16, name="k_bf", align_bytes=64)
         k_scales = keep.tile([P, N], U8, name="k_scales", align_bytes=64)
-        kt_codes = keep.tile([P, D], U32, name="kt_codes", align_bytes=64)
+        kt_codes = keep.tile([P, D], U32, name="kt_codes", tag="norm_then_codes", align_bytes=64)
         kt_scales = keep.tile([P, D], U8, name="kt_scales", align_bytes=64)
         k_codes = keep.tile([P, N], U32, name="k_codes", align_bytes=64)
         made = {}
@@ -257,48 +268,41 @@ def tile_attend_gpq_sqh_x_kernel(tc, xT, cb, norm, ts, y, wt, offs, out):
                     result[:, piece, :].rearrange("r p t -> r (p t)"),
                 )
 
-        for t in range(LAST_PLANE):
+        for t in range(PACK):
             gather(t)
             if t == 1:
                 nc.vector.scalar_tensor_tensor(neg_ts_squared[:], abs_ts[:], -1.0, abs_ts[:], ALU.mult, ALU.mult)
                 interleave(nc.scalar.copy, k_bf[:, :, 0:2], k_f32[:, 0:2, :])
-                kt_quantise(0)
             k_runs(t)
-            if t == 2:
-                kt_quantise(1)
             k_turn(t)
-            kt_round(t)
-        gather(LAST_PLANE)
-        interleave(nc.scalar.copy, k_bf[:, HALVES[0], 2:4], k_f32[:, 2:4, HALVES[0]])
-        interleave(nc.vector.tensor_copy, k_bf[:, HALVES[1], 2:4], k_f32[:, 2:4, HALVES[1]])
-        kt_quantise(2)
-        k_quantise(HALVES[1])
-        k_quantise(HALVES[0])
+            if t < LAST_PLANE:
+                kt_round(t)
+        for cols in HALVES:
+            interleave(nc.vector.tensor_copy, k_bf[:, cols, 2:4], k_f32[:, 2:4, cols])
+        for cols in HALVES:
+            k_quantise(cols)
 
-        pipeline = (
-            (margin, 2),
-            (y_times_s, 0),
-            (x_round, -2),
-            (kt_round, 1),
-            (store, 5),
-            (yw_turn, 2),
-            (ys_turn, 1),
-            (h_quantise, 3),
-            (h_round, 2),
-            (gradient, 4),
-            (scores, -1),
-            (kt_quantise, 2),
-            (x_quantise, -2),
-            (k_runs, -1),
-            (y_times_wt, -2),
-            (k_turn, 0),
-        )
-        plane_stages = (k_runs, k_turn, kt_round, kt_quantise)
-        lags = [lag for stage, lag in pipeline]
-        for step in range(min(lags), BLOCKS + max(lags)):
-            for stage, lag in pipeline:
-                if stage in plane_stages:
-                    if step == lag:
-                        stage(LAST_PLANE)
-                elif 0 <= step - lag < BLOCKS:
-                    stage(step - lag)
+        stages = {
+            "xr": (x_round, 0, ()),
+            "xq": (x_quantise, 0, ("xr",)),
+            "S": (scores, 0, ("xq",)),
+            "ys": (y_times_s, 0, ("S",)),
+            "yw": (y_times_wt, 0, ()),
+            "ty": (ys_turn, 0, ("ys",)),
+            "tw": (yw_turn, 0, ("yw",)),
+            "m": (margin, 0, ("ty",)),
+            "hr": (h_round, 0, ("m", "tw")),
+            "hq": (h_quantise, 0, ("hr",)),
+            "G": (gradient, 0, ("hq",)),
+            "st": (store, 0, ("G",)),
+            "kc": (kt_round, LAST_PLANE, ()),
+            "kq": (kt_quantise, 0, ("kc",)),
+        }
+        upcoming = {word: first for word, (stage, first, reads) in stages.items()}
+        left = [list(VECTOR_ORDER), list(SCALAR_ORDER), list(TENSOR_ORDER)]
+        while any(left):
+            for order in left:
+                while order and all(upcoming[read] > upcoming[order[0]] for read in stages[order[0]][2]):
+                    word = order.pop(0)
+                    stages[word][0](upcoming[word])
+                    upcoming[word] += 1

@@ -27,6 +27,7 @@ LAST_PLANE = PACK - 1
 VECTOR_RING = 32
 SCALAR_RING = 20
 PSUM_BANKS = 8
+WARM_PASSES = 4
 
 VECTOR_ORDER = (
     "xq yw yw xq kq kq ys kq xq ys xq yw yw ys hr kq xq ys xq hq yw hr ys hr hq xq yw hq "
@@ -268,6 +269,25 @@ def tile_attend_gpq_sqh_x_kernel(tc, xT, cb, norm, ts, y, wt, offs, out):
                     result[:, piece, :].rearrange("r p t -> r (p t)"),
                 )
 
+        warm_bf = keep.tile([P, N * PACK], BF16, name="warm_bf", align_bytes=64)
+        nc.vector.memset(warm_bf[:], 1.0)
+        warm_codes = keep.tile([P, N], U32, name="warm_codes", align_bytes=64)
+        warm_scales = keep.tile([P, N], U8, name="warm_scales", align_bytes=64)
+        nc.vector.quantize_mx(warm_codes[:].bitcast(E4M3), warm_scales[:], warm_bf[:])
+
+        def warm_up():
+            warm_bank = bank([P, N])
+            for step in range(WARM_PASSES):
+                nc.tensor.matmul_mx(
+                    warm_bank[:],
+                    lhsT=warm_codes[:, 0:P].bitcast(E4M3),
+                    lhsT_scale=warm_scales[:, 0:P],
+                    rhs=warm_codes[:].bitcast(E4M3),
+                    rhs_scale=warm_scales[:],
+                    start=True,
+                    stop=True,
+                )
+
         for t in range(PACK):
             gather(t)
             if t == 1:
@@ -275,6 +295,8 @@ def tile_attend_gpq_sqh_x_kernel(tc, xT, cb, norm, ts, y, wt, offs, out):
                 interleave(nc.scalar.copy, k_bf[:, :, 0:2], k_f32[:, 0:2, :])
             k_runs(t)
             k_turn(t)
+            if t == LAST_PLANE - 1:
+                warm_up()
             if t < LAST_PLANE:
                 kt_round(t)
         for cols in HALVES:

@@ -8,6 +8,7 @@ FLOPS = 2 * 2 * R * N * D
 
 F32 = mybir.dt.float32
 BF16 = mybir.dt.bfloat16
+I32 = mybir.dt.int32
 U32 = mybir.dt.uint32
 U16 = mybir.dt.uint16
 U8 = mybir.dt.uint8
@@ -22,23 +23,19 @@ RUN = 8
 LIST = 16
 BLOCKS = R // P
 CHUNK = 2 * P
-HALVES = (slice(0, N // 2), slice(N // 2, N))
-LAST_PLANE = PACK - 1
+HALF = N // 2
 VECTOR_RING = 32
 SCALAR_RING = 20
+POOL_RING = 8
 PSUM_BANKS = 8
 WARM_PASSES = 4
+BF16_ONES = 0x3F803F80
 
-VECTOR_ORDER = (
-    "xq yw yw xq kq kq ys kq xq ys xq yw yw ys hr kq xq ys xq hq yw hr ys hr hq xq yw hq "
-    "xq ys hr yw ys ys hq hr hr hq yw hq hr hq hr hq"
-).split()
-SCALAR_ORDER = (
-    "xr xr kc xr xr m xr xr m m xr st xr m m st st m m m st st st st st"
-).split()
-TENSOR_ORDER = (
-    "S S tw ty S S tw ty tw ty S G S ty tw ty G S G S ty tw tw ty ty tw G G tw G G G"
-).split()
+STEP = {"ys":0,"S":-2,"xq":-3,"ty":1,"xr":-4,"m":2,"hr":3,"hq":4,"G":5,"st":6,"tw":1,"yw":0}
+X_ROUND = "SSSSSSSS"
+Y_WT = "GGGGGGGG"
+STORE = "SSSSSSVS"
+ORDER = {"V":"ys hr yw xr hq xq k st","S":"m st yw xr k","P":"ty tw k G S","G":"yw xr"}
 
 
 def tile_attend_gpq_sqh_x_kernel(tc, xT, cb, norm, ts, y, wt, offs, out):
@@ -47,6 +44,7 @@ def tile_attend_gpq_sqh_x_kernel(tc, xT, cb, norm, ts, y, wt, offs, out):
         keep = ctx.enter_context(tc.tile_pool(name="keep", bufs=1))
         by_vector = ctx.enter_context(tc.tile_pool(name="by_vector", bufs=VECTOR_RING))
         by_scalar = ctx.enter_context(tc.tile_pool(name="by_scalar", bufs=SCALAR_RING))
+        by_pool = ctx.enter_context(tc.tile_pool(name="by_pool", bufs=POOL_RING))
         scales = ctx.enter_context(tc.tile_pool(name="scales", bufs=BLOCKS))
         banks = ctx.enter_context(tc.psum_pool(name="banks", bufs=PSUM_BANKS))
 
@@ -55,6 +53,9 @@ def tile_attend_gpq_sqh_x_kernel(tc, xT, cb, norm, ts, y, wt, offs, out):
 
         def scalar_tile(shape, dtype):
             return by_scalar.tile(shape, dtype, name="ring", align_bytes=64)
+
+        def pool_tile(shape, dtype):
+            return by_pool.tile(shape, dtype, name="ring", align_bytes=64)
 
         def bank(shape):
             return banks.tile(shape, F32, name="bank")
@@ -76,13 +77,24 @@ def tile_attend_gpq_sqh_x_kernel(tc, xT, cb, norm, ts, y, wt, offs, out):
             nc.sync.dma_start(books[t][:], cb_planes[t])
 
         x_planes = xT.rearrange("(p t) r -> p t r", t=PACK)
-        x_raw, y_raw = [], []
-        for c in range(R // CHUNK):
-            rows = slice(c * CHUNK, (c + 1) * CHUNK)
-            x_raw.append(keep.tile([P, PACK, CHUNK], F32, name=f"x{c}"))
-            nc.sync.dma_start(x_raw[c][:], x_planes[:, :, rows])
-            y_raw.append(keep.tile([P, CHUNK // P, N], F32, name=f"y{c}"))
-            nc.sync.dma_start(y_raw[c][:], y[rows, :].rearrange("(b p) n -> p b n", p=P))
+        x_raw, y_raw = {}, {}
+
+        def load_x(c):
+            x_raw[c] = keep.tile([P, PACK, CHUNK], F32, name=f"x{c}")
+            nc.sync.dma_start(x_raw[c][:], x_planes[:, :, c * CHUNK : (c + 1) * CHUNK])
+
+        def load_y(c):
+            y_raw[c] = keep.tile([P, CHUNK // P, N], F32, name=f"y{c}")
+            nc.sync.dma_start(y_raw[c][:], y[c * CHUNK : (c + 1) * CHUNK, :].rearrange("(b p) n -> p b n", p=P))
+
+        load_x(0)
+        load_x(1)
+        load_y(0)
+        load_x(2)
+        load_y(1)
+        load_x(3)
+        load_y(2)
+        load_y(3)
 
         ident = keep.tile([P, P], F32, name="ident")
         make_identity(nc, ident[:])
@@ -99,15 +111,34 @@ def tile_attend_gpq_sqh_x_kernel(tc, xT, cb, norm, ts, y, wt, offs, out):
                 nc.tensor.transpose(turned[:, j, :], runs[:, j, :], ident[:])
             return turned
 
-        twice_step = keep.tile([P, PACK], F32, name="twice_step")
+        twice_step = vector_tile([P, PACK], F32)
         nc.vector.tensor_scalar(twice_step[:], ts_cols[:], 0.0, 2.0, ALU.is_ge, ALU.mult)
-        signed_cols = keep.tile([P, PACK], F32, name="signed_cols")
+        signed_cols = vector_tile([P, PACK], F32)
         nc.vector.scalar_tensor_tensor(signed_cols[:], twice_step[:], -1.0, norm_cols[:], ALU.add, ALU.mult)
         signed_norm = keep.tile([P, N], F32, name="signed_norm", tag="norm_then_codes", align_bytes=64)
         nc.scalar.copy(
             signed_norm[:].rearrange("m (p e) -> m p e", e=PACK),
             spread(signed_cols)[:].rearrange("m e p -> m p e"),
         )
+
+        warm_bf = keep.tile([P, N * PACK], BF16, name="warm_bf", align_bytes=64)
+        nc.gpsimd.memset(warm_bf[:].bitcast(I32), BF16_ONES)
+        warm_codes = vector_tile([P, N], U32)
+        warm_scales = keep.tile([P, N], U8, name="warm_scales", align_bytes=64)
+        nc.vector.quantize_mx(warm_codes[:].bitcast(E4M3), warm_scales[:], warm_bf[:])
+
+        def warm_up():
+            warm_bank = bank([P, N])
+            for step in range(WARM_PASSES):
+                nc.tensor.matmul_mx(
+                    warm_bank[:],
+                    lhsT=warm_codes[:, 0:P].bitcast(E4M3),
+                    lhsT_scale=warm_scales[:, 0:P],
+                    rhs=warm_codes[:].bitcast(E4M3),
+                    rhs_scale=warm_scales[:],
+                    start=True,
+                    stop=True,
+                )
 
         wt_bank = bank([P, P])
         nc.tensor.transpose(wt_bank[:], wt_rows[:], ident[:])
@@ -133,44 +164,42 @@ def tile_attend_gpq_sqh_x_kernel(tc, xT, cb, norm, ts, y, wt, offs, out):
         k_codes = keep.tile([P, N], U32, name="k_codes", align_bytes=64)
         made = {}
 
-        def interleave(copy, dst, src):
-            copy(dst.rearrange("p (c i) t -> p c t i", i=4), src.rearrange("p t (c i) -> p c t i", i=4))
-
         def read_in_runs(by_column):
             return by_column.rearrange("p (q j i) -> p j q i", j=PACK, i=RUN)
 
         def write_in_runs(runs):
-            return runs[:].rearrange("p j (q i) -> p j q i", i=RUN)
+            return runs.rearrange("p j (q i) -> p j q i", i=RUN)
 
-        def gather(t):
-            for cols in HALVES:
-                listed = books[t][:].indirect(offsets[:, cols.start // LIST : cols.stop // LIST])
-                nc.vector.tensor_tensor(k_f32[:, t, cols], listed, signed_norm[:, cols], ALU.mult)
+        def gather(t, half):
+            cols = slice(half * HALF, (half + 1) * HALF)
+            listed = books[t][:].indirect(offsets[:, cols.start // LIST : cols.stop // LIST])
+            nc.vector.tensor_tensor(k_f32[:, t, cols], listed, signed_norm[:, cols], ALU.mult)
 
-        def k_runs(t):
-            if t == LAST_PLANE:
-                made["k_runs", t] = scalar_tile([P, PACK, P], F32)
-                nc.scalar.copy(write_in_runs(made["k_runs", t]), read_in_runs(k_f32[:, t, :]))
-            else:
-                made["k_runs", t] = vector_tile([P, PACK, P], F32)
-                nc.vector.tensor_copy(write_in_runs(made["k_runs", t]), read_in_runs(k_f32[:, t, :]))
+        def k_round(copy, u, half):
+            qs = slice(half * 8, (half + 1) * 8)
+            dst = k_bf[:].rearrange("p (j q i) t -> p q j t i", j=PACK, i=RUN)[:, qs, :, 2 * u : 2 * u + 2, :]
+            src = k_f32[:].rearrange("p t (q j i) -> p q j t i", j=PACK, i=RUN)[:, qs, :, 2 * u : 2 * u + 2, :]
+            copy(dst, src)
 
-        def k_turn(t):
-            made["k_turned", t] = turn(made["k_runs", t])
-
-        def kt_round(t):
-            made["kt_bf", t] = scalar_tile([P, P, PACK], BF16)
-            nc.scalar.copy(made["kt_bf", t][:], made["k_turned", t][:].rearrange("p j w -> p w j"))
-
-        def kt_quantise(t):
-            cols = slice(t * P, (t + 1) * P)
-            nc.vector.quantize_mx(
-                kt_codes[:, cols].bitcast(E4M3), kt_scales[:, cols], made["kt_bf", t][:].rearrange("p w j -> p (w j)")
-            )
-
-        def k_quantise(cols):
+        def k_quantise(half):
+            cols = slice(half * HALF, (half + 1) * HALF)
             nc.vector.quantize_mx(
                 k_codes[:, cols].bitcast(E4M3), k_scales[:, cols], k_bf[:, cols, :].rearrange("p n t -> p (n t)")
+            )
+
+        def k_turn(u):
+            words = k_bf[:].rearrange("p n t -> p (n t)").bitcast(F32).rearrange("p (j m u) -> p j m u", j=PACK, u=2)
+            made["k_turned", u] = turn(words[:, :, :, u])
+
+        def kt_copy(u):
+            made["kt_bf", u] = scalar_tile([P, 2 * P, PACK], BF16)
+            turned = made["k_turned", u][:].rearrange("m j p -> m (j p)").bitcast(BF16)
+            nc.scalar.copy(made["kt_bf", u][:], turned.rearrange("m (j c) -> m c j", j=PACK))
+
+        def kt_quantise(u):
+            cols = slice(u * 2 * P, (u + 1) * 2 * P)
+            nc.vector.quantize_mx(
+                kt_codes[:, cols].bitcast(E4M3), kt_scales[:, cols], made["kt_bf", u][:].rearrange("p c j -> p (c j)")
             )
 
         def y_block(b):
@@ -178,8 +207,16 @@ def tile_attend_gpq_sqh_x_kernel(tc, xT, cb, norm, ts, y, wt, offs, out):
 
         def x_round(b):
             first = b * P % CHUNK
-            made["x_bf", b] = scalar_tile([P, P, PACK], BF16)
-            interleave(nc.scalar.copy, made["x_bf", b][:], x_raw[b * P // CHUNK][:, :, first : first + P])
+            src = x_raw[b * P // CHUNK][:, :, first : first + P].rearrange("p t (c i) -> p c t i", i=4)
+            if X_ROUND[b] == "S":
+                made["x_bf", b] = scalar_tile([P, P, PACK], BF16)
+                nc.scalar.copy(made["x_bf", b][:].rearrange("p (c i) t -> p c t i", i=4), src)
+            elif X_ROUND[b] == "V":
+                made["x_bf", b] = vector_tile([P, P, PACK], BF16)
+                nc.vector.tensor_copy(made["x_bf", b][:].rearrange("p (c i) t -> p c t i", i=4), src)
+            else:
+                made["x_bf", b] = pool_tile([P, P, PACK], BF16)
+                nc.gpsimd.tensor_scalar(made["x_bf", b][:].rearrange("p (c i) t -> p c t i", i=4), src, 1.0, 0.0, ALU.mult, ALU.add)
 
         def x_quantise(b):
             made["x_codes", b] = vector_tile([P, P], U32)
@@ -189,9 +226,9 @@ def tile_attend_gpq_sqh_x_kernel(tc, xT, cb, norm, ts, y, wt, offs, out):
             )
 
         def scores(b):
-            made["s", b] = bank([P, N])
+            made["s", b] = bank([P, PACK, P])
             nc.tensor.matmul_mx(
-                made["s", b][:],
+                made["s", b][:].rearrange("r j m -> r (j m)"),
                 lhsT=made["x_codes", b][:].bitcast(E4M3),
                 lhsT_scale=made["x_scales", b][:],
                 rhs=k_codes[:].bitcast(E4M3),
@@ -203,14 +240,23 @@ def tile_attend_gpq_sqh_x_kernel(tc, xT, cb, norm, ts, y, wt, offs, out):
         def y_times_s(b):
             made["ys", b] = vector_tile([P, PACK, P], F32)
             nc.vector.tensor_tensor(
-                write_in_runs(made["ys", b]), read_in_runs(made["s", b][:]), read_in_runs(y_block(b)), ALU.mult
+                write_in_runs(made["ys", b][:]), write_in_runs(made["s", b][:]), read_in_runs(y_block(b)), ALU.mult
             )
 
         def y_times_wt(b):
-            made["yw", b] = vector_tile([P, PACK, P], F32)
-            nc.vector.tensor_scalar(
-                write_in_runs(made["yw", b]), read_in_runs(y_block(b)), neg_wt[:, b : b + 1], None, ALU.mult
-            )
+            if Y_WT[b] == "V":
+                made["yw", b] = vector_tile([P, PACK, P], F32)
+                nc.vector.tensor_scalar(
+                    write_in_runs(made["yw", b][:]), read_in_runs(y_block(b)), neg_wt[:, b : b + 1], None, ALU.mult
+                )
+            elif Y_WT[b] == "S":
+                made["yw", b] = scalar_tile([P, PACK, P], F32)
+                nc.scalar.activation(write_in_runs(made["yw", b][:]), read_in_runs(y_block(b)), ACT.Copy, scale=neg_wt[:, b : b + 1])
+            else:
+                made["yw", b] = pool_tile([P, PACK, P], F32)
+                nc.gpsimd.tensor_scalar(
+                    write_in_runs(made["yw", b][:]), read_in_runs(y_block(b)), neg_wt[:, b : b + 1], 0.0, ALU.mult, ALU.add
+                )
 
         def ys_turn(b):
             made["ys_turned", b] = turn(made["ys", b])
@@ -258,73 +304,67 @@ def tile_attend_gpq_sqh_x_kernel(tc, xT, cb, norm, ts, y, wt, offs, out):
             )
 
         def store(b):
-            result = scalar_tile([P, P, PACK], F32)
+            on_vector = STORE[b] == "V"
+            result = (vector_tile if on_vector else scalar_tile)([P, P, 2, 2], F32)
+            copy = nc.vector.tensor_copy if on_vector else nc.scalar.copy
             parts = 2 if b == BLOCKS - 1 else 1
             width = P // parts
             for part in range(parts):
                 piece = slice(part * width, (part + 1) * width)
-                nc.scalar.copy(result[:, piece, :], made["o", b][:].rearrange("r (t p) -> r p t", t=PACK)[:, piece, :])
+                copy(result[:, piece], made["o", b][:].rearrange("r (u p e) -> r p u e", u=2, e=2)[:, piece])
                 nc.sync.dma_start(
                     out[b * P : (b + 1) * P, piece.start * PACK : piece.stop * PACK],
-                    result[:, piece, :].rearrange("r p t -> r (p t)"),
-                )
-
-        warm_bf = keep.tile([P, N * PACK], BF16, name="warm_bf", align_bytes=64)
-        nc.vector.memset(warm_bf[:], 1.0)
-        warm_codes = keep.tile([P, N], U32, name="warm_codes", align_bytes=64)
-        warm_scales = keep.tile([P, N], U8, name="warm_scales", align_bytes=64)
-        nc.vector.quantize_mx(warm_codes[:].bitcast(E4M3), warm_scales[:], warm_bf[:])
-
-        def warm_up():
-            warm_bank = bank([P, N])
-            for step in range(WARM_PASSES):
-                nc.tensor.matmul_mx(
-                    warm_bank[:],
-                    lhsT=warm_codes[:, 0:P].bitcast(E4M3),
-                    lhsT_scale=warm_scales[:, 0:P],
-                    rhs=warm_codes[:].bitcast(E4M3),
-                    rhs_scale=warm_scales[:],
-                    start=True,
-                    stop=True,
+                    result[:, piece].rearrange("r p u e -> r (p u e)"),
                 )
 
         for t in range(PACK):
-            gather(t)
+            for half in range(2):
+                gather(t, half)
             if t == 1:
                 nc.vector.scalar_tensor_tensor(neg_ts_squared[:], abs_ts[:], -1.0, abs_ts[:], ALU.mult, ALU.mult)
-                interleave(nc.scalar.copy, k_bf[:, :, 0:2], k_f32[:, 0:2, :])
-            k_runs(t)
-            k_turn(t)
-            if t == LAST_PLANE - 1:
+                for half in range(2):
+                    k_round(nc.scalar.copy, 0, half)
+                k_turn(0)
                 warm_up()
-            if t < LAST_PLANE:
-                kt_round(t)
-        for cols in HALVES:
-            interleave(nc.vector.tensor_copy, k_bf[:, cols, 2:4], k_f32[:, 2:4, cols])
-        for cols in HALVES:
-            k_quantise(cols)
+        for b in range(2):
+            x_round(b)
+        for half in range(2):
+            k_round(nc.vector.tensor_copy, 1, half)
+        x_quantise(0)
+        for half in range(2):
+            k_quantise(half)
+        x_quantise(1)
 
         stages = {
-            "xr": (x_round, 0, ()),
-            "xq": (x_quantise, 0, ("xr",)),
-            "S": (scores, 0, ("xq",)),
-            "ys": (y_times_s, 0, ("S",)),
-            "yw": (y_times_wt, 0, ()),
-            "ty": (ys_turn, 0, ("ys",)),
-            "tw": (yw_turn, 0, ("yw",)),
-            "m": (margin, 0, ("ty",)),
-            "hr": (h_round, 0, ("m", "tw")),
-            "hq": (h_quantise, 0, ("hr",)),
-            "G": (gradient, 0, ("hq",)),
-            "st": (store, 0, ("G",)),
-            "kc": (kt_round, LAST_PLANE, ()),
-            "kq": (kt_quantise, 0, ("kc",)),
+            "xr": x_round, "xq": x_quantise, "S": scores, "ys": y_times_s, "yw": y_times_wt, "ty": ys_turn, "tw": yw_turn,
+            "m": margin, "hr": h_round, "hq": h_quantise, "G": gradient, "st": store,
         }
-        upcoming = {word: first for word, (stage, first, reads) in stages.items()}
-        left = [list(VECTOR_ORDER), list(SCALAR_ORDER), list(TENSOR_ORDER)]
-        while any(left):
-            for order in left:
-                while order and all(upcoming[read] > upcoming[order[0]] for read in stages[order[0]][2]):
-                    word = order.pop(0)
-                    stages[word][0](upcoming[word])
-                    upcoming[word] += 1
+        single = {("kc", 0): -3, ("kt", 1): -1, ("kc", 1): 0, ("kq", 0): 0, ("kq", 1): 2}
+        reads = {
+            "xr": (), "xq": ("xr",), "S": ("xq",), "ys": ("S",), "yw": (), "ty": ("ys",), "tw": ("yw",), "m": ("ty",),
+            "hr": ("m", "tw"), "hq": ("hr",), "G": ("hq",), "st": ("G",),
+            "kc": ("kt",), "kt": (), "kq": ("kc",),
+        }
+        stages["kc"], stages["kt"], stages["kq"] = kt_copy, k_turn, kt_quantise
+        engine = {"xq": "V", "ys": "V", "hr": "V", "hq": "V", "kq": "V", "m": "S", "kc": "S", "S": "P", "G": "P", "ty": "P", "tw": "P", "kt": "P"}
+        queues = {"V": [], "S": [], "P": [], "G": []}
+        for step in range(-6, 20):
+            for e, words in ORDER.items():
+                for word in words.split():
+                    if word == "k":
+                        queues[e].extend(item for item, at in single.items() if at == step and engine[item[0]] == e)
+                        continue
+                    b = step - STEP[word]
+                    if 0 <= b < BLOCKS and not (word in ("xr", "xq") and b < 2):
+                        if {"xr": X_ROUND, "yw": Y_WT, "st": STORE}.get(word, engine.get(word, "") * BLOCKS)[b] == e:
+                            queues[e].append((word, b))
+        done = {("xr", 0), ("xr", 1), ("xq", 0), ("xq", 1), ("kt", 0)}
+        while any(queues.values()):
+            for e in "VSPG":
+                order = queues[e]
+                while order and all((read, order[0][1]) in done for read in reads[order[0][0]]) and (
+                    order[0][0] != "G" or ("kq", 1) in done
+                ):
+                    word, b = order.pop(0)
+                    stages[word](b)
+                    done.add((word, b))

@@ -31,11 +31,12 @@ PSUM_BANKS = 8
 WARM_PASSES = 4
 BF16_ONES = 0x3F803F80
 
-STEP = {"ys":0,"S":-2,"xq":-3,"ty":1,"xr":-4,"m":2,"hr":3,"hq":4,"G":5,"st":6,"tw":1,"yw":0}
+STEP = {"ys":0,"S":-1,"xq":-2,"ty":0,"xr":-4,"m":1,"hr":3,"hq":4,"G":5,"st":5,"tw":1,"yw":0,"nw":-1}
+EARLY_YW = 0
 X_ROUND = "SSSSSSSS"
-Y_WT = "GGGGGGGG"
+Y_WT = "VVVGGGGG"
 STORE = "SSSSSSVS"
-ORDER = {"V":"ys hr yw xr hq xq k st","S":"m st yw xr k","P":"ty tw k G S","G":"yw xr"}
+ORDER = {"V":"ys hr yw xr k nw hq xq st","S":"m st yw xr k","P":"G S ty tw k","G":"yw xr"}
 
 
 def tile_attend_gpq_sqh_x_kernel(tc, xT, cb, norm, ts, y, wt, offs, out):
@@ -61,9 +62,9 @@ def tile_attend_gpq_sqh_x_kernel(tc, xT, cb, norm, ts, y, wt, offs, out):
             return banks.tile(shape, F32, name="bank")
 
         norm_cols = keep.tile([P, PACK], F32, name="norm_cols")
-        nc.sync.dma_start(norm_cols[:], norm[0:1, :].rearrange("o (p e) -> (o p) e", e=PACK))
+        nc.scalar.dma_start(norm_cols[:], norm[0:1, :].rearrange("o (p e) -> (o p) e", e=PACK))
         ts_cols = keep.tile([P, PACK], F32, name="ts_cols")
-        nc.sync.dma_start(ts_cols[:], ts[0:1, :].rearrange("o (p e) -> (o p) e", e=PACK))
+        nc.scalar.dma_start(ts_cols[:], ts[0:1, :].rearrange("o (p e) -> (o p) e", e=PACK))
 
         cb_planes = cb.rearrange("(p t) c -> t p c", t=PACK)
         books = [keep.tile([P, C], F32, name=f"book{t}") for t in range(PACK)]
@@ -152,8 +153,8 @@ def tile_attend_gpq_sqh_x_kernel(tc, xT, cb, norm, ts, y, wt, offs, out):
             )
         abs_ts = keep.tile([P, PACK], F32, name="abs_ts")
         nc.scalar.copy(abs_ts[:], turn(ts_runs)[:, :, 0])
-        neg_wt = keep.tile([P, BLOCKS], F32, name="neg_wt")
-        nc.scalar.activation(neg_wt[:], wt_bank[:, 0:BLOCKS], ACT.Copy, scale=-1.0)
+        wt_cols = keep.tile([P, BLOCKS], F32, name="wt_cols")
+        nc.scalar.copy(wt_cols[:], wt_bank[:, 0:BLOCKS])
         neg_ts_squared = keep.tile([P, PACK], F32, name="neg_ts_squared")
 
         k_f32 = keep.tile([P, PACK, N], F32, name="k_f32")
@@ -247,16 +248,20 @@ def tile_attend_gpq_sqh_x_kernel(tc, xT, cb, norm, ts, y, wt, offs, out):
             if Y_WT[b] == "V":
                 made["yw", b] = vector_tile([P, PACK, P], F32)
                 nc.vector.tensor_scalar(
-                    write_in_runs(made["yw", b][:]), read_in_runs(y_block(b)), neg_wt[:, b : b + 1], None, ALU.mult
+                    write_in_runs(made["yw", b][:]), read_in_runs(y_block(b)), wt_cols[:, b : b + 1], -1.0, ALU.mult, ALU.mult
                 )
             elif Y_WT[b] == "S":
                 made["yw", b] = scalar_tile([P, PACK, P], F32)
-                nc.scalar.activation(write_in_runs(made["yw", b][:]), read_in_runs(y_block(b)), ACT.Copy, scale=neg_wt[:, b : b + 1])
+                nc.scalar.activation(write_in_runs(made["yw", b][:]), read_in_runs(y_block(b)), ACT.Copy, scale=made["neg_wt", b][:])
             else:
                 made["yw", b] = pool_tile([P, PACK, P], F32)
                 nc.gpsimd.tensor_scalar(
-                    write_in_runs(made["yw", b][:]), read_in_runs(y_block(b)), neg_wt[:, b : b + 1], 0.0, ALU.mult, ALU.add
+                    write_in_runs(made["yw", b][:]), read_in_runs(y_block(b)), made["neg_wt", b][:], 0.0, ALU.mult, ALU.add
                 )
+
+        def negate_wt(b):
+            made["neg_wt", b] = vector_tile([P, 1], F32)
+            nc.vector.tensor_scalar(made["neg_wt", b][:], wt_cols[:, b : b + 1], -1.0, None, ALU.mult)
 
         def ys_turn(b):
             made["ys_turned", b] = turn(made["ys", b])
@@ -325,6 +330,7 @@ def tile_attend_gpq_sqh_x_kernel(tc, xT, cb, norm, ts, y, wt, offs, out):
                 for half in range(2):
                     k_round(nc.scalar.copy, 0, half)
                 k_turn(0)
+                kt_copy(0)
                 warm_up()
         for b in range(2):
             x_round(b)
@@ -334,19 +340,21 @@ def tile_attend_gpq_sqh_x_kernel(tc, xT, cb, norm, ts, y, wt, offs, out):
         for half in range(2):
             k_quantise(half)
         x_quantise(1)
+        for b in range(EARLY_YW):
+            y_times_wt(b)
 
         stages = {
             "xr": x_round, "xq": x_quantise, "S": scores, "ys": y_times_s, "yw": y_times_wt, "ty": ys_turn, "tw": yw_turn,
-            "m": margin, "hr": h_round, "hq": h_quantise, "G": gradient, "st": store,
+            "m": margin, "hr": h_round, "hq": h_quantise, "G": gradient, "st": store, "nw": negate_wt,
         }
-        single = {("kc", 0): -3, ("kt", 1): -1, ("kc", 1): 0, ("kq", 0): 0, ("kq", 1): 2}
+        single = {("kt", 1): -2, ("kc", 1): -1, ("kq", 0): -1, ("kq", 1): 1}
         reads = {
-            "xr": (), "xq": ("xr",), "S": ("xq",), "ys": ("S",), "yw": (), "ty": ("ys",), "tw": ("yw",), "m": ("ty",),
+            "xr": (), "xq": ("xr",), "S": ("xq",), "ys": ("S",), "yw": (), "nw": (), "ty": ("ys",), "tw": ("yw",), "m": ("ty",),
             "hr": ("m", "tw"), "hq": ("hr",), "G": ("hq",), "st": ("G",),
             "kc": ("kt",), "kt": (), "kq": ("kc",),
         }
         stages["kc"], stages["kt"], stages["kq"] = kt_copy, k_turn, kt_quantise
-        engine = {"xq": "V", "ys": "V", "hr": "V", "hq": "V", "kq": "V", "m": "S", "kc": "S", "S": "P", "G": "P", "ty": "P", "tw": "P", "kt": "P"}
+        engine = {"xq": "V", "ys": "V", "hr": "V", "hq": "V", "kq": "V", "nw": "V", "m": "S", "kc": "S", "S": "P", "G": "P", "ty": "P", "tw": "P", "kt": "P"}
         queues = {"V": [], "S": [], "P": [], "G": []}
         for step in range(-6, 20):
             for e, words in ORDER.items():
@@ -355,16 +363,18 @@ def tile_attend_gpq_sqh_x_kernel(tc, xT, cb, norm, ts, y, wt, offs, out):
                         queues[e].extend(item for item, at in single.items() if at == step and engine[item[0]] == e)
                         continue
                     b = step - STEP[word]
-                    if 0 <= b < BLOCKS and not (word in ("xr", "xq") and b < 2):
+                    if 0 <= b < BLOCKS and not (word in ("xr", "xq") and b < 2) and not (word == "yw" and b < EARLY_YW) and not (word == "nw" and Y_WT[b] != "G"):
                         if {"xr": X_ROUND, "yw": Y_WT, "st": STORE}.get(word, engine.get(word, "") * BLOCKS)[b] == e:
                             queues[e].append((word, b))
-        done = {("xr", 0), ("xr", 1), ("xq", 0), ("xq", 1), ("kt", 0)}
+        done = {("xr", 0), ("xr", 1), ("xq", 0), ("xq", 1), ("kt", 0), ("kc", 0)}
+        for b in range(EARLY_YW):
+            done.add(("yw", b))
         while any(queues.values()):
             for e in "VSPG":
                 order = queues[e]
                 while order and all((read, order[0][1]) in done for read in reads[order[0][0]]) and (
                     order[0][0] != "G" or ("kq", 1) in done
-                ):
+                ) and (e != "G" or ("nw", order[0][1]) in done):
                     word, b = order.pop(0)
                     stages[word](b)
                     done.add((word, b))

@@ -21,22 +21,22 @@ P = 128
 PACK = 4
 RUN = 8
 LIST = 16
+LINE = 4
 BLOCKS = R // P
 CHUNK = 2 * P
 HALF = N // 2
+MX_BLOCKS_IN_HALF = HALF // (PACK * RUN)
 VECTOR_RING = 32
 SCALAR_RING = 20
-POOL_RING = 8
 PSUM_BANKS = 8
 WARM_PASSES = 4
 BF16_ONES = 0x3F803F80
 
-STEP = {"ys":0,"S":-1,"xq":-2,"ty":0,"xr":-4,"m":1,"hr":3,"hq":4,"G":5,"st":5,"tw":1,"yw":0,"nw":-1}
-EARLY_YW = 0
-X_ROUND = "SSSSSSSS"
-Y_WT = "VVVGGGGG"
-STORE = "SSSSSSVS"
-ORDER = {"V":"ys hr yw xr k nw hq xq st","S":"m st yw xr k","P":"G S ty tw k","G":"yw xr"}
+LAG_X_ROUND, LAG_X_QUANTISE, LAG_SCORES = -4, -2, -1
+LAG_TURN_YW = LAG_MARGIN = 1
+LAG_H_ROUND, LAG_H_QUANTISE, LAG_GRADIENT = 3, 4, 5
+FIRST_ON_GPSIMD = LAG_H_ROUND
+RESULT_ON_VECTOR = BLOCKS - 2
 
 
 def tile_attend_gpq_sqh_x_kernel(tc, xT, cb, norm, ts, y, wt, offs, out):
@@ -45,7 +45,7 @@ def tile_attend_gpq_sqh_x_kernel(tc, xT, cb, norm, ts, y, wt, offs, out):
         keep = ctx.enter_context(tc.tile_pool(name="keep", bufs=1))
         by_vector = ctx.enter_context(tc.tile_pool(name="by_vector", bufs=VECTOR_RING))
         by_scalar = ctx.enter_context(tc.tile_pool(name="by_scalar", bufs=SCALAR_RING))
-        by_pool = ctx.enter_context(tc.tile_pool(name="by_pool", bufs=POOL_RING))
+        by_gpsimd = ctx.enter_context(tc.tile_pool(name="by_gpsimd", bufs=BLOCKS - FIRST_ON_GPSIMD))
         scales = ctx.enter_context(tc.tile_pool(name="scales", bufs=BLOCKS))
         banks = ctx.enter_context(tc.psum_pool(name="banks", bufs=PSUM_BANKS))
 
@@ -55,16 +55,16 @@ def tile_attend_gpq_sqh_x_kernel(tc, xT, cb, norm, ts, y, wt, offs, out):
         def scalar_tile(shape, dtype):
             return by_scalar.tile(shape, dtype, name="ring", align_bytes=64)
 
-        def pool_tile(shape, dtype):
-            return by_pool.tile(shape, dtype, name="ring", align_bytes=64)
+        def gpsimd_tile(shape, dtype):
+            return by_gpsimd.tile(shape, dtype, name="ring", align_bytes=64)
 
         def bank(shape):
             return banks.tile(shape, F32, name="bank")
 
         norm_cols = keep.tile([P, PACK], F32, name="norm_cols")
-        nc.scalar.dma_start(norm_cols[:], norm[0:1, :].rearrange("o (p e) -> (o p) e", e=PACK))
+        nc.sync.dma_start(norm_cols[:], norm[0:1, :].rearrange("o (p e) -> (o p) e", e=PACK))
         ts_cols = keep.tile([P, PACK], F32, name="ts_cols")
-        nc.scalar.dma_start(ts_cols[:], ts[0:1, :].rearrange("o (p e) -> (o p) e", e=PACK))
+        nc.sync.dma_start(ts_cols[:], ts[0:1, :].rearrange("o (p e) -> (o p) e", e=PACK))
 
         cb_planes = cb.rearrange("(p t) c -> t p c", t=PACK)
         books = [keep.tile([P, C], F32, name=f"book{t}") for t in range(PACK)]
@@ -78,24 +78,13 @@ def tile_attend_gpq_sqh_x_kernel(tc, xT, cb, norm, ts, y, wt, offs, out):
             nc.sync.dma_start(books[t][:], cb_planes[t])
 
         x_planes = xT.rearrange("(p t) r -> p t r", t=PACK)
-        x_raw, y_raw = {}, {}
-
-        def load_x(c):
-            x_raw[c] = keep.tile([P, PACK, CHUNK], F32, name=f"x{c}")
-            nc.sync.dma_start(x_raw[c][:], x_planes[:, :, c * CHUNK : (c + 1) * CHUNK])
-
-        def load_y(c):
-            y_raw[c] = keep.tile([P, CHUNK // P, N], F32, name=f"y{c}")
+        x_raw = [keep.tile([P, PACK, CHUNK], F32, name=f"x{c}") for c in range(R // CHUNK)]
+        y_raw = [keep.tile([P, CHUNK // P, N], F32, name=f"y{c}") for c in range(R // CHUNK)]
+        nc.sync.dma_start(x_raw[0][:], x_planes[:, :, 0:CHUNK])
+        for c in range(R // CHUNK):
+            if c + 1 < R // CHUNK:
+                nc.sync.dma_start(x_raw[c + 1][:], x_planes[:, :, (c + 1) * CHUNK : (c + 2) * CHUNK])
             nc.sync.dma_start(y_raw[c][:], y[c * CHUNK : (c + 1) * CHUNK, :].rearrange("(b p) n -> p b n", p=P))
-
-        load_x(0)
-        load_x(1)
-        load_y(0)
-        load_x(2)
-        load_y(1)
-        load_x(3)
-        load_y(2)
-        load_y(3)
 
         ident = keep.tile([P, P], F32, name="ident")
         make_identity(nc, ident[:])
@@ -130,7 +119,7 @@ def tile_attend_gpq_sqh_x_kernel(tc, xT, cb, norm, ts, y, wt, offs, out):
 
         def warm_up():
             warm_bank = bank([P, N])
-            for step in range(WARM_PASSES):
+            for repeat in range(WARM_PASSES):
                 nc.tensor.matmul_mx(
                     warm_bank[:],
                     lhsT=warm_codes[:, 0:P].bitcast(E4M3),
@@ -159,16 +148,16 @@ def tile_attend_gpq_sqh_x_kernel(tc, xT, cb, norm, ts, y, wt, offs, out):
 
         k_f32 = keep.tile([P, PACK, N], F32, name="k_f32")
         k_bf = keep.tile([P, N, PACK], BF16, name="k_bf", align_bytes=64)
+        k_codes = keep.tile([P, N], U32, name="k_codes", align_bytes=64)
         k_scales = keep.tile([P, N], U8, name="k_scales", align_bytes=64)
         kt_codes = keep.tile([P, D], U32, name="kt_codes", tag="norm_then_codes", align_bytes=64)
         kt_scales = keep.tile([P, D], U8, name="kt_scales", align_bytes=64)
-        k_codes = keep.tile([P, N], U32, name="k_codes", align_bytes=64)
         made = {}
 
-        def read_in_runs(by_column):
+        def by_runs(by_column):
             return by_column.rearrange("p (q j i) -> p j q i", j=PACK, i=RUN)
 
-        def write_in_runs(runs):
+        def in_runs(runs):
             return runs.rearrange("p j (q i) -> p j q i", i=RUN)
 
         def gather(t, half):
@@ -177,10 +166,12 @@ def tile_attend_gpq_sqh_x_kernel(tc, xT, cb, norm, ts, y, wt, offs, out):
             nc.vector.tensor_tensor(k_f32[:, t, cols], listed, signed_norm[:, cols], ALU.mult)
 
         def k_round(copy, u, half):
-            qs = slice(half * 8, (half + 1) * 8)
-            dst = k_bf[:].rearrange("p (j q i) t -> p q j t i", j=PACK, i=RUN)[:, qs, :, 2 * u : 2 * u + 2, :]
-            src = k_f32[:].rearrange("p t (q j i) -> p q j t i", j=PACK, i=RUN)[:, qs, :, 2 * u : 2 * u + 2, :]
-            copy(dst, src)
+            mx_blocks = slice(half * MX_BLOCKS_IN_HALF, (half + 1) * MX_BLOCKS_IN_HALF)
+            planes = slice(2 * u, 2 * u + 2)
+            copy(
+                k_bf[:].rearrange("p (j q i) t -> p q j t i", j=PACK, i=RUN)[:, mx_blocks, :, planes, :],
+                k_f32[:].rearrange("p t (q j i) -> p q j t i", j=PACK, i=RUN)[:, mx_blocks, :, planes, :],
+            )
 
         def k_quantise(half):
             cols = slice(half * HALF, (half + 1) * HALF)
@@ -200,7 +191,7 @@ def tile_attend_gpq_sqh_x_kernel(tc, xT, cb, norm, ts, y, wt, offs, out):
         def kt_quantise(u):
             cols = slice(u * 2 * P, (u + 1) * 2 * P)
             nc.vector.quantize_mx(
-                kt_codes[:, cols].bitcast(E4M3), kt_scales[:, cols], made["kt_bf", u][:].rearrange("p c j -> p (c j)")
+                kt_codes[:, cols].bitcast(E4M3), kt_scales[:, cols], made["kt_bf", u][:].rearrange("m c j -> m (c j)")
             )
 
         def y_block(b):
@@ -208,16 +199,11 @@ def tile_attend_gpq_sqh_x_kernel(tc, xT, cb, norm, ts, y, wt, offs, out):
 
         def x_round(b):
             first = b * P % CHUNK
-            src = x_raw[b * P // CHUNK][:, :, first : first + P].rearrange("p t (c i) -> p c t i", i=4)
-            if X_ROUND[b] == "S":
-                made["x_bf", b] = scalar_tile([P, P, PACK], BF16)
-                nc.scalar.copy(made["x_bf", b][:].rearrange("p (c i) t -> p c t i", i=4), src)
-            elif X_ROUND[b] == "V":
-                made["x_bf", b] = vector_tile([P, P, PACK], BF16)
-                nc.vector.tensor_copy(made["x_bf", b][:].rearrange("p (c i) t -> p c t i", i=4), src)
-            else:
-                made["x_bf", b] = pool_tile([P, P, PACK], BF16)
-                nc.gpsimd.tensor_scalar(made["x_bf", b][:].rearrange("p (c i) t -> p c t i", i=4), src, 1.0, 0.0, ALU.mult, ALU.add)
+            made["x_bf", b] = scalar_tile([P, P, PACK], BF16)
+            nc.scalar.copy(
+                made["x_bf", b][:].rearrange("p (c i) t -> p c t i", i=LINE),
+                x_raw[b * P // CHUNK][:, :, first : first + P].rearrange("p t (c i) -> p c t i", i=LINE),
+            )
 
         def x_quantise(b):
             made["x_codes", b] = vector_tile([P, P], U32)
@@ -240,28 +226,23 @@ def tile_attend_gpq_sqh_x_kernel(tc, xT, cb, norm, ts, y, wt, offs, out):
 
         def y_times_s(b):
             made["ys", b] = vector_tile([P, PACK, P], F32)
-            nc.vector.tensor_tensor(
-                write_in_runs(made["ys", b][:]), write_in_runs(made["s", b][:]), read_in_runs(y_block(b)), ALU.mult
-            )
-
-        def y_times_wt(b):
-            if Y_WT[b] == "V":
-                made["yw", b] = vector_tile([P, PACK, P], F32)
-                nc.vector.tensor_scalar(
-                    write_in_runs(made["yw", b][:]), read_in_runs(y_block(b)), wt_cols[:, b : b + 1], -1.0, ALU.mult, ALU.mult
-                )
-            elif Y_WT[b] == "S":
-                made["yw", b] = scalar_tile([P, PACK, P], F32)
-                nc.scalar.activation(write_in_runs(made["yw", b][:]), read_in_runs(y_block(b)), ACT.Copy, scale=made["neg_wt", b][:])
-            else:
-                made["yw", b] = pool_tile([P, PACK, P], F32)
-                nc.gpsimd.tensor_scalar(
-                    write_in_runs(made["yw", b][:]), read_in_runs(y_block(b)), made["neg_wt", b][:], 0.0, ALU.mult, ALU.add
-                )
+            nc.vector.tensor_tensor(in_runs(made["ys", b][:]), in_runs(made["s", b][:]), by_runs(y_block(b)), ALU.mult)
 
         def negate_wt(b):
             made["neg_wt", b] = vector_tile([P, 1], F32)
             nc.vector.tensor_scalar(made["neg_wt", b][:], wt_cols[:, b : b + 1], -1.0, None, ALU.mult)
+
+        def y_times_wt(b):
+            if b < FIRST_ON_GPSIMD:
+                made["yw", b] = vector_tile([P, PACK, P], F32)
+                nc.vector.tensor_scalar(
+                    in_runs(made["yw", b][:]), by_runs(y_block(b)), wt_cols[:, b : b + 1], -1.0, ALU.mult, ALU.mult
+                )
+            else:
+                made["yw", b] = gpsimd_tile([P, PACK, P], F32)
+                nc.gpsimd.tensor_scalar(
+                    in_runs(made["yw", b][:]), by_runs(y_block(b)), made["neg_wt", b][:], 0.0, ALU.mult, ALU.add
+                )
 
         def ys_turn(b):
             made["ys_turned", b] = turn(made["ys", b])
@@ -283,9 +264,9 @@ def tile_attend_gpq_sqh_x_kernel(tc, xT, cb, norm, ts, y, wt, offs, out):
         def h_round(b):
             made["h_bf", b] = vector_tile([P, P, PACK], BF16)
             nc.vector.tensor_tensor(
-                made["h_bf", b][:].rearrange("p (c i) j -> p c j i", i=4),
-                made["yw_turned", b][:].rearrange("p j (c i) -> p c j i", i=4),
-                made["margin", b][:].rearrange("p j (c i) -> p c j i", i=4),
+                made["h_bf", b][:].rearrange("p (c i) j -> p c j i", i=LINE),
+                made["yw_turned", b][:].rearrange("p j (c i) -> p c j i", i=LINE),
+                made["margin", b][:].rearrange("p j (c i) -> p c j i", i=LINE),
                 ALU.mult,
             )
 
@@ -309,9 +290,8 @@ def tile_attend_gpq_sqh_x_kernel(tc, xT, cb, norm, ts, y, wt, offs, out):
             )
 
         def store(b):
-            on_vector = STORE[b] == "V"
-            result = (vector_tile if on_vector else scalar_tile)([P, P, 2, 2], F32)
-            copy = nc.vector.tensor_copy if on_vector else nc.scalar.copy
+            new_tile, copy = (vector_tile, nc.vector.tensor_copy) if b == RESULT_ON_VECTOR else (scalar_tile, nc.scalar.copy)
+            result = new_tile([P, P, 2, 2], F32)
             parts = 2 if b == BLOCKS - 1 else 1
             width = P // parts
             for part in range(parts):
@@ -332,49 +312,40 @@ def tile_attend_gpq_sqh_x_kernel(tc, xT, cb, norm, ts, y, wt, offs, out):
                 k_turn(0)
                 kt_copy(0)
                 warm_up()
-        for b in range(2):
-            x_round(b)
+
+        x_round(0)
+        x_round(1)
         for half in range(2):
             k_round(nc.vector.tensor_copy, 1, half)
         x_quantise(0)
         for half in range(2):
             k_quantise(half)
         x_quantise(1)
-        for b in range(EARLY_YW):
-            y_times_wt(b)
+        kt_quantise(0)
+        x_round(2)
+        x_round(3)
+        k_turn(1)
+        kt_copy(1)
+        scores(0)
 
-        stages = {
-            "xr": x_round, "xq": x_quantise, "S": scores, "ys": y_times_s, "yw": y_times_wt, "ty": ys_turn, "tw": yw_turn,
-            "m": margin, "hr": h_round, "hq": h_quantise, "G": gradient, "st": store, "nw": negate_wt,
-        }
-        single = {("kt", 1): -2, ("kc", 1): -1, ("kq", 0): -1, ("kq", 1): 1}
-        reads = {
-            "xr": (), "xq": ("xr",), "S": ("xq",), "ys": ("S",), "yw": (), "nw": (), "ty": ("ys",), "tw": ("yw",), "m": ("ty",),
-            "hr": ("m", "tw"), "hq": ("hr",), "G": ("hq",), "st": ("G",),
-            "kc": ("kt",), "kt": (), "kq": ("kc",),
-        }
-        stages["kc"], stages["kt"], stages["kq"] = kt_copy, k_turn, kt_quantise
-        engine = {"xq": "V", "ys": "V", "hr": "V", "hq": "V", "kq": "V", "nw": "V", "m": "S", "kc": "S", "S": "P", "G": "P", "ty": "P", "tw": "P", "kt": "P"}
-        queues = {"V": [], "S": [], "P": [], "G": []}
-        for step in range(-6, 20):
-            for e, words in ORDER.items():
-                for word in words.split():
-                    if word == "k":
-                        queues[e].extend(item for item, at in single.items() if at == step and engine[item[0]] == e)
-                        continue
-                    b = step - STEP[word]
-                    if 0 <= b < BLOCKS and not (word in ("xr", "xq") and b < 2) and not (word == "yw" and b < EARLY_YW) and not (word == "nw" and Y_WT[b] != "G"):
-                        if {"xr": X_ROUND, "yw": Y_WT, "st": STORE}.get(word, engine.get(word, "") * BLOCKS)[b] == e:
-                            queues[e].append((word, b))
-        done = {("xr", 0), ("xr", 1), ("xq", 0), ("xq", 1), ("kt", 0), ("kc", 0)}
-        for b in range(EARLY_YW):
-            done.add(("yw", b))
-        while any(queues.values()):
-            for e in "VSPG":
-                order = queues[e]
-                while order and all((read, order[0][1]) in done for read in reads[order[0][0]]) and (
-                    order[0][0] != "G" or ("kq", 1) in done
-                ) and (e != "G" or ("nw", order[0][1]) in done):
-                    word, b = order.pop(0)
-                    stages[word](b)
-                    done.add((word, b))
+        def at(step, stage, lag):
+            if 0 <= step - lag < BLOCKS:
+                stage(step - lag)
+
+        for step in range(BLOCKS + LAG_GRADIENT):
+            at(step, gradient, LAG_GRADIENT)
+            at(step, scores, LAG_SCORES)
+            at(step, y_times_s, 0)
+            at(step, h_round, LAG_H_ROUND)
+            at(step, y_times_wt, 0)
+            if step == 1:
+                kt_quantise(1)
+            if FIRST_ON_GPSIMD <= step + 1 < BLOCKS:
+                negate_wt(step + 1)
+            at(step, h_quantise, LAG_H_QUANTISE)
+            at(step, x_quantise, LAG_X_QUANTISE)
+            at(step, margin, LAG_MARGIN)
+            at(step, store, LAG_GRADIENT)
+            at(step, x_round, LAG_X_ROUND)
+            at(step, ys_turn, 0)
+            at(step, yw_turn, LAG_TURN_YW)

@@ -25,18 +25,18 @@ LINE = 4
 BLOCKS = R // P
 CHUNK = 2 * P
 HALF = N // 2
-MX_BLOCKS_IN_HALF = HALF // (PACK * RUN)
+LAST_PLANE = PACK - 1
 VECTOR_RING = 32
 SCALAR_RING = 20
 PSUM_BANKS = 8
 WARM_PASSES = 4
 BF16_ONES = 0x3F803F80
 
-LAG_X_ROUND, LAG_X_QUANTISE, LAG_SCORES = -4, -2, -1
-LAG_TURN_YW = LAG_MARGIN = 1
+LAG_X_ROUND, LAG_X_QUANTISE, LAG_SCORES, LAG_Y_TIMES_WT = -4, -3, -2, -1
+LAG_MARGIN = 1
 LAG_H_ROUND, LAG_H_QUANTISE, LAG_GRADIENT = 3, 4, 5
-FIRST_ON_GPSIMD = LAG_H_ROUND
-RESULT_ON_VECTOR = BLOCKS - 2
+FIRST_ON_GPSIMD = LAG_H_ROUND - LAG_Y_TIMES_WT
+RESULT_ON_VECTOR = BLOCKS - 1
 
 
 def tile_attend_gpq_sqh_x_kernel(tc, xT, cb, norm, ts, y, wt, offs, out):
@@ -62,9 +62,9 @@ def tile_attend_gpq_sqh_x_kernel(tc, xT, cb, norm, ts, y, wt, offs, out):
             return banks.tile(shape, F32, name="bank")
 
         norm_cols = keep.tile([P, PACK], F32, name="norm_cols")
-        nc.sync.dma_start(norm_cols[:], norm[0:1, :].rearrange("o (p e) -> (o p) e", e=PACK))
+        nc.scalar.dma_start(norm_cols[:], norm[0:1, :].rearrange("o (p e) -> (o p) e", e=PACK))
         ts_cols = keep.tile([P, PACK], F32, name="ts_cols")
-        nc.sync.dma_start(ts_cols[:], ts[0:1, :].rearrange("o (p e) -> (o p) e", e=PACK))
+        nc.scalar.dma_start(ts_cols[:], ts[0:1, :].rearrange("o (p e) -> (o p) e", e=PACK))
 
         cb_planes = cb.rearrange("(p t) c -> t p c", t=PACK)
         books = [keep.tile([P, C], F32, name=f"book{t}") for t in range(PACK)]
@@ -166,11 +166,11 @@ def tile_attend_gpq_sqh_x_kernel(tc, xT, cb, norm, ts, y, wt, offs, out):
             nc.vector.tensor_tensor(k_f32[:, t, cols], listed, signed_norm[:, cols], ALU.mult)
 
         def k_round(copy, u, half):
-            mx_blocks = slice(half * MX_BLOCKS_IN_HALF, (half + 1) * MX_BLOCKS_IN_HALF)
+            cols = slice(half * HALF, (half + 1) * HALF)
             planes = slice(2 * u, 2 * u + 2)
             copy(
-                k_bf[:].rearrange("p (j q i) t -> p q j t i", j=PACK, i=RUN)[:, mx_blocks, :, planes, :],
-                k_f32[:].rearrange("p t (q j i) -> p q j t i", j=PACK, i=RUN)[:, mx_blocks, :, planes, :],
+                k_bf[:, cols, planes].rearrange("p (c i) t -> p c t i", i=LINE),
+                k_f32[:, planes, cols].rearrange("p t (c i) -> p c t i", i=LINE),
             )
 
         def k_quantise(half):
@@ -179,19 +179,29 @@ def tile_attend_gpq_sqh_x_kernel(tc, xT, cb, norm, ts, y, wt, offs, out):
                 k_codes[:, cols].bitcast(E4M3), k_scales[:, cols], k_bf[:, cols, :].rearrange("p n t -> p (n t)")
             )
 
-        def k_turn(u):
-            words = k_bf[:].rearrange("p n t -> p (n t)").bitcast(F32).rearrange("p (j m u) -> p j m u", j=PACK, u=2)
-            made["k_turned", u] = turn(words[:, :, :, u])
+        def k_pairs(t):
+            made["k_pairs", t] = scalar_tile([P, 2, P, 2], BF16)
+            nc.scalar.copy(
+                made["k_pairs", t][:].rearrange("p v (q i) e -> p v q i e", i=RUN),
+                k_f32[:, t, :].rearrange("p (q v e i) -> p v q i e", v=2, e=2, i=RUN),
+            )
 
-        def kt_copy(u):
-            made["kt_bf", u] = scalar_tile([P, 2 * P, PACK], BF16)
-            turned = made["k_turned", u][:].rearrange("m j p -> m (j p)").bitcast(BF16)
-            nc.scalar.copy(made["kt_bf", u][:], turned.rearrange("m (j c) -> m c j", j=PACK))
+        def k_turn(t):
+            words = made["k_pairs", t][:].rearrange("p v m e -> p (v m e)").bitcast(F32)
+            made["k_turned", t] = bank([P, 2, P])
+            for v in range(2):
+                nc.tensor.transpose(made["k_turned", t][:, v, :], words[:, v * P : (v + 1) * P], ident[:])
 
-        def kt_quantise(u):
-            cols = slice(u * 2 * P, (u + 1) * 2 * P)
+        def kt_copy(t):
+            made["kt_words", t] = scalar_tile([P, P, 2], F32)
+            nc.scalar.copy(made["kt_words", t][:], made["k_turned", t][:].rearrange("m v p -> m p v"))
+
+        def kt_quantise(t):
+            cols = slice(t * P, (t + 1) * P)
             nc.vector.quantize_mx(
-                kt_codes[:, cols].bitcast(E4M3), kt_scales[:, cols], made["kt_bf", u][:].rearrange("m c j -> m (c j)")
+                kt_codes[:, cols].bitcast(E4M3),
+                kt_scales[:, cols],
+                made["kt_words", t][:].rearrange("m p v -> m (p v)").bitcast(BF16),
             )
 
         def y_block(b):
@@ -213,9 +223,9 @@ def tile_attend_gpq_sqh_x_kernel(tc, xT, cb, norm, ts, y, wt, offs, out):
             )
 
         def scores(b):
-            made["s", b] = bank([P, PACK, P])
+            made["s", b] = bank([P, N])
             nc.tensor.matmul_mx(
-                made["s", b][:].rearrange("r j m -> r (j m)"),
+                made["s", b][:],
                 lhsT=made["x_codes", b][:].bitcast(E4M3),
                 lhsT_scale=made["x_scales", b][:],
                 rhs=k_codes[:].bitcast(E4M3),
@@ -226,7 +236,7 @@ def tile_attend_gpq_sqh_x_kernel(tc, xT, cb, norm, ts, y, wt, offs, out):
 
         def y_times_s(b):
             made["ys", b] = vector_tile([P, PACK, P], F32)
-            nc.vector.tensor_tensor(in_runs(made["ys", b][:]), in_runs(made["s", b][:]), by_runs(y_block(b)), ALU.mult)
+            nc.vector.tensor_tensor(in_runs(made["ys", b][:]), by_runs(made["s", b][:]), by_runs(y_block(b)), ALU.mult)
 
         def negate_wt(b):
             made["neg_wt", b] = vector_tile([P, 1], F32)
@@ -291,61 +301,60 @@ def tile_attend_gpq_sqh_x_kernel(tc, xT, cb, norm, ts, y, wt, offs, out):
 
         def store(b):
             new_tile, copy = (vector_tile, nc.vector.tensor_copy) if b == RESULT_ON_VECTOR else (scalar_tile, nc.scalar.copy)
-            result = new_tile([P, P, 2, 2], F32)
+            result = new_tile([P, P, PACK], F32)
             parts = 2 if b == BLOCKS - 1 else 1
             width = P // parts
             for part in range(parts):
                 piece = slice(part * width, (part + 1) * width)
-                copy(result[:, piece], made["o", b][:].rearrange("r (u p e) -> r p u e", u=2, e=2)[:, piece])
+                copy(result[:, piece], made["o", b][:].rearrange("r (t p) -> r p t", t=PACK)[:, piece])
                 nc.sync.dma_start(
                     out[b * P : (b + 1) * P, piece.start * PACK : piece.stop * PACK],
-                    result[:, piece].rearrange("r p u e -> r (p u e)"),
+                    result[:, piece].rearrange("r p t -> r (p t)"),
                 )
 
         for t in range(PACK):
             for half in range(2):
                 gather(t, half)
+            if t < LAST_PLANE:
+                k_pairs(t)
             if t == 1:
                 nc.vector.scalar_tensor_tensor(neg_ts_squared[:], abs_ts[:], -1.0, abs_ts[:], ALU.mult, ALU.mult)
                 for half in range(2):
                     k_round(nc.scalar.copy, 0, half)
-                k_turn(0)
-                kt_copy(0)
+            if t < LAST_PLANE:
+                k_turn(t)
+            if t < 2:
+                kt_copy(t)
+            if t == 1:
                 warm_up()
 
         x_round(0)
         x_round(1)
         for half in range(2):
             k_round(nc.vector.tensor_copy, 1, half)
+        k_quantise(0)
         x_quantise(0)
-        for half in range(2):
-            k_quantise(half)
-        x_quantise(1)
-        kt_quantise(0)
-        x_round(2)
-        x_round(3)
-        k_turn(1)
-        kt_copy(1)
-        scores(0)
+        k_quantise(1)
 
-        def at(step, stage, lag):
-            if 0 <= step - lag < BLOCKS:
+        def at(step, stage, lag, first=0, end=BLOCKS):
+            if first <= step - lag < end:
                 stage(step - lag)
 
-        for step in range(BLOCKS + LAG_GRADIENT):
+        for step in range(LAG_SCORES, BLOCKS + LAG_GRADIENT):
             at(step, gradient, LAG_GRADIENT)
             at(step, scores, LAG_SCORES)
             at(step, y_times_s, 0)
             at(step, h_round, LAG_H_ROUND)
-            at(step, y_times_wt, 0)
-            if step == 1:
-                kt_quantise(1)
-            if FIRST_ON_GPSIMD <= step + 1 < BLOCKS:
-                negate_wt(step + 1)
+            at(step, y_times_wt, LAG_Y_TIMES_WT)
+            at(step, kt_quantise, -1, end=PACK)
+            at(step, negate_wt, LAG_Y_TIMES_WT - 1, first=FIRST_ON_GPSIMD)
             at(step, h_quantise, LAG_H_QUANTISE)
             at(step, x_quantise, LAG_X_QUANTISE)
             at(step, margin, LAG_MARGIN)
             at(step, store, LAG_GRADIENT)
             at(step, x_round, LAG_X_ROUND)
+            at(step, k_pairs, LAG_SCORES - LAST_PLANE, first=LAST_PLANE, end=PACK)
+            at(step, kt_copy, -LAST_PLANE, first=2, end=PACK)
             at(step, ys_turn, 0)
-            at(step, yw_turn, LAG_TURN_YW)
+            at(step, yw_turn, 0)
+            at(step, k_turn, -1 - LAST_PLANE, first=LAST_PLANE, end=PACK)

@@ -29,14 +29,12 @@ LAST_PLANE = PACK - 1
 VECTOR_RING = 32
 SCALAR_RING = 20
 PSUM_BANKS = 8
+PAIRS = PACK // 2
 WARM_PASSES = 4
 BF16_ONES = 0x3F803F80
 
-LAG_X_ROUND, LAG_X_QUANTISE, LAG_SCORES, LAG_Y_TIMES_WT = -4, -3, -2, -1
-LAG_MARGIN = 1
-LAG_H_ROUND, LAG_H_QUANTISE, LAG_GRADIENT = 3, 4, 5
-FIRST_ON_GPSIMD = LAG_H_ROUND - LAG_Y_TIMES_WT
-RESULT_ON_VECTOR = BLOCKS - 1
+LAG_X_ROUND, LAG_X_QUANTISE, LAG_SCORES = -4, -3, -2
+LAG_MARGIN, LAG_H_ROUND, LAG_H_QUANTISE, LAG_STORE = 1, 2, 3, 4
 
 
 def tile_attend_gpq_sqh_x_kernel(tc, xT, cb, norm, ts, y, wt, offs, out):
@@ -45,7 +43,6 @@ def tile_attend_gpq_sqh_x_kernel(tc, xT, cb, norm, ts, y, wt, offs, out):
         keep = ctx.enter_context(tc.tile_pool(name="keep", bufs=1))
         by_vector = ctx.enter_context(tc.tile_pool(name="by_vector", bufs=VECTOR_RING))
         by_scalar = ctx.enter_context(tc.tile_pool(name="by_scalar", bufs=SCALAR_RING))
-        by_gpsimd = ctx.enter_context(tc.tile_pool(name="by_gpsimd", bufs=BLOCKS - FIRST_ON_GPSIMD))
         scales = ctx.enter_context(tc.tile_pool(name="scales", bufs=BLOCKS))
         banks = ctx.enter_context(tc.psum_pool(name="banks", bufs=PSUM_BANKS))
 
@@ -55,25 +52,23 @@ def tile_attend_gpq_sqh_x_kernel(tc, xT, cb, norm, ts, y, wt, offs, out):
         def scalar_tile(shape, dtype):
             return by_scalar.tile(shape, dtype, name="ring", align_bytes=64)
 
-        def gpsimd_tile(shape, dtype):
-            return by_gpsimd.tile(shape, dtype, name="ring", align_bytes=64)
-
         def bank(shape):
             return banks.tile(shape, F32, name="bank")
 
         norm_cols = keep.tile([P, PACK], F32, name="norm_cols")
-        nc.scalar.dma_start(norm_cols[:], norm[0:1, :].rearrange("o (p e) -> (o p) e", e=PACK))
+        nc.sync.dma_start(norm_cols[:], norm[0:1, :].rearrange("o (p e) -> (o p) e", e=PACK))
         ts_cols = keep.tile([P, PACK], F32, name="ts_cols")
-        nc.scalar.dma_start(ts_cols[:], ts[0:1, :].rearrange("o (p e) -> (o p) e", e=PACK))
+        nc.sync.dma_start(ts_cols[:], ts[0:1, :].rearrange("o (p e) -> (o p) e", e=PACK))
+
+        wt_rows = keep.tile([P, P], F32, name="wt_rows")
+        nc.vector.memset(wt_rows[:], 0.0)
+        nc.scalar.dma_start(wt_rows[0:BLOCKS, :], wt.rearrange("(b q) o -> b (q o)", q=P))
 
         cb_planes = cb.rearrange("(p t) c -> t p c", t=PACK)
-        books = [keep.tile([P, C], F32, name=f"book{t}") for t in range(PACK)]
+        books = [keep.tile([P, C], F32, name=f"book{t}", align_bytes=64) for t in range(PACK)]
         nc.sync.dma_start(books[0][:], cb_planes[0])
         offsets = keep.tile([P, N // LIST], U16, name="offsets")
         nc.sync.dma_start(offsets[:], offs)
-        wt_rows = keep.tile([P, P], F32, name="wt_rows")
-        nc.vector.memset(wt_rows[:], 0.0)
-        nc.sync.dma_start(wt_rows[0:BLOCKS, :], wt.rearrange("(b q) o -> b (q o)", q=P))
         for t in range(1, PACK):
             nc.sync.dma_start(books[t][:], cb_planes[t])
 
@@ -101,56 +96,42 @@ def tile_attend_gpq_sqh_x_kernel(tc, xT, cb, norm, ts, y, wt, offs, out):
                 nc.tensor.transpose(turned[:, j, :], runs[:, j, :], ident[:])
             return turned
 
+        warm_bf = keep.tile([P, N * PACK], BF16, name="warm_bf", align_bytes=64)
+        nc.vector.memset(warm_bf[:].bitcast(I32), BF16_ONES)
+        warm_codes = vector_tile([P, N], U32)
+        warm_scales = keep.tile([P, N], U8, name="warm_scales", align_bytes=64)
+        nc.vector.quantize_mx(warm_codes[:].bitcast(E4M3), warm_scales[:], warm_bf[:])
+
         twice_step = vector_tile([P, PACK], F32)
         nc.vector.tensor_scalar(twice_step[:], ts_cols[:], 0.0, 2.0, ALU.is_ge, ALU.mult)
         signed_cols = vector_tile([P, PACK], F32)
         nc.vector.scalar_tensor_tensor(signed_cols[:], twice_step[:], -1.0, norm_cols[:], ALU.add, ALU.mult)
-        signed_norm = keep.tile([P, N], F32, name="signed_norm", tag="norm_then_codes", align_bytes=64)
+        signed_norm = keep.tile([P, N], F32, name="signed_norm")
         nc.scalar.copy(
             signed_norm[:].rearrange("m (p e) -> m p e", e=PACK),
             spread(signed_cols)[:].rearrange("m e p -> m p e"),
         )
 
-        warm_bf = keep.tile([P, N * PACK], BF16, name="warm_bf", align_bytes=64)
-        nc.gpsimd.memset(warm_bf[:].bitcast(I32), BF16_ONES)
-        warm_codes = vector_tile([P, N], U32)
-        warm_scales = keep.tile([P, N], U8, name="warm_scales", align_bytes=64)
-        nc.vector.quantize_mx(warm_codes[:].bitcast(E4M3), warm_scales[:], warm_bf[:])
-
-        def warm_up():
-            warm_bank = bank([P, N])
-            for repeat in range(WARM_PASSES):
-                nc.tensor.matmul_mx(
-                    warm_bank[:],
-                    lhsT=warm_codes[:, 0:P].bitcast(E4M3),
-                    lhsT_scale=warm_scales[:, 0:P],
-                    rhs=warm_codes[:].bitcast(E4M3),
-                    rhs_scale=warm_scales[:],
-                    start=True,
-                    stop=True,
-                )
-
+        abs_cols = vector_tile([P, PACK], F32)
+        nc.vector.scalar_tensor_tensor(abs_cols[:], twice_step[:], -1.0, ts_cols[:], ALU.add, ALU.mult)
+        ts_runs = vector_tile([P, PACK, P], F32)
+        nc.vector.tensor_copy(
+            ts_runs[:].rearrange("m j (q g e) -> m j q g e", g=2, e=PACK),
+            spread(abs_cols)[:].rearrange("m e (q j g) -> m j q g e", j=PACK, g=2),
+        )
         wt_bank = bank([P, P])
         nc.tensor.transpose(wt_bank[:], wt_rows[:], ident[:])
-        ts_spread = spread(ts_cols)
-        ts_runs = keep.tile([P, PACK, P], F32, name="ts_runs")
-        for j in range(PACK):
-            nc.scalar.activation(
-                ts_runs[:, j, :].rearrange("m (q g e) -> m q g e", g=2, e=PACK),
-                ts_spread[:].rearrange("m e (q j g) -> m j q g e", j=PACK, g=2)[:, j],
-                ACT.Abs,
-            )
         abs_ts = keep.tile([P, PACK], F32, name="abs_ts")
         nc.scalar.copy(abs_ts[:], turn(ts_runs)[:, :, 0])
-        wt_cols = keep.tile([P, BLOCKS], F32, name="wt_cols")
-        nc.scalar.copy(wt_cols[:], wt_bank[:, 0:BLOCKS])
+        neg_wt = keep.tile([P, BLOCKS], F32, name="neg_wt")
+        nc.scalar.activation(neg_wt[:], wt_bank[:, 0:BLOCKS], ACT.Copy, scale=-1.0)
         neg_ts_squared = keep.tile([P, PACK], F32, name="neg_ts_squared")
 
         k_f32 = keep.tile([P, PACK, N], F32, name="k_f32")
         k_bf = keep.tile([P, N, PACK], BF16, name="k_bf", align_bytes=64)
         k_codes = keep.tile([P, N], U32, name="k_codes", align_bytes=64)
         k_scales = keep.tile([P, N], U8, name="k_scales", align_bytes=64)
-        kt_codes = keep.tile([P, D], U32, name="kt_codes", tag="norm_then_codes", align_bytes=64)
+        kt_codes = keep.tile([P, D], U32, name="kt_codes", tag=f"book{LAST_PLANE - 1}", align_bytes=64)
         kt_scales = keep.tile([P, D], U8, name="kt_scales", align_bytes=64)
         made = {}
 
@@ -188,39 +169,55 @@ def tile_attend_gpq_sqh_x_kernel(tc, xT, cb, norm, ts, y, wt, offs, out):
 
         def k_turn(t):
             words = made["k_pairs", t][:].rearrange("p v m e -> p (v m e)").bitcast(F32)
-            made["k_turned", t] = bank([P, 2, P])
+            if t % 2 == 0:
+                made["k_turned", t // 2] = bank([P, 2, 2, P])
             for v in range(2):
-                nc.tensor.transpose(made["k_turned", t][:, v, :], words[:, v * P : (v + 1) * P], ident[:])
+                nc.tensor.transpose(made["k_turned", t // 2][:, t % 2, v, :], words[:, v * P : (v + 1) * P], ident[:])
 
-        def kt_copy(t):
-            made["kt_words", t] = scalar_tile([P, P, 2], F32)
-            nc.scalar.copy(made["kt_words", t][:], made["k_turned", t][:].rearrange("m v p -> m p v"))
+        def kt_copy(u):
+            made["kt_words", u] = scalar_tile([P, 2, P, 2], F32)
+            nc.scalar.copy(made["kt_words", u][:], made["k_turned", u][:].rearrange("m t v p -> m t p v"))
 
-        def kt_quantise(t):
-            cols = slice(t * P, (t + 1) * P)
+        def kt_quantise(u):
+            cols = slice(u * 2 * P, (u + 1) * 2 * P)
             nc.vector.quantize_mx(
                 kt_codes[:, cols].bitcast(E4M3),
                 kt_scales[:, cols],
-                made["kt_words", t][:].rearrange("m p v -> m (p v)").bitcast(BF16),
+                made["kt_words", u][:].rearrange("m t p v -> m (t p v)").bitcast(BF16),
             )
+
+        def warm_up():
+            warm_bank = bank([P, N])
+            for repeat in range(WARM_PASSES):
+                nc.tensor.matmul_mx(
+                    warm_bank[:],
+                    lhsT=warm_codes[:, 0:P].bitcast(E4M3),
+                    lhsT_scale=warm_scales[:, 0:P],
+                    rhs=warm_codes[:].bitcast(E4M3),
+                    rhs_scale=warm_scales[:],
+                    start=True,
+                    stop=True,
+                )
 
         def y_block(b):
             return y_raw[b * P // CHUNK][:, b % (CHUNK // P), :]
 
+        def as_bf16(buffer):
+            return buffer[:, 0 : N // 2].bitcast(BF16)
+
         def x_round(b):
             first = b * P % CHUNK
-            made["x_bf", b] = scalar_tile([P, P, PACK], BF16)
+            made["x_bf", b] = scalar_tile([P, N], F32)
             nc.scalar.copy(
-                made["x_bf", b][:].rearrange("p (c i) t -> p c t i", i=LINE),
+                as_bf16(made["x_bf", b]).rearrange("p (c i t) -> p c t i", i=LINE, t=PACK),
                 x_raw[b * P // CHUNK][:, :, first : first + P].rearrange("p t (c i) -> p c t i", i=LINE),
             )
 
         def x_quantise(b):
             made["x_codes", b] = vector_tile([P, P], U32)
             made["x_scales", b] = scales.tile([P, P], U8, name="x_scales", align_bytes=64)
-            nc.vector.quantize_mx(
-                made["x_codes", b][:].bitcast(E4M3), made["x_scales", b][:], made["x_bf", b][:].rearrange("p r t -> p (r t)")
-            )
+            nc.vector.quantize_mx(made["x_codes", b][:].bitcast(E4M3), made["x_scales", b][:], as_bf16(made["x_bf", b]))
+            made["last quantised"] = made["x_bf", b]
 
         def scores(b):
             made["s", b] = bank([P, N])
@@ -238,27 +235,27 @@ def tile_attend_gpq_sqh_x_kernel(tc, xT, cb, norm, ts, y, wt, offs, out):
             made["ys", b] = vector_tile([P, PACK, P], F32)
             nc.vector.tensor_tensor(in_runs(made["ys", b][:]), by_runs(made["s", b][:]), by_runs(y_block(b)), ALU.mult)
 
-        def negate_wt(b):
-            made["neg_wt", b] = vector_tile([P, 1], F32)
-            nc.vector.tensor_scalar(made["neg_wt", b][:], wt_cols[:, b : b + 1], -1.0, None, ALU.mult)
-
         def y_times_wt(b):
-            if b < FIRST_ON_GPSIMD:
-                made["yw", b] = vector_tile([P, PACK, P], F32)
-                nc.vector.tensor_scalar(
-                    in_runs(made["yw", b][:]), by_runs(y_block(b)), wt_cols[:, b : b + 1], -1.0, ALU.mult, ALU.mult
-                )
+            if b == 0:
+                made["yw", b] = vector_tile([P, N], F32)
+                engine = nc.vector
             else:
-                made["yw", b] = gpsimd_tile([P, PACK, P], F32)
-                nc.gpsimd.tensor_scalar(
-                    in_runs(made["yw", b][:]), by_runs(y_block(b)), made["neg_wt", b][:], 0.0, ALU.mult, ALU.add
-                )
+                made["yw", b] = made["last quantised"]
+                engine = nc.gpsimd
+            engine.tensor_scalar(
+                in_runs(made["yw", b][:].rearrange("p (j m) -> p j m", j=PACK)),
+                by_runs(y_block(b)),
+                neg_wt[:, b : b + 1],
+                0.0,
+                ALU.mult,
+                ALU.add,
+            )
 
         def ys_turn(b):
             made["ys_turned", b] = turn(made["ys", b])
 
         def yw_turn(b):
-            made["yw_turned", b] = turn(made["yw", b])
+            made["yw_turned", b] = turn(made["yw", b][:].rearrange("p (j m) -> p j m", j=PACK))
 
         def margin(b):
             made["margin", b] = scalar_tile([P, PACK, P], F32)
@@ -272,9 +269,9 @@ def tile_attend_gpq_sqh_x_kernel(tc, xT, cb, norm, ts, y, wt, offs, out):
                 )
 
         def h_round(b):
-            made["h_bf", b] = vector_tile([P, P, PACK], BF16)
+            made["h_bf", b] = vector_tile([P, N], F32)
             nc.vector.tensor_tensor(
-                made["h_bf", b][:].rearrange("p (c i) j -> p c j i", i=LINE),
+                as_bf16(made["h_bf", b]).rearrange("p (c i j) -> p c j i", i=LINE, j=PACK),
                 made["yw_turned", b][:].rearrange("p j (c i) -> p c j i", i=LINE),
                 made["margin", b][:].rearrange("p j (c i) -> p c j i", i=LINE),
                 ALU.mult,
@@ -283,9 +280,8 @@ def tile_attend_gpq_sqh_x_kernel(tc, xT, cb, norm, ts, y, wt, offs, out):
         def h_quantise(b):
             made["h_codes", b] = vector_tile([P, P], U32)
             made["h_scales", b] = scales.tile([P, P], U8, name="h_scales", align_bytes=64)
-            nc.vector.quantize_mx(
-                made["h_codes", b][:].bitcast(E5M2), made["h_scales", b][:], made["h_bf", b][:].rearrange("p r j -> p (r j)")
-            )
+            nc.vector.quantize_mx(made["h_codes", b][:].bitcast(E5M2), made["h_scales", b][:], as_bf16(made["h_bf", b]))
+            made["last quantised"] = made["h_bf", b]
 
         def gradient(b):
             made["o", b] = bank([P, D])
@@ -300,7 +296,7 @@ def tile_attend_gpq_sqh_x_kernel(tc, xT, cb, norm, ts, y, wt, offs, out):
             )
 
         def store(b):
-            new_tile, copy = (vector_tile, nc.vector.tensor_copy) if b == RESULT_ON_VECTOR else (scalar_tile, nc.scalar.copy)
+            new_tile, copy = (vector_tile, nc.vector.tensor_copy) if b == BLOCKS - 1 else (scalar_tile, nc.scalar.copy)
             result = new_tile([P, P, PACK], F32)
             parts = 2 if b == BLOCKS - 1 else 1
             width = P // parts
@@ -317,44 +313,50 @@ def tile_attend_gpq_sqh_x_kernel(tc, xT, cb, norm, ts, y, wt, offs, out):
                 gather(t, half)
             if t < LAST_PLANE:
                 k_pairs(t)
+                k_turn(t)
             if t == 1:
                 nc.vector.scalar_tensor_tensor(neg_ts_squared[:], abs_ts[:], -1.0, abs_ts[:], ALU.mult, ALU.mult)
-                for half in range(2):
-                    k_round(nc.scalar.copy, 0, half)
-            if t < LAST_PLANE:
-                k_turn(t)
-            if t < 2:
-                kt_copy(t)
-            if t == 1:
+                k_round(nc.scalar.copy, 0, 0)
+                kt_copy(0)
+            if t == 2:
                 warm_up()
+                k_round(nc.scalar.copy, 0, 1)
 
         x_round(0)
-        x_round(1)
         for half in range(2):
             k_round(nc.vector.tensor_copy, 1, half)
         k_quantise(0)
         x_quantise(0)
         k_quantise(1)
+        x_round(1)
+        k_pairs(LAST_PLANE)
+        x_round(2)
+        x_round(3)
+        scores(0)
+        x_quantise(1)
+        kt_quantise(0)
+        y_times_wt(0)
+        scores(1)
+        k_turn(LAST_PLANE)
+        x_quantise(2)
 
         def at(step, stage, lag, first=0, end=BLOCKS):
             if first <= step - lag < end:
                 stage(step - lag)
 
-        for step in range(LAG_SCORES, BLOCKS + LAG_GRADIENT):
-            at(step, gradient, LAG_GRADIENT)
-            at(step, scores, LAG_SCORES)
+        for step in range(BLOCKS + LAG_STORE):
+            at(step, y_times_wt, 0, first=1)
             at(step, y_times_s, 0)
             at(step, h_round, LAG_H_ROUND)
-            at(step, y_times_wt, LAG_Y_TIMES_WT)
-            at(step, kt_quantise, -1, end=PACK)
-            at(step, negate_wt, LAG_Y_TIMES_WT - 1, first=FIRST_ON_GPSIMD)
-            at(step, h_quantise, LAG_H_QUANTISE)
+            at(step, h_quantise, LAG_H_QUANTISE, end=BLOCKS - 2)
+            at(step, h_quantise, LAG_H_ROUND, first=BLOCKS - 2)
+            at(step, kt_quantise, 0, first=1, end=PAIRS)
             at(step, x_quantise, LAG_X_QUANTISE)
             at(step, margin, LAG_MARGIN)
-            at(step, store, LAG_GRADIENT)
+            at(step, kt_copy, -1, first=1, end=PAIRS)
             at(step, x_round, LAG_X_ROUND)
-            at(step, k_pairs, LAG_SCORES - LAST_PLANE, first=LAST_PLANE, end=PACK)
-            at(step, kt_copy, -LAST_PLANE, first=2, end=PACK)
+            at(step, store, LAG_STORE)
             at(step, ys_turn, 0)
             at(step, yw_turn, 0)
-            at(step, k_turn, -1 - LAST_PLANE, first=LAST_PLANE, end=PACK)
+            at(step, gradient, LAG_H_QUANTISE)
+            at(step, scores, LAG_SCORES)

@@ -34,6 +34,7 @@ WARM_PASSES = 4
 BF16_ONES = 0x3F803F80
 
 LAG_X_ROUND, LAG_X_QUANTISE, LAG_SCORES = -4, -3, -2
+FIRST_ON_GPSIMD = 2
 LAG_MARGIN, LAG_H_ROUND, LAG_H_QUANTISE, LAG_STORE = 1, 2, 3, 4
 
 
@@ -135,6 +136,8 @@ def tile_attend_gpq_sqh_x_kernel(tc, xT, cb, norm, ts, y, wt, offs, out):
         kt_scales = keep.tile([P, D], U8, name="kt_scales", align_bytes=64)
         made = {}
 
+        read_out = []
+
         def by_runs(by_column):
             return by_column.rearrange("p (q j i) -> p j q i", j=PACK, i=RUN)
 
@@ -175,16 +178,20 @@ def tile_attend_gpq_sqh_x_kernel(tc, xT, cb, norm, ts, y, wt, offs, out):
                 nc.tensor.transpose(made["k_turned", t // 2][:, t % 2, v, :], words[:, v * P : (v + 1) * P], ident[:])
 
         def kt_copy(u):
-            made["kt_words", u] = scalar_tile([P, 2, P, 2], F32)
-            nc.scalar.copy(made["kt_words", u][:], made["k_turned", u][:].rearrange("m t v p -> m t p v"))
+            made["kt_words", u] = scalar_tile([P, N], F32)
+            nc.scalar.copy(
+                made["kt_words", u][:].rearrange("m (t p v) -> m t p v", t=2, v=2),
+                made["k_turned", u][:].rearrange("m t v p -> m t p v"),
+            )
 
         def kt_quantise(u):
             cols = slice(u * 2 * P, (u + 1) * 2 * P)
             nc.vector.quantize_mx(
                 kt_codes[:, cols].bitcast(E4M3),
                 kt_scales[:, cols],
-                made["kt_words", u][:].rearrange("m t p v -> m (t p v)").bitcast(BF16),
+                made["kt_words", u][:].bitcast(BF16),
             )
+            read_out.append(made["kt_words", u])
 
         def warm_up():
             warm_bank = bank([P, N])
@@ -217,7 +224,7 @@ def tile_attend_gpq_sqh_x_kernel(tc, xT, cb, norm, ts, y, wt, offs, out):
             made["x_codes", b] = vector_tile([P, P], U32)
             made["x_scales", b] = scales.tile([P, P], U8, name="x_scales", align_bytes=64)
             nc.vector.quantize_mx(made["x_codes", b][:].bitcast(E4M3), made["x_scales", b][:], as_bf16(made["x_bf", b]))
-            made["last quantised"] = made["x_bf", b]
+            read_out.append(made["x_bf", b])
 
         def scores(b):
             made["s", b] = bank([P, N])
@@ -236,11 +243,11 @@ def tile_attend_gpq_sqh_x_kernel(tc, xT, cb, norm, ts, y, wt, offs, out):
             nc.vector.tensor_tensor(in_runs(made["ys", b][:]), by_runs(made["s", b][:]), by_runs(y_block(b)), ALU.mult)
 
         def y_times_wt(b):
-            if b == 0:
+            if b < FIRST_ON_GPSIMD:
                 made["yw", b] = vector_tile([P, N], F32)
                 engine = nc.vector
             else:
-                made["yw", b] = made["last quantised"]
+                made["yw", b] = read_out[-2]
                 engine = nc.gpsimd
             engine.tensor_scalar(
                 in_runs(made["yw", b][:].rearrange("p (j m) -> p j m", j=PACK)),
@@ -258,10 +265,10 @@ def tile_attend_gpq_sqh_x_kernel(tc, xT, cb, norm, ts, y, wt, offs, out):
             made["yw_turned", b] = turn(made["yw", b][:].rearrange("p (j m) -> p j m", j=PACK))
 
         def margin(b):
-            made["margin", b] = scalar_tile([P, PACK, P], F32)
+            made["margin", b] = scalar_tile([P, N], F32)
             for j in range(PACK):
                 nc.scalar.activation(
-                    made["margin", b][:, j, :],
+                    made["margin", b][:, j * P : (j + 1) * P],
                     made["ys_turned", b][:, j, :],
                     ACT.Relu,
                     bias=abs_ts[:, j : j + 1],
@@ -273,15 +280,16 @@ def tile_attend_gpq_sqh_x_kernel(tc, xT, cb, norm, ts, y, wt, offs, out):
             nc.vector.tensor_tensor(
                 as_bf16(made["h_bf", b]).rearrange("p (c i j) -> p c j i", i=LINE, j=PACK),
                 made["yw_turned", b][:].rearrange("p j (c i) -> p c j i", i=LINE),
-                made["margin", b][:].rearrange("p j (c i) -> p c j i", i=LINE),
+                made["margin", b][:].rearrange("p (j c i) -> p c j i", j=PACK, i=LINE),
                 ALU.mult,
             )
+            read_out.append(made["margin", b])
 
         def h_quantise(b):
             made["h_codes", b] = vector_tile([P, P], U32)
             made["h_scales", b] = scales.tile([P, P], U8, name="h_scales", align_bytes=64)
             nc.vector.quantize_mx(made["h_codes", b][:].bitcast(E5M2), made["h_scales", b][:], as_bf16(made["h_bf", b]))
-            made["last quantised"] = made["h_bf", b]
+            read_out.append(made["h_bf", b])
 
         def gradient(b):
             made["o", b] = bank([P, D])
@@ -345,18 +353,19 @@ def tile_attend_gpq_sqh_x_kernel(tc, xT, cb, norm, ts, y, wt, offs, out):
                 stage(step - lag)
 
         for step in range(BLOCKS + LAG_STORE):
-            at(step, y_times_wt, 0, first=1)
+            at(step, y_times_wt, 0, first=FIRST_ON_GPSIMD)
             at(step, y_times_s, 0)
             at(step, h_round, LAG_H_ROUND)
             at(step, h_quantise, LAG_H_QUANTISE, end=BLOCKS - 2)
             at(step, h_quantise, LAG_H_ROUND, first=BLOCKS - 2)
             at(step, kt_quantise, 0, first=1, end=PAIRS)
             at(step, x_quantise, LAG_X_QUANTISE)
+            at(step, y_times_wt, -1, end=FIRST_ON_GPSIMD)
             at(step, margin, LAG_MARGIN)
             at(step, kt_copy, -1, first=1, end=PAIRS)
             at(step, x_round, LAG_X_ROUND)
             at(step, store, LAG_STORE)
             at(step, ys_turn, 0)
             at(step, yw_turn, 0)
-            at(step, gradient, LAG_H_QUANTISE)
             at(step, scores, LAG_SCORES)
+            at(step, gradient, LAG_H_QUANTISE)

@@ -8,7 +8,6 @@ FLOPS = 2 * 2 * R * N * D
 
 F32 = mybir.dt.float32
 BF16 = mybir.dt.bfloat16
-I32 = mybir.dt.int32
 U32 = mybir.dt.uint32
 U16 = mybir.dt.uint16
 U8 = mybir.dt.uint8
@@ -30,8 +29,6 @@ VECTOR_RING = 32
 SCALAR_RING = 20
 PSUM_BANKS = 8
 PAIRS = PACK // 2
-WARM_PASSES = 4
-BF16_ONES = 0x3F803F80
 
 LAG_X_ROUND, LAG_X_QUANTISE, LAG_SCORES = -4, -3, -2
 FIRST_ON_GPSIMD = 2
@@ -96,12 +93,6 @@ def tile_attend_gpq_sqh_x_kernel(tc, xT, cb, norm, ts, y, wt, offs, out):
             for j in range(PACK):
                 nc.tensor.transpose(turned[:, j, :], runs[:, j, :], ident[:])
             return turned
-
-        warm_bf = keep.tile([P, N * PACK], BF16, name="warm_bf", align_bytes=64)
-        nc.vector.memset(warm_bf[:].bitcast(I32), BF16_ONES)
-        warm_codes = vector_tile([P, N], U32)
-        warm_scales = keep.tile([P, N], U8, name="warm_scales", align_bytes=64)
-        nc.vector.quantize_mx(warm_codes[:].bitcast(E4M3), warm_scales[:], warm_bf[:])
 
         twice_step = vector_tile([P, PACK], F32)
         nc.vector.tensor_scalar(twice_step[:], ts_cols[:], 0.0, 2.0, ALU.is_ge, ALU.mult)
@@ -192,19 +183,6 @@ def tile_attend_gpq_sqh_x_kernel(tc, xT, cb, norm, ts, y, wt, offs, out):
                 made["kt_words", u][:].bitcast(BF16),
             )
             read_out.append(made["kt_words", u])
-
-        def warm_up():
-            warm_bank = bank([P, N])
-            for repeat in range(WARM_PASSES):
-                nc.tensor.matmul_mx(
-                    warm_bank[:],
-                    lhsT=warm_codes[:, 0:P].bitcast(E4M3),
-                    lhsT_scale=warm_scales[:, 0:P],
-                    rhs=warm_codes[:].bitcast(E4M3),
-                    rhs_scale=warm_scales[:],
-                    start=True,
-                    stop=True,
-                )
 
         def y_block(b):
             return y_raw[b * P // CHUNK][:, b % (CHUNK // P), :]
@@ -327,7 +305,6 @@ def tile_attend_gpq_sqh_x_kernel(tc, xT, cb, norm, ts, y, wt, offs, out):
                 k_round(nc.scalar.copy, 0, 0)
                 kt_copy(0)
             if t == 2:
-                warm_up()
                 k_round(nc.scalar.copy, 0, 1)
 
         x_round(0)

@@ -54,9 +54,9 @@ def tile_attend_gpq_sqh_x_kernel(tc, xT, cb, norm, ts, y, wt, offs, out):
             return banks.tile(shape, F32, name="bank")
 
         norm_cols = keep.tile([P, PACK], F32, name="norm_cols")
-        nc.sync.dma_start(norm_cols[:], norm[0:1, :].rearrange("o (p e) -> (o p) e", e=PACK))
+        nc.scalar.dma_start(norm_cols[:], norm[0:1, :].rearrange("o (p e) -> (o p) e", e=PACK))
         ts_cols = keep.tile([P, PACK], F32, name="ts_cols")
-        nc.sync.dma_start(ts_cols[:], ts[0:1, :].rearrange("o (p e) -> (o p) e", e=PACK))
+        nc.scalar.dma_start(ts_cols[:], ts[0:1, :].rearrange("o (p e) -> (o p) e", e=PACK))
 
         wt_rows = keep.tile([P, P], F32, name="wt_rows")
         nc.vector.memset(wt_rows[:], 0.0)
@@ -72,12 +72,27 @@ def tile_attend_gpq_sqh_x_kernel(tc, xT, cb, norm, ts, y, wt, offs, out):
 
         x_planes = xT.rearrange("(p t) r -> p t r", t=PACK)
         x_raw = [keep.tile([P, PACK, CHUNK], F32, name=f"x{c}") for c in range(R // CHUNK)]
-        y_raw = [keep.tile([P, CHUNK // P, N], F32, name=f"y{c}") for c in range(R // CHUNK)]
-        nc.sync.dma_start(x_raw[0][:], x_planes[:, :, 0:CHUNK])
-        for c in range(R // CHUNK):
-            if c + 1 < R // CHUNK:
-                nc.sync.dma_start(x_raw[c + 1][:], x_planes[:, :, (c + 1) * CHUNK : (c + 2) * CHUNK])
-            nc.sync.dma_start(y_raw[c][:], y[c * CHUNK : (c + 1) * CHUNK, :].rearrange("(b p) n -> p b n", p=P))
+        y_tiles = {}
+
+        def load_x(c):
+            nc.sync.dma_start(x_raw[c][:], x_planes[:, :, c * CHUNK : (c + 1) * CHUNK])
+
+        def load_y(first, count):
+            y_raw = keep.tile([P, count, N], F32, name=f"y{first}")
+            nc.sync.dma_start(y_raw[:], y[first * P : (first + count) * P, :].rearrange("(b p) n -> p b n", p=P))
+            for b in range(count):
+                y_tiles[first + b] = y_raw[:, b, :]
+
+        load_x(0)
+        load_x(1)
+        load_y(0, 1)
+        load_x(2)
+        load_y(1, 1)
+        load_y(2, 1)
+        load_x(3)
+        load_y(3, 1)
+        load_y(4, 2)
+        load_y(6, 2)
 
         ident = keep.tile([P, P], F32, name="ident")
         make_identity(nc, ident[:])
@@ -185,7 +200,7 @@ def tile_attend_gpq_sqh_x_kernel(tc, xT, cb, norm, ts, y, wt, offs, out):
             read_out.append(made["kt_words", u])
 
         def y_block(b):
-            return y_raw[b * P // CHUNK][:, b % (CHUNK // P), :]
+            return y_tiles[b]
 
         def as_bf16(buffer):
             return buffer[:, 0 : N // 2].bitcast(BF16)
@@ -332,15 +347,15 @@ def tile_attend_gpq_sqh_x_kernel(tc, xT, cb, norm, ts, y, wt, offs, out):
         for step in range(BLOCKS + LAG_STORE):
             at(step, y_times_wt, 0, first=FIRST_ON_GPSIMD)
             at(step, y_times_s, 0)
+            at(step, y_times_wt, 0, first=1, end=FIRST_ON_GPSIMD)
             at(step, h_round, LAG_H_ROUND)
             at(step, h_quantise, LAG_H_QUANTISE, end=BLOCKS - 2)
             at(step, h_quantise, LAG_H_ROUND, first=BLOCKS - 2)
             at(step, kt_quantise, 0, first=1, end=PAIRS)
             at(step, x_quantise, LAG_X_QUANTISE)
-            at(step, y_times_wt, -1, end=FIRST_ON_GPSIMD)
             at(step, margin, LAG_MARGIN)
-            at(step, kt_copy, -1, first=1, end=PAIRS)
             at(step, x_round, LAG_X_ROUND)
+            at(step, kt_copy, -1, first=1, end=PAIRS)
             at(step, store, LAG_STORE)
             at(step, ys_turn, 0)
             at(step, yw_turn, 0)

@@ -23,6 +23,8 @@ LIST = 16
 LINE = 4
 BLOCKS = R // P
 CHUNK = 2 * P
+CHUNKS = R // CHUNK
+X_AHEAD = 2
 HALF = N // 2
 LAST_PLANE = PACK - 1
 VECTOR_RING = 32
@@ -31,8 +33,9 @@ PSUM_BANKS = 8
 PAIRS = PACK // 2
 
 LAG_X_ROUND, LAG_X_QUANTISE, LAG_SCORES = -4, -3, -2
-FIRST_ON_GPSIMD = 2
 LAG_MARGIN, LAG_H_ROUND, LAG_H_QUANTISE, LAG_STORE = 1, 2, 3, 4
+FIRST_ON_GPSIMD = LAG_H_ROUND
+FIRST_DRAINED = BLOCKS - LAG_H_ROUND
 
 
 def tile_attend_gpq_sqh_x_kernel(tc, xT, cb, norm, ts, y, wt, offs, out):
@@ -71,8 +74,8 @@ def tile_attend_gpq_sqh_x_kernel(tc, xT, cb, norm, ts, y, wt, offs, out):
             nc.sync.dma_start(books[t][:], cb_planes[t])
 
         x_planes = xT.rearrange("(p t) r -> p t r", t=PACK)
-        x_raw = [keep.tile([P, PACK, CHUNK], F32, name=f"x{c}") for c in range(R // CHUNK)]
-        y_tiles = {}
+        x_raw = [keep.tile([P, PACK, CHUNK], F32, name=f"x{c}") for c in range(CHUNKS)]
+        y_rows = {}
 
         def load_x(c):
             nc.sync.dma_start(x_raw[c][:], x_planes[:, :, c * CHUNK : (c + 1) * CHUNK])
@@ -81,18 +84,17 @@ def tile_attend_gpq_sqh_x_kernel(tc, xT, cb, norm, ts, y, wt, offs, out):
             y_raw = keep.tile([P, count, N], F32, name=f"y{first}")
             nc.sync.dma_start(y_raw[:], y[first * P : (first + count) * P, :].rearrange("(b p) n -> p b n", p=P))
             for b in range(count):
-                y_tiles[first + b] = y_raw[:, b, :]
+                y_rows[first + b] = y_raw[:, b, :]
 
-        load_x(0)
-        load_x(1)
-        load_y(0, 1)
-        load_x(2)
-        load_y(1, 1)
-        load_y(2, 1)
-        load_x(3)
-        load_y(3, 1)
-        load_y(4, 2)
-        load_y(6, 2)
+        for c in range(X_AHEAD):
+            load_x(c)
+        for c in range(CHUNKS):
+            if c + X_AHEAD < CHUNKS:
+                load_y(2 * c, 1)
+                load_x(c + X_AHEAD)
+                load_y(2 * c + 1, 1)
+            else:
+                load_y(2 * c, 2)
 
         ident = keep.tile([P, P], F32, name="ident")
         make_identity(nc, ident[:])
@@ -121,8 +123,8 @@ def tile_attend_gpq_sqh_x_kernel(tc, xT, cb, norm, ts, y, wt, offs, out):
 
         abs_cols = vector_tile([P, PACK], F32)
         nc.vector.scalar_tensor_tensor(abs_cols[:], twice_step[:], -1.0, ts_cols[:], ALU.add, ALU.mult)
-        ts_runs = vector_tile([P, PACK, P], F32)
-        nc.vector.tensor_copy(
+        ts_runs = scalar_tile([P, PACK, P], F32)
+        nc.scalar.copy(
             ts_runs[:].rearrange("m j (q g e) -> m j q g e", g=2, e=PACK),
             spread(abs_cols)[:].rearrange("m e (q j g) -> m j q g e", j=PACK, g=2),
         )
@@ -141,7 +143,6 @@ def tile_attend_gpq_sqh_x_kernel(tc, xT, cb, norm, ts, y, wt, offs, out):
         kt_codes = keep.tile([P, D], U32, name="kt_codes", tag=f"book{LAST_PLANE - 1}", align_bytes=64)
         kt_scales = keep.tile([P, D], U8, name="kt_scales", align_bytes=64)
         made = {}
-
         read_out = []
 
         def by_runs(by_column):
@@ -199,9 +200,6 @@ def tile_attend_gpq_sqh_x_kernel(tc, xT, cb, norm, ts, y, wt, offs, out):
             )
             read_out.append(made["kt_words", u])
 
-        def y_block(b):
-            return y_tiles[b]
-
         def as_bf16(buffer):
             return buffer[:, 0 : N // 2].bitcast(BF16)
 
@@ -233,7 +231,7 @@ def tile_attend_gpq_sqh_x_kernel(tc, xT, cb, norm, ts, y, wt, offs, out):
 
         def y_times_s(b):
             made["ys", b] = vector_tile([P, PACK, P], F32)
-            nc.vector.tensor_tensor(in_runs(made["ys", b][:]), by_runs(made["s", b][:]), by_runs(y_block(b)), ALU.mult)
+            nc.vector.tensor_tensor(in_runs(made["ys", b][:]), by_runs(made["s", b][:]), by_runs(y_rows[b]), ALU.mult)
 
         def y_times_wt(b):
             if b < FIRST_ON_GPSIMD:
@@ -244,7 +242,7 @@ def tile_attend_gpq_sqh_x_kernel(tc, xT, cb, norm, ts, y, wt, offs, out):
                 engine = nc.gpsimd
             engine.tensor_scalar(
                 in_runs(made["yw", b][:].rearrange("p (j m) -> p j m", j=PACK)),
-                by_runs(y_block(b)),
+                by_runs(y_rows[b]),
                 neg_wt[:, b : b + 1],
                 0.0,
                 ALU.mult,
@@ -318,9 +316,8 @@ def tile_attend_gpq_sqh_x_kernel(tc, xT, cb, norm, ts, y, wt, offs, out):
             if t == 1:
                 nc.vector.scalar_tensor_tensor(neg_ts_squared[:], abs_ts[:], -1.0, abs_ts[:], ALU.mult, ALU.mult)
                 k_round(nc.scalar.copy, 0, 0)
+                k_round(nc.vector.tensor_copy, 0, 1)
                 kt_copy(0)
-            if t == 2:
-                k_round(nc.scalar.copy, 0, 1)
 
         x_round(0)
         for half in range(2):
@@ -349,8 +346,8 @@ def tile_attend_gpq_sqh_x_kernel(tc, xT, cb, norm, ts, y, wt, offs, out):
             at(step, y_times_s, 0)
             at(step, y_times_wt, 0, first=1, end=FIRST_ON_GPSIMD)
             at(step, h_round, LAG_H_ROUND)
-            at(step, h_quantise, LAG_H_QUANTISE, end=BLOCKS - 2)
-            at(step, h_quantise, LAG_H_ROUND, first=BLOCKS - 2)
+            at(step, h_quantise, LAG_H_QUANTISE, end=FIRST_DRAINED)
+            at(step, h_quantise, LAG_H_ROUND, first=FIRST_DRAINED)
             at(step, kt_quantise, 0, first=1, end=PAIRS)
             at(step, x_quantise, LAG_X_QUANTISE)
             at(step, margin, LAG_MARGIN)

from contextlib import ExitStack

import concourse.mybir as mybir
from concourse.masks import make_identity

N, C, D, R = 512, 2048, 512, 1024
FLOPS = 2 * 2 * R * N * D

F32 = mybir.dt.float32
BF16 = mybir.dt.bfloat16
U32 = mybir.dt.uint32
U16 = mybir.dt.uint16
U8 = mybir.dt.uint8
E4M3 = mybir.dt.float8_e4m3fn_x4
E5M2 = mybir.dt.float8_e5m2_x4
ALU = mybir.AluOpType
ACT = mybir.ActivationFunctionType

P = 128
PACK = 4
RUN = 8
LIST = 16
LINE = 4
BLOCKS = R // P
CHUNK = 2 * P
CHUNKS = R // CHUNK
X_AHEAD = 2
HALF = N // 2
LAST_PLANE = PACK - 1
VECTOR_RING = 32
SCALAR_RING = 20
PSUM_BANKS = 8
PAIRS = PACK // 2

LAG_X_ROUND, LAG_X_QUANTISE, LAG_SCORES = -4, -3, -2
LAG_MARGIN, LAG_H_ROUND, LAG_H_QUANTISE, LAG_STORE = 1, 2, 3, 4
FIRST_ON_GPSIMD = LAG_H_ROUND
FIRST_DRAINED = BLOCKS - LAG_H_ROUND


def tile_attend_gpq_sqh_x_kernel(tc, xT, cb, norm, ts, y, wt, offs, out):
    nc = tc.nc
    with ExitStack() as ctx:
        keep = ctx.enter_context(tc.tile_pool(name="keep", bufs=1))
        by_vector = ctx.enter_context(tc.tile_pool(name="by_vector", bufs=VECTOR_RING))
        by_scalar = ctx.enter_context(tc.tile_pool(name="by_scalar", bufs=SCALAR_RING))
        scales = ctx.enter_context(tc.tile_pool(name="scales", bufs=BLOCKS))
        banks = ctx.enter_context(tc.psum_pool(name="banks", bufs=PSUM_BANKS))

        def vector_tile(shape, dtype):
            return by_vector.tile(shape, dtype, name="ring", align_bytes=64)

        def scalar_tile(shape, dtype):
            return by_scalar.tile(shape, dtype, name="ring", align_bytes=64)

        def bank(shape):
            return banks.tile(shape, F32, name="bank")

        norm_cols = keep.tile([P, PACK], F32, name="norm_cols")
        nc.scalar.dma_start(norm_cols[:], norm[0:1, :].rearrange("o (p e) -> (o p) e", e=PACK))
        ts_cols = keep.tile([P, PACK], F32, name="ts_cols")
        nc.scalar.dma_start(ts_cols[:], ts[0:1, :].rearrange("o (p e) -> (o p) e", e=PACK))

        wt_rows = keep.tile([P, P], F32, name="wt_rows")
        nc.vector.memset(wt_rows[:], 0.0)
        nc.scalar.dma_start(wt_rows[0:BLOCKS, :], wt.rearrange("(b q) o -> b (q o)", q=P))

        cb_planes = cb.rearrange("(p t) c -> t p c", t=PACK)
        books = [keep.tile([P, C], F32, name=f"book{t}", align_bytes=64) for t in range(PACK)]
        nc.sync.dma_start(books[0][:], cb_planes[0])
        offsets = keep.tile([P, N // LIST], U16, name="offsets")
        nc.sync.dma_start(offsets[:], offs)
        for t in range(1, PACK):
            nc.sync.dma_start(books[t][:], cb_planes[t])

        x_planes = xT.rearrange("(p t) r -> p t r", t=PACK)
        x_raw = [keep.tile([P, PACK, CHUNK], F32, name=f"x{c}") for c in range(CHUNKS)]
        y_rows = {}

        def load_x(c):
            nc.sync.dma_start(x_raw[c][:], x_planes[:, :, c * CHUNK : (c + 1) * CHUNK])

        def load_y(first, count):
            y_raw = keep.tile([P, count, N], F32, name=f"y{first}")
            nc.sync.dma_start(y_raw[:], y[first * P : (first + count) * P, :].rearrange("(b p) n -> p b n", p=P))
            for b in range(count):
                y_rows[first + b] = y_raw[:, b, :]

        for c in range(X_AHEAD):
            load_x(c)
        for c in range(CHUNKS):
            if c + X_AHEAD < CHUNKS:
                load_y(2 * c, 1)
                load_x(c + X_AHEAD)
                load_y(2 * c + 1, 1)
            else:
                load_y(2 * c, 2)

        ident = keep.tile([P, P], F32, name="ident")
        make_identity(nc, ident[:])

        def spread(cols):
            spread_bank = bank([P, PACK, P])
            for e in range(PACK):
                nc.tensor.transpose(spread_bank[:, e, :], cols[:, e : e + 1].to_broadcast([P, P]), ident[:])
            return spread_bank

        def turn(runs):
            turned = bank([P, PACK, P])
            for j in range(PACK):
                nc.tensor.transpose(turned[:, j, :], runs[:, j, :], ident[:])
            return turned

        twice_step = vector_tile([P, PACK], F32)
        nc.vector.tensor_scalar(twice_step[:], ts_cols[:], 0.0, 2.0, ALU.is_ge, ALU.mult)
        signed_cols = vector_tile([P, PACK], F32)
        nc.vector.scalar_tensor_tensor(signed_cols[:], twice_step[:], -1.0, norm_cols[:], ALU.add, ALU.mult)
        signed_norm = keep.tile([P, N], F32, name="signed_norm")
        nc.scalar.copy(
            signed_norm[:].rearrange("m (p e) -> m p e", e=PACK),
            spread(signed_cols)[:].rearrange("m e p -> m p e"),
        )

        abs_cols = vector_tile([P, PACK], F32)
        nc.vector.scalar_tensor_tensor(abs_cols[:], twice_step[:], -1.0, ts_cols[:], ALU.add, ALU.mult)
        ts_runs = scalar_tile([P, PACK, P], F32)
        nc.scalar.copy(
            ts_runs[:].rearrange("m j (q g e) -> m j q g e", g=2, e=PACK),
            spread(abs_cols)[:].rearrange("m e (q j g) -> m j q g e", j=PACK, g=2),
        )
        wt_bank = bank([P, P])
        nc.tensor.transpose(wt_bank[:], wt_rows[:], ident[:])
        abs_ts = keep.tile([P, PACK], F32, name="abs_ts")
        nc.scalar.copy(abs_ts[:], turn(ts_runs)[:, :, 0])
        neg_wt = keep.tile([P, BLOCKS], F32, name="neg_wt")
        nc.scalar.activation(neg_wt[:], wt_bank[:, 0:BLOCKS], ACT.Copy, scale=-1.0)
        neg_ts_squared = keep.tile([P, PACK], F32, name="neg_ts_squared")

        k_f32 = keep.tile([P, PACK, N], F32, name="k_f32")
        k_bf = keep.tile([P, N, PACK], BF16, name="k_bf", align_bytes=64)
        k_codes = keep.tile([P, N], U32, name="k_codes", align_bytes=64)
        k_scales = keep.tile([P, N], U8, name="k_scales", align_bytes=64)
        kt_codes = keep.tile([P, D], U32, name="kt_codes", tag=f"book{LAST_PLANE - 1}", align_bytes=64)
        kt_scales = keep.tile([P, D], U8, name="kt_scales", align_bytes=64)
        made = {}
        read_out = []

        def by_runs(by_column):
            return by_column.rearrange("p (q j i) -> p j q i", j=PACK, i=RUN)

        def in_runs(runs):
            return runs.rearrange("p j (q i) -> p j q i", i=RUN)

        def gather(t, half):
            cols = slice(half * HALF, (half + 1) * HALF)
            listed = books[t][:].indirect(offsets[:, cols.start // LIST : cols.stop // LIST])
            nc.vector.tensor_tensor(k_f32[:, t, cols], listed, signed_norm[:, cols], ALU.mult)

        def k_round(copy, u, half):
            cols = slice(half * HALF, (half + 1) * HALF)
            planes = slice(2 * u, 2 * u + 2)
            copy(
                k_bf[:, cols, planes].rearrange("p (c i) t -> p c t i", i=LINE),
                k_f32[:, planes, cols].rearrange("p t (c i) -> p c t i", i=LINE),
            )

        def k_quantise(half):
            cols = slice(half * HALF, (half + 1) * HALF)
            nc.vector.quantize_mx(
                k_codes[:, cols].bitcast(E4M3), k_scales[:, cols], k_bf[:, cols, :].rearrange("p n t -> p (n t)")
            )

        def k_pairs(t):
            made["k_pairs", t] = scalar_tile([P, 2, P, 2], BF16)
            nc.scalar.copy(
                made["k_pairs", t][:].rearrange("p v (q i) e -> p v q i e", i=RUN),
                k_f32[:, t, :].rearrange("p (q v e i) -> p v q i e", v=2, e=2, i=RUN),
            )

        def k_turn(t):
            words = made["k_pairs", t][:].rearrange("p v m e -> p (v m e)").bitcast(F32)
            if t % 2 == 0:
                made["k_turned", t // 2] = bank([P, 2, 2, P])
            for v in range(2):
                nc.tensor.transpose(made["k_turned", t // 2][:, t % 2, v, :], words[:, v * P : (v + 1) * P], ident[:])

        def kt_copy(u):
            made["kt_words", u] = scalar_tile([P, N], F32)
            nc.scalar.copy(
                made["kt_words", u][:].rearrange("m (t p v) -> m t p v", t=2, v=2),
                made["k_turned", u][:].rearrange("m t v p -> m t p v"),
            )

        def kt_quantise(u):
            cols = slice(u * 2 * P, (u + 1) * 2 * P)
            nc.vector.quantize_mx(
                kt_codes[:, cols].bitcast(E4M3),
                kt_scales[:, cols],
                made["kt_words", u][:].bitcast(BF16),
            )
            read_out.append(made["kt_words", u])

        def as_bf16(buffer):
            return buffer[:, 0 : N // 2].bitcast(BF16)

        def x_round(b):
            first = b * P % CHUNK
            made["x_bf", b] = scalar_tile([P, N], F32)
            nc.scalar.copy(
                as_bf16(made["x_bf", b]).rearrange("p (c i t) -> p c t i", i=LINE, t=PACK),
                x_raw[b * P // CHUNK][:, :, first : first + P].rearrange("p t (c i) -> p c t i", i=LINE),
            )

        def x_quantise(b):
            made["x_codes", b] = vector_tile([P, P], U32)
            made["x_scales", b] = scales.tile([P, P], U8, name="x_scales", align_bytes=64)
            nc.vector.quantize_mx(made["x_codes", b][:].bitcast(E4M3), made["x_scales", b][:], as_bf16(made["x_bf", b]))
            read_out.append(made["x_bf", b])

        def scores(b):
            made["s", b] = bank([P, N])
            nc.tensor.matmul_mx(
                made["s", b][:],
                lhsT=made["x_codes", b][:].bitcast(E4M3),
                lhsT_scale=made["x_scales", b][:],
                rhs=k_codes[:].bitcast(E4M3),
                rhs_scale=k_scales[:],
                start=True,
                stop=True,
            )

        def y_times_s(b):
            made["ys", b] = vector_tile([P, PACK, P], F32)
            nc.vector.tensor_tensor(in_runs(made["ys", b][:]), by_runs(made["s", b][:]), by_runs(y_rows[b]), ALU.mult)

        def y_times_wt(b):
            if b < FIRST_ON_GPSIMD:
                made["yw", b] = vector_tile([P, N], F32)
                engine = nc.vector
            else:
                made["yw", b] = read_out[-2]
                engine = nc.gpsimd
            engine.tensor_scalar(
                in_runs(made["yw", b][:].rearrange("p (j m) -> p j m", j=PACK)),
                by_runs(y_rows[b]),
                neg_wt[:, b : b + 1],
                0.0,
                ALU.mult,
                ALU.add,
            )

        def ys_turn(b):
            made["ys_turned", b] = turn(made["ys", b])

        def yw_turn(b):
            made["yw_turned", b] = turn(made["yw", b][:].rearrange("p (j m) -> p j m", j=PACK))

        def margin(b):
            made["margin", b] = scalar_tile([P, N], F32)
            for j in range(PACK):
                nc.scalar.activation(
                    made["margin", b][:, j * P : (j + 1) * P],
                    made["ys_turned", b][:, j, :],
                    ACT.Relu,
                    bias=abs_ts[:, j : j + 1],
                    scale=neg_ts_squared[:, j : j + 1],
                )

        def h_round(b):
            made["h_bf", b] = vector_tile([P, N], F32)
            nc.vector.tensor_tensor(
                as_bf16(made["h_bf", b]).rearrange("p (c i j) -> p c j i", i=LINE, j=PACK),
                made["yw_turned", b][:].rearrange("p j (c i) -> p c j i", i=LINE),
                made["margin", b][:].rearrange("p (j c i) -> p c j i", j=PACK, i=LINE),
                ALU.mult,
            )
            read_out.append(made["margin", b])

        def h_quantise(b):
            made["h_codes", b] = vector_tile([P, P], U32)
            made["h_scales", b] = scales.tile([P, P], U8, name="h_scales", align_bytes=64)
            nc.vector.quantize_mx(made["h_codes", b][:].bitcast(E5M2), made["h_scales", b][:], as_bf16(made["h_bf", b]))
            read_out.append(made["h_bf", b])

        def gradient(b):
            made["o", b] = bank([P, D])
            nc.tensor.matmul_mx(
                made["o", b][:],
                lhsT=made["h_codes", b][:].bitcast(E5M2),
                lhsT_scale=made["h_scales", b][:],
                rhs=kt_codes[:].bitcast(E4M3),
                rhs_scale=kt_scales[:],
                start=True,
                stop=True,
            )

        def store(b):
            new_tile, copy = (vector_tile, nc.vector.tensor_copy) if b == BLOCKS - 1 else (scalar_tile, nc.scalar.copy)
            result = new_tile([P, P, PACK], F32)
            parts = 2 if b == BLOCKS - 1 else 1
            width = P // parts
            for part in range(parts):
                piece = slice(part * width, (part + 1) * width)
                copy(result[:, piece], made["o", b][:].rearrange("r (t p) -> r p t", t=PACK)[:, piece])
                nc.sync.dma_start(
                    out[b * P : (b + 1) * P, piece.start * PACK : piece.stop * PACK],
                    result[:, piece].rearrange("r p t -> r (p t)"),
                )

        for t in range(PACK):
            for half in range(2):
                gather(t, half)
            if t < LAST_PLANE:
                k_pairs(t)
                k_turn(t)
            if t == 1:
                nc.vector.scalar_tensor_tensor(neg_ts_squared[:], abs_ts[:], -1.0, abs_ts[:], ALU.mult, ALU.mult)
                k_round(nc.scalar.copy, 0, 0)
                k_round(nc.vector.tensor_copy, 0, 1)
                kt_copy(0)

        x_round(0)
        for half in range(2):
            k_round(nc.vector.tensor_copy, 1, half)
        k_quantise(0)
        x_quantise(0)
        k_quantise(1)
        x_round(1)
        k_pairs(LAST_PLANE)
        x_round(2)
        x_round(3)
        scores(0)
        x_quantise(1)
        kt_quantise(0)
        y_times_wt(0)
        scores(1)
        k_turn(LAST_PLANE)
        x_quantise(2)

        def at(step, stage, lag, first=0, end=BLOCKS):
            if first <= step - lag < end:
                stage(step - lag)

        for step in range(BLOCKS + LAG_STORE):
            at(step, y_times_wt, 0, first=FIRST_ON_GPSIMD)
            at(step, y_times_s, 0)
            at(step, y_times_wt, 0, first=1, end=FIRST_ON_GPSIMD)
            at(step, h_round, LAG_H_ROUND)
            at(step, h_quantise, LAG_H_QUANTISE, end=FIRST_DRAINED)
            at(step, h_quantise, LAG_H_ROUND, first=FIRST_DRAINED)
            at(step, kt_quantise, 0, first=1, end=PAIRS)
            at(step, x_quantise, LAG_X_QUANTISE)
            at(step, margin, LAG_MARGIN)
            at(step, x_round, LAG_X_ROUND)
            at(step, kt_copy, -1, first=1, end=PAIRS)
            at(step, store, LAG_STORE)
            at(step, ys_turn, 0)
            at(step, yw_turn, 0)
            at(step, scores, LAG_SCORES)
            at(step, gradient, LAG_H_QUANTISE)
